import numpy as np, ml_dtypes
CORES = [16,18,20,22]
N = 4
BF = ml_dtypes.bfloat16
W, E, B, C, RO, NC = 1024, 2048, 256, 11, 3, 32
def group(rng, noise, good, mode, proto):
    n = W // NC; mem = rng.permutation(W).reshape(NC, n); cl = np.zeros(W, np.int64); cl[mem] = np.arange(NC)[:, None]
    x = np.minimum(np.maximum(proto[:, cl] + rng.integers(-noise, noise + 1, (16, W)), 0), 63)
    nx = rng.integers(0, NC, (16, NC))
    if mode == 1: nx[:] = np.arange(NC)
    if mode == 2: nx[:] = cl[0]
    if mode == 3: nx[:] = cl[W - 1]
    l = mem[nx[:, cl], rng.integers(0, n, (16, W))]
    if mode == 1: l[:] = np.arange(W)
    if mode == 2: l[:] = 0
    if mode == 3: l[:] = W - 1
    i = np.zeros((16, E), np.int64); q = rng.integers(0, NC, E)
    for k in range(16):
        i[k] = mem[q, rng.integers(0, n, E)]
        if k < 15:
            go = nx[k, q]; q = np.where(good[k], go, (go + rng.integers(1, NC, E)) % NC)
    return x, i, l
def parts(rng, style):
    x = np.zeros((N, 8, 16, W), np.int64); i = np.zeros((N, 8, 16, E), np.int64); l = np.zeros((N, 8, 16, W), np.int64)
    for a in range(N):
        for g in range(8):
            noise = int(rng.integers(1, 4)); mode = 0; proto = rng.integers(0, 64, (16, NC))
            good = rng.random((15, E)) < rng.choice(np.array([0.2, 0.6, 0.8, 0.95, 1.0]), E)
            if style == "ties": noise = 0; proto = 16 + 8 * rng.integers(0, 2, (16, NC))
            if style == "corners":
                noise = 0; mode = (a + g) % 4; n = rng.choice(np.array([0, 1, C - 1, C, C + 1, 15]), E)
                good = np.argsort(np.argsort(rng.random((15, E)), axis=0), axis=0) < n
            x[a, g], i[a, g], l[a, g] = group(rng, noise, good, mode, proto)
    t = np.stack([rng.integers(20, 70, (N, 8, 16)), rng.integers(200, 420, (N, 8, 16))], axis=-1)
    return x, rng.integers(0, 64, (N, 8, 16, E)), i, l, rng.integers(0, 64, (N, 8, 16, B)), rng.integers(0, 256, (N, 8, 16, 1)), rng.integers(0, 2048, (N, 8, 16, 2)), t
def pack(x, gs, i, l, z, w, h, t):
    def bf(v): return np.ascontiguousarray(v.reshape(N, 128, -1)).astype(np.float32).astype(BF)
    def whole(v): return np.ascontiguousarray(v.reshape(N, 128, -1)).astype(np.int32)
    return {"xc": bf(x), "gi": bf(gs), "ix": whole(i), "lk": whole(l), "zc": bf(z), "wt": whole(w), "hk": whole(h), "th": whole(t)}
def ends(rng, lo, hi, shape, share):
    v = np.where(rng.random(shape) < 0.5, lo, hi)
    return np.where(rng.random(shape) < share, v, rng.integers(lo, hi + 1, shape))
def records(rng, n):
    k = rng.integers(0, 3, (N, 8, 1, n))
    return np.where(k == 0, 0, np.where(k == 1, 63, ends(rng, 0, 63, (N, 8, 16, n), 1.0)))
def full(rng, p):
    u = rng.permutation(4096); f, k = np.unique(((u * u >> 5) + p * u) & (E - 1), return_index=True)
    return u[rng.permutation(k)[:B]]
def setup_inputs(rng):
    return pack(*parts(rng, "plain"))
def setup_inputs_ties(rng):
    x, gs, i, l, z, w, h, t = parts(rng, "ties")
    gs = 16 + 8 * rng.integers(0, 2, gs.shape); z = 16 + 8 * rng.integers(0, 2, z.shape)
    t = rng.choice(np.array([56, 63, 64, 65, 72]), t.shape)
    for a in range(N):
        for g in (6, 7):
            v = (256, 257, 259, 513, 515, 767, 1005, 1007)[(a + g) & 7]; base = int(rng.integers(0, 1008 - v))
            m = rng.permutation(W); low = np.flatnonzero(m < W // 2); high = np.flatnonzero(m >= W // 2)
            size = base + np.where(m < W // 2, 0, v + (rng.random(W) < 0.3).astype(np.int64))
            x[a, g] = (size >> 4) + (np.arange(16)[:, None] < (size & 15)).astype(np.int64)
            i[a, g] = low[rng.integers(0, W // 2, (16, E))]; l[a, g] = high[rng.integers(0, W // 2, (16, W))]
            t[a, g, :, 0] = v; t[a, g, :, 1] = 1008
    return pack(x, gs, i, l, z, w, h, t)
def setup_inputs_corners(rng):
    x, gs, i, l, z, w, h, t = parts(rng, "corners")
    for a in range(N):
        for g in range(8):
            kind = (3 * a + g) % 4
            if kind == 0: w[a, g] = 255
            if kind == 1: w[a, g] = 255 * rng.integers(0, 2, (16, 1))
            if kind == 2: w[a, g] = 0; w[a, g, 15] = 1
            t[a, g, :, 0] = (0, 1, 40, 0, 0, 1008, 40, 1)[(a + g) % 8]
            t[a, g, :, 1] = rng.choice(np.array([0, 340, 1008]), 16)
            h[a, g] = np.where(rng.random((16, 2)) < 0.4, 2047 * rng.integers(0, 2, (16, 2)), h[a, g])
    k = rng.integers(0, 4, (N, 8, 1, B)); z = np.where(k == 0, 0, np.where(k == 1, 63, z))
    k = rng.integers(0, 4, (N, 8, 1, E)); gs = np.where(k == 0, 0, np.where(k == 1, 63, gs))
    i = np.where(rng.random((N, 8, 1, E)) < 0.1, (W - 1) * rng.integers(0, 2, (N, 8, 1, E)), i)
    return pack(x, gs, i, l, z, w, h, t)
def setup_inputs_crowd(rng):
    x, gs, i, l, z, w, h, t = parts(rng, "plain")
    w[:, 0::4] = 0; w[:, 0::4, 5] = 1; z[:, 0::4, 5] = rng.integers(0, 6, (N, 2, B)); h[:, 0::4, :, 0] = 0
    i[:, 1] = rng.choice(np.array([0, 1, W // 2, W - 2, W - 1]), (N, 16, E)); gs[:, 1] = 30
    w[:, 2] = 0
    z[:, 3] = z[:, 3][..., rng.integers(0, 3, B)]
    for a in range(N):
        for g in (5, 6, 7):
            w[a, g] = 0; w[a, g, 0] = 1; w[a, g, 1] = 64; gs[a, g] = 0
            p = int(h[a, g, 0, 0]); u = full(rng, p)
            if g == 5: u[B // 2:] = u[:B // 2]
            z[a, g, 0] = u & 63; z[a, g, 1] = u >> 6
            e = ((u * u >> 5) + p * u) & (E - 1)
            if g == 5:
                side = rng.random(B // 2) < 0.5; side[0] = True; side[1] = False; near = np.concatenate([side, ~side])
                x[a, g] = rng.integers(16, 25, (16, W)); i[a, g] = rng.integers(0, W, (16, E))
                z[a, g, 2:] = np.where(near, rng.integers(16, 25, (14, B)), rng.integers(56, 64, (14, B)))
                t[a, g, :, 0] = 0; t[a, g, :, 1] = rng.integers(206, 448, 16)
            if g == 6:
                o = rng.permutation(W); i[a, g][:, e] = o[(np.arange(16)[:, None] % (W // B)) * B + np.arange(B)]
                t[a, g, :, 0] = 0
            if g == 7: t[a, g, :, 0] = 1008
    t[2, :, :, 0] = 0
    gs[2, 3] = 30; c = int(rng.integers(0, W)); u = np.add.reduce(w[2, 3] * z[2, 3], axis=0) & 4095
    e = ((u * u >> 5) + h[2, 3, 0, 0] * u) & (E - 1)
    i[2, 3][:, e] = c; l[2, 3][:, c] = c
    return pack(x, gs, i, l, z, w, h, t)
def setup_inputs_spread(rng):
    x, gs, i, l, z, w, h, t = parts(rng, "plain")
    x = x >> rng.integers(0, 7, (N, 8, 1, W)); gs = gs >> rng.integers(0, 7, (N, 8, 1, E)); z = z >> rng.integers(0, 7, (N, 8, 1, B))
    i[:, ::2] = (W * rng.random((N, 4, 16, E)) ** 3).astype(np.int64); l[:, ::4] = (W * rng.random((N, 2, 16, W)) ** 3).astype(np.int64)
    w = np.exp2(8 * rng.random(w.shape)).astype(np.int64); h = np.exp2(11 * rng.random(h.shape)).astype(np.int64)
    t = np.minimum(np.exp2(10.2 * rng.random(t.shape)).astype(np.int64), 1008)
    return pack(x, gs, i, l, z, np.minimum(w, 255), np.minimum(h, 2047), t)
def setup_inputs_ends(rng):
    x = records(rng, W); gs = records(rng, E); z = records(rng, B)
    x[:, 0::2, :, 0] = 63; x[:, 0::2, :, W - 1] = 0; x[:, 1::2, :, 0] = 0; x[:, 1::2, :, W - 1] = 63
    i = ends(rng, 0, W - 1, (N, 8, 16, E), 0.75); l = ends(rng, 0, W - 1, (N, 8, 16, W), 0.75)
    w = ends(rng, 0, 255, (N, 8, 16, 1), 0.75); w[:, 7] = 255
    h = ends(rng, 0, 2047, (N, 8, 16, 2), 0.8); t = ends(rng, 0, 1008, (N, 8, 16, 2), 1.0)
    t[0, :, :, 0] = 1008; a = N - 1; t[a, 7, :, 0] = 0
    i[0, 5] = W - 1; l[0, 5, :, W - 1] = 0
    t[1, :, :, 0] = 1008; t[1, 6, :, 0] = 0
    w[1, 6] = 0; w[1, 6, 15] = 255; z[1, 6, 15] = 0; z[1, 6, 15, B - 1] = 63; h[1, 6, :, 0] = 2047 * rng.integers(0, 2, 16)
    i[1, 6] = W - 1; i[1, 6, :, 0] = 0; l[1, 6, :, 0] = 0; l[1, 6, :, W - 1] = 0
    v = z[a, 7]; v[:, B - 1] = 63; v[:, B - 2] = 0; v[15, B - 2] = 63; v[:, B - 3] = 0; v[:4, B - 3] = 63; v[4, B - 3] = 5
    h[a, 7, 0, 0] = 2047; h[a, 7, 1, 0] = 0; h[a, 7, 15, 1] = 2047
    h[a, 7, 15, 0] = ((E - 1 - (3777 * 3777 >> 5)) * pow(3777, -1, E)) % E
    c = ((3088 * 3088 >> 5) + h[a, 7, :, 0] * 3088) & (E - 1)
    gs[a, 7][:, c] = 0; gs[a, 7, :, E - 1] = v[:, B - 2]
    i[a, 7, :, c[1]] = 0; i[a, 7, :, c[0]] = W - 1; i[a, 7, :8, E - 1] = 0; i[a, 7, 8:, E - 1] = W - 1
    l[a, 7, :, 0] = 0; l[a, 7, :, W - 1] = 0
    return pack(x, gs, i, l, z, w, h, t)
def check_inputs(d):
    bad = []
    for k, lo, hi in (("xc", 0, 63), ("gi", 0, 63), ("ix", 0, W - 1), ("lk", 0, W - 1), ("zc", 0, 63), ("wt", 0, 255), ("hk", 0, 2047), ("th", 0, 1008)):
        v = np.asarray(d[k]).astype(np.float64)
        if not np.all((v >= lo) & (v <= hi) & (v == np.floor(v))): bad.append("range of " + k)
    return bad
def reference(xc, gi, ix, lk, zc, wt, hk, th):
    def cut(v): return np.asarray(v).astype(np.float32).astype(np.int64).reshape(N, 8, 16, -1)
    X, G, I, L, Z, w, h, t = cut(xc), cut(gi), cut(ix), cut(lk), cut(zc), cut(wt), cut(hk), cut(th)
    A = np.zeros(N, np.int64); lane = np.arange(B)
    for rnd in range(RO):
        count = np.zeros(N, np.int64)
        for a in range(N):
            r = (a - rnd) % N
            for g in range(8):
                z = Z[r, g]
                u = np.add.reduce(w[a, g] * z, axis=0) & 4095
                em = ((u * u >> 5) + h[a, g, :, 0:1] * u + A[a]) & (E - 1)
                d = np.add.reduce(np.abs(G[a, g][:, em] - z[:, None, :]), axis=0)
                e = em[np.argmin(d, axis=0), lane]
                J = I[a, g][:, e]
                x = X[a, g][:, J]
                y = X[a, g][:, np.take_along_axis(L[a, g], J, 1)]
                s = np.add.reduce(np.abs(y[:, :15] - x[:, 1:]), axis=0)
                far = np.add.reduce(np.abs(x - z[:, None, :]), axis=0)
                rec = np.add.reduce((s <= t[a, g, :15, 0:1]).astype(np.int64), axis=0) >= C
                fresh = ((u * u >> 4) + h[a, g, :, 1:2] * u) & (W - 1)
                col = np.where(rec[None, :] | (far > t[a, g, :, 1:2]), fresh, J)
                ks = np.argmax(s, axis=0)
                f, first = np.unique(e, return_index=True)
                I[a, g][:, f] = col[:, first]
                if rnd < RO - 1:
                    o = first[rec[first]]; G[a, g][:, e[o]] = z[:, o]
                q = np.flatnonzero(~rec); c, one = np.unique(J[ks[q], q], return_index=True); q = q[one]
                L[a, g][ks[q], c] = J[ks[q] + 1, q]
                count[a] += np.count_nonzero(rec)
                Z[r, g] = (z + np.maximum.reduce(x, axis=1)) >> 1
        A = count
    return {"yz": Z.reshape(N, 128, B).astype(np.float32).astype(BF), "yi": I.reshape(N, 128, E).astype(np.float32), "yl": L.reshape(N, 128, W).astype(np.float32)}

@@ -1,0 +1,626 @@
+import numpy as np
+from concourse.mybir import AluOpType as OP, ActivationFunctionType as AF, AxisListType as AX
+
+W, E, B, RO, NEED = 1024, 2048, 256, 3, 11
+NENG = 4
+GPLAN = ("SVSV", "SVSV", "VSVS")
+YPLAN = ("SVSV", "SSSV", "SVSV")
+ZPLAN = ("VVVV", "VGVG", "VVVG")
+FPLAN = "SS"
+TRIES, ORDER = 2000, {}
+HEAD, HZ, HC, LOOK = 0.0, 2.0, 6.0, 0.04
+F32, BF, F16, I32, U16 = "float32", "bfloat16", "float16", "int32", "uint16"
+
+SCRATCH = {
+    "gist": ("sbuf", [128, E + B], BF), "nm": ("sbuf", [128, E + B], F32), "lkt": ("sbuf", [128, W + B], F32),
+    "xcb": ("sbuf", [128, W], BF), "ixi": ("sbuf", [128, E], I32), "lki": ("sbuf", [128, W], I32),
+    "wti": ("sbuf", [128, 1], I32), "hki": ("sbuf", [128, 2], I32), "thi": ("sbuf", [128, 2], I32),
+    "zin0": ("sbuf", [128, B], BF), "zin1": ("sbuf", [128, B], BF), "zin2": ("sbuf", [128, B], BF), "zfin": ("sbuf", [128, B], BF),
+    "zo0": ("sbuf", [128, B], BF), "zo1": ("sbuf", [128, B], BF), "zo2": ("sbuf", [128, B], BF),
+    "S": ("sbuf", [128, 2048], BF), "SF": ("sbuf", [128, 2048], F16), "SW": ("sbuf", [128, 2048], BF), "D": ("sbuf", [128, 2048], F16), "R": ("sbuf", [128, 2048], F16),
+    "NS": ("sbuf", [128, 2048], BF), "rz": ("sbuf", [128, 2048], BF), "zr0": ("sbuf", [128, 4096], BF), "zr1": ("sbuf", [128, 4096], BF),
+    "eq": ("sbuf", [128, 16, 256], BF), "eq2": ("sbuf", [128, 16, 256], BF),
+}
+for _k in (0, 1):
+    for _n, _d, _w in (("gd", BF, 2048), ("fa", BF, 2048), ("nx", BF, 2064), ("lg", F16, 2048), ("yb", BF, 2048), ("zs", BF, 2048)):
+        SCRATCH["%s%d" % (_n, _k)] = ("sbuf", [128, _w], _d)
+    SCRATCH["aa%d" % _k] = ("sbuf", [128, 8, 16, 16], BF)
+    SCRATCH["ya%d" % _k] = ("sbuf", [128, 8, 16, 16], BF)
+_SMALL = {
+    F32: (("wtf", 1), ("hkf", 2), ("thf", 2), ("one", 128), ("idf", 128), ("blk", 128), ("wblk", 128), ("zer", 128), ("pm64", 64), ("pm32", 32), ("pm", 16), ("im", 16),
+          ("half", 16), ("zero", 16), ("pw", 16), ("tw", 16), ("tr", 16), ("wcol", 1), ("rcol", 1), ("kcol", 1), ("thr", 256), ("lane", 32), ("lan0", 16),
+          ("pd", 32), ("akey", 128), ("rmin", 128), ("rmax", 128), ("xe", 256), ("xq", 256), ("e0", 256), ("elf", 16),
+          ("ja", 256), ("rec", 16), ("nrec", 16), ("acol", 1), ("loL", 16), ("dE", 32), ("dT", 64), ("oT", 64), ("gT", 16),
+          ("IL", 16), ("dl", 256), ("nl", 256), ("pn", 256)),
+    F16: (("id16", 128), ("ni16", 128), ("hi16", 128), ("nh16", 128), ("sh16", 128), ("bo16", 128), ("nb16", 128), ("one16", 512), ("r0k", 128), ("prow", 128), ("imr", 128), ("c8k", 128),
+          ("ksr", 128), ("cf", 48), ("v160", 256), ("v161", 256), ("elh", 16), ("jh", 256), ("nh", 256), ("jr", 16), ("eB", 256), ("IB", 256), ("lo", 512),
+          ("oh", 256), ("pj", 256)),
+    BF: (("idb", 128), ("nib", 128), ("k1b", 128), ("oneb", 128), ("wd", 128), ("bo4", 128), ("rcnt", 128), ("ze", 256), ("cm0", 128), ("cm1", 128), ("cn", 256),
+         ("recb", 16), ("rB", 256), ("mk", 256)),
+    I32: (("kx", 256), ("km0", 128), ("km1", 128), ("ui", 32), ("sq", 16), ("cmb0", 48), ("cmb1", 48), ("bs", 16), ("ei", 256), ("ej", 256), ("vi", 256), ("vj", 256), ("ki", 64), ("el", 16), ("kj", 32)),
+    U16: (("e16", 256), ("elu", 16), ("ju", 256), ("nu", 256), ("of", 64), ("ILu", 16)),
+}
+PLACE = {}
+for _d, _a in ((F32, "fA"), (F16, "hA"), (BF, "bA"), (I32, "iA"), (U16, "uA")):
+    _at = 0
+    for _n, _w in _SMALL[_d]:
+        PLACE[_n] = (_a, _at, _w)
+        _at += -(-_w // 32) * 32
+    SCRATCH[_a] = ("sbuf", [128, _at], _d)
+for _k in range(8):
+    SCRATCH["ps%d" % _k] = ("psum", [128, 512], F32)
+NDMA = 20
+SEMAPHORES = ["eV", "eS", "eP", "eG", "snd", "arr1", "arr2", "arr3"] + ["d%d" % k for k in range(NDMA)]
+
+CY = 0.00083 * 1.15
+GA, SC, PEC, VO, WAKE = 1.4, 3.0, 0.0005, 0.03, 0.06
+
+
+def rank_program(g, core, T, topo):
+    rank = T.rank_of(core)
+    if rank is None:
+        return
+    ops, hist, head = [], {}, [0.0]
+    queues = {"V": g.vector, "S": g.scalar, "P": g.tensor, "G": g, "Y": g.sync}
+
+    def A(name, lo=0, hi=None, step=1):
+        if name in PLACE:
+            name, at, w = PLACE[name]
+            lo, hi = at + lo, at + (w if hi is None else hi)
+        hi = T[name].shape[1] if hi is None else hi
+        return (T[name][:, lo:hi] if step == 1 else T[name][:, lo:hi:step], (name, lo, hi, step))
+
+    def meets(a, b):
+        if a[1] >= b[2] or b[1] >= a[2]:
+            return False
+        return not (a[3] == b[3] and a[3] > 1 and a[1] % a[3] != b[1] % b[3])
+
+    def add(q, calls, w, r, cost, lat=0.0, kind="c", sem=None, val=1):
+        o = {"q": q, "calls": calls, "cost": cost, "lat": lat, "kind": kind, "sem": sem, "val": val, "deps": {}, "i": len(ops), "head": head[0]}
+        for regs, isw in ((r, False), (w, True)):
+            for reg in regs:
+                ps = reg[0][:2] == "ps"
+                for (p, preg, pw) in hist.setdefault(reg[0], []):
+                    same = p["q"] == q and p["kind"] == "c" and kind == "c"
+                    if ps and not same:
+                        o["deps"][p["i"]] = True
+                    elif meets(reg, preg) and (isw or pw):
+                        need = not (same and q == "P")
+                        o["deps"][p["i"]] = o["deps"].get(p["i"], False) or need
+        for regs, isw in ((r, False), (w, True)):
+            for reg in regs:
+                h = hist[reg[0]]
+                if isw and reg[3] == 1 and reg[0][:2] != "ps":
+                    h[:] = [x for x in h if not (x[0] is not o and x[1][1] >= reg[1] and x[1][2] <= reg[2])]
+                h.append((o, reg, isw))
+        ops.append(o)
+
+    def vcost(n, f=1.0):
+        return VO + max(64.0, n * f) * CY
+
+    def width(x):
+        return (x[1][2] - x[1][1] + x[1][3] - 1) // x[1][3]
+
+    def fast(*xs):
+        return 0.5 if all(SCRATCH[x[1][0]][2] in (BF, F16, U16) for x in xs) else 1.0
+
+    def cp(o, i):
+        add("V", [lambda: g.vector.tensor_copy(o[0], i[0])], [o[1]], [i[1]], vcost(width(i), fast(o, i)))
+
+    def tt(o, a, b, op):
+        f = 1.0 if a[1][0][:2] == "ps" or b[1][0][:2] == "ps" else 2.0
+        add("V", [lambda: g.vector.tensor_tensor(o[0], a[0], b[0], op)], [o[1]], [a[1], b[1]], vcost(width(a), f))
+
+    def ts(o, a, s1, op0, s2=None, op1=None):
+        r = [a[1]] + [s[1] for s in (s1, s2) if isinstance(s, tuple)]
+        x1 = s1[0] if isinstance(s1, tuple) else s1
+        x2 = s2[0] if isinstance(s2, tuple) else s2
+        if op1 is None:
+            f = lambda: g.vector.tensor_scalar(o[0], a[0], x1, None, op0)
+        else:
+            f = lambda: g.vector.tensor_scalar(o[0], a[0], x1, x2, op0, op1)
+        add("V", [f], [o[1]], r, vcost(width(a), fast(o, a)))
+
+    def ms(o, v):
+        add("V", [lambda: g.vector.memset(o[0], v)], [o[1]], [], vcost(width(o), fast(o)))
+
+    def scan(o, d0, d1, init, op0, op1):
+        add("V", [lambda: g.vector.tensor_tensor_scan(o[0], d0[0], d1[0], init, op0, op1)], [o[1]], [d0[1], d1[1]], vcost(width(d1), fast(o, d0, d1)))
+
+    def total_of(o, i):
+        add("V", [lambda: g.vector.tensor_reduce(o[0], i[0], AX.X, OP.add)], [o[1]], [i[1]], vcost(width(i)))
+
+    def act(o, i, func, scale=1.0, bias=0.0):
+        r = [i[1]] + ([scale[1]] if isinstance(scale, tuple) else [])
+        sc = scale[0] if isinstance(scale, tuple) else scale
+        add("S", [lambda: g.scalar.activation(o[0], i[0], func, bias, sc)], [o[1]], r, 0.07 + width(i) * CY)
+
+    def gat(q, o, win, off, scale=1.0):
+        if q == "V":
+            f = lambda: g.vector.tensor_copy(o[0], win[0].indirect(off[0]))
+        else:
+            f = lambda: g.scalar.activation(o[0], win[0].indirect(off[0]), AF.Copy, 0.0, scale)
+        add(q, [f], [o[1]], [win[1], off[1]], 0.07 + 16 * width(off) * GA * CY)
+
+    def gatop(o, win, off, b, op):
+        add("V", [lambda: g.vector.tensor_tensor(o[0], win[0].indirect(off[0]), b[0], op)], [o[1]], [win[1], off[1], b[1]], 0.07 + 16 * width(off) * GA * CY)
+
+    def pe(out, terms, first=True, last=True):
+        calls, regs, n, c = [], [], len(terms), 0.05
+        for k, (po, l, r) in enumerate(terms):
+            calls.append(lambda po=po, l=l, r=r, k=k: g.tensor.matmul(po[0], l[0], r[0], first and k == 0, last and k == n - 1))
+            regs += [l[1], r[1]]
+            c += max(64, width(po)) * PEC
+        add("P", calls, [out[1]], sorted(set(regs)), c)
+
+    def spread(out_name, lo, src):
+        calls, regs = [], [src[1]]
+        w = 16 * width(src)
+        for rho in range(16):
+            po = A(out_name, lo + rho, lo + w, 16)
+            l = A("R", rho * 128, rho * 128 + 128)
+            calls.append(lambda po=po, l=l: g.tensor.matmul(po[0], l[0], src[0], True, True))
+            regs.append(l[1])
+        add("P", calls, [(out_name, lo, lo + w, 1)], regs, 0.05 + 16 * 64 * PEC)
+
+    def collect(out, src, lo):
+        pe(out, [(out, A("SF", rho * 128, rho * 128 + 128), A(src, lo + rho, lo + 256, 16)) for rho in range(16)])
+
+    dn = [0]
+
+    def dma(q, o, i, lat, regs_w, regs_r, acc=False):
+        sem = "d%d" % dn[0]
+        dn[0] += 1
+        if acc:
+            f = lambda: g.dma_start(o, i, accum_op=OP.add, max_dma_last_dim=4096)
+        else:
+            f = lambda: queues[q].dma_start(o, i)
+        add(q, [f], regs_w, regs_r, 1.0 if q == "G" else 0.1, lat, "d", sem, 16)
+
+    def load(q, name, src, lat, hi=None):
+        a = A(name, 0, hi)
+        dma(q, a[0], T[src][:], lat, [a[1]], [])
+
+    load("Y", "hki", "hk", 2.2)
+    load("S", "wti", "wt", 2.2)
+    load("Y", "zin0", "zc", 2.4)
+    load("S", "thi", "th", 2.4)
+    load("Y", "gist", "gi", 4.0, E)
+    load("Y", "ixi", "ix", 6.0)
+    load("Y", "lki", "lk", 7.0)
+    load("Y", "xcb", "xc", 8.0)
+
+    def aff(o, i, pat, op, base, cm, fill=0.0):
+        add("G", [lambda: g.affine_select(o[0], i[0], pat, op, fill, base, cm)], [o[1]], [i[1]], 0.2 + 2 * width(i) * CY)
+
+    def gcp(o, i):
+        add("G", [lambda: g.affine_select(o[0], i[0], [[1, width(o)]], OP.is_ge, 0.0, 1, 0)], [o[1]], [i[1]], 0.2 + 2 * width(o) * CY)
+
+    def iot(o, pat, base, cm):
+        add("G", [lambda: g.iota(o[0], pat, base, cm, allow_small_or_imprecise_dtypes=True)], [o[1]], [], 0.16 + 2 * width(o) * CY)
+
+    def rep(name, n, w, cp=cp):
+        k = w
+        while k < n:
+            cp(A(name, k, 2 * k), A(name, 0, k))
+            k *= 2
+
+    head[0] = 80.0
+    ms(A("one"), 1.0)
+    head[0] = 70.0
+    ms(A("one16"), 1.0)
+    ms(A("SW"), 0.0)
+    head[0] = 0.0
+    for k in range(0, 2048, 512):
+        ms(A("S", k, k + 512), 0.0)
+    head[0] = 60.0
+    aff(A("blk"), A("one"), [[-16, 8], [0, 16]], OP.is_ge, 0, 1)
+    aff(A("blk"), A("blk"), [[16, 8], [0, 16]], OP.is_ge, 15, -1)
+    aff(A("idf"), A("one"), [[-1, 128]], OP.is_equal, 0, 1)
+    tt(A("pm64"), A("idf", 0, 64), A("idf", 64, 128), OP.add)
+    tt(A("pm32"), A("pm64", 0, 32), A("pm64", 32, 64), OP.add)
+    tt(A("pm"), A("pm32", 0, 16), A("pm32", 16, 32), OP.add)
+    cp(A("wtf"), A("wti"))
+    ts(A("wblk"), A("blk"), A("wtf"), OP.mult)
+    for k in range(0, 16, 2):
+        cp(A("SW", k * 129, k * 128 + 128, 16), A("wblk", 0, 128, 16))
+        act(A("SW", k * 129 + 129, k * 128 + 256, 16), A("blk", 0, 128, 16), AF.Copy, A("wtf"))
+    head[0] = 0.0
+    for k in range(16):
+        act(A("S", k * 129, k * 128 + 128, 16), A("blk", 0, 128, 16), AF.Copy)
+    cp(A("hkf"), A("hki"))
+    cp(A("thf"), A("thi"))
+    head[0] = 60.0
+    for k in range(0, 16, 4):
+        aff(A("R", k * 128, k * 128 + 512), A("one16"), [[-1, 4], [-16, 8], [0, 16]], OP.is_equal, -k, 1)
+    head[0] = 0.0
+    iot(A("im"), [[1, 16]], 0, 0)
+    ts(A("pd", 0, 16), A("pm"), A("hkf", 0, 1), OP.mult)
+    ts(A("pd", 16, 32), A("pm"), A("thf", 0, 1), OP.mult)
+    pe(A("ps5", 64, 96), [(A("ps5", 64, 96), A("blk"), A("pd"))])
+    cp(A("prow", 0, 16), A("ps5", 64, 80))
+    rep("prow", 128, 16)
+    cp(A("imr", 0, 16), A("im"))
+    rep("imr", 128, 16)
+    ms(A("c8k"), -8192.0)
+    ts(A("r0k"), A("R", 0, 128), 2048.0, OP.mult)
+    ms(A("rmin"), -4.0e7)
+    ms(A("rmin", 0, 128, 16), 4.0e7)
+    ms(A("zer"), 0.0)
+    for name, c, off in (("idb", 1.0, 0), ("nib", -1.0, 0), ("id16", 1.0, 0), ("ni16", -1.0, 0), ("hi16", 0.5, 0), ("nh16", -0.5, 0), ("k1b", 1024.0, 0), ("sh16", 1.0, -1)):
+        aff(A(name), A("zer"), [[-1, 128]], OP.not_equal, off, 1, c)
+    aff(A("D"), A("R"), [[1, 16], [0, 8], [-1, 16]], OP.is_equal, 0, 0)
+    ms(A("nx0", 2048, 2064), 0.0)
+    ms(A("nx1", 2048, 2064), 0.0)
+    for k in range(0, 2048, 512):
+        ms(A("rz", k, k + 512), -100.0)
+        ms(A("rz", k, k + 512, 16), 100.0)
+    ms(A("half"), 0.5)
+    ms(A("zero"), 0.0)
+    scan(A("pw"), A("half"), A("zero"), 2.0, OP.mult, OP.add)
+    tt(A("tw"), A("pw"), A("pm"), OP.mult)
+    total_of(A("wcol"), A("tw"))
+    tt(A("tr"), A("im"), A("pm"), OP.mult)
+    total_of(A("rcol"), A("tr"))
+    act(A("wd"), A("blk"), AF.Copy, A("wcol"))
+    act(A("bo4"), A("blk"), AF.Copy, 4.0)
+    ts(A("thr", 0, 16), A("pw"), 2.0, OP.mult)
+    rep("thr", 256, 16, gcp)
+    iot(A("lan0"), [[16, 16]], E, 0)
+    ts(A("lane", 0, 16), A("lan0"), A("rcol"), OP.add)
+    ts(A("lane", 16, 32), A("lane", 0, 16), float(E - W), OP.subtract)
+    ts(A("kcol"), A("rcol"), -1.0, OP.mult, 15.0, OP.add)
+    for k in range(0, 2048, 512):
+        gcp(A("SF", k, k + 512), A("S", k, k + 512))
+    if "V" in FPLAN:
+        for k in range(0, 2048, 1024):
+            act(A("NS", k, k + 1024), A("S", k, k + 1024), AF.Copy, -1.0)
+    ts(A("ksr", 0, 16), A("im"), -1.0, OP.mult, 15.0, OP.add)
+    ts(A("akey", 0, 16), A("ps5", 80, 96), 16.0, OP.mult)
+    tt(A("akey", 0, 16), A("akey", 0, 16), A("ksr", 0, 16), OP.add)
+    ms(A("ksr", 15, 16), -32768.0)
+    ms(A("akey", 15, 16), -1.0e6)
+    rep("ksr", 128, 16, gcp)
+    rep("akey", 128, 16, gcp)
+    ms(A("rmax"), 4.0e7)
+    ms(A("rmax", 0, 128, 16), -4.0e7)
+    ms(A("rcnt"), 1.0)
+    ms(A("rcnt", 0, 128, 16), 0.0)
+    ms(A("oneb"), 1.0)
+    gcp(A("bo16"), A("blk"))
+    ts(A("thf", 1, 2), A("thf", 1, 2), -1.0, OP.mult, -0.5, OP.add)
+    ts(A("nb16"), A("idf"), A("thf", 1, 2), OP.mult)
+
+    def quad(name, c0, c1):
+        return (T[name][:, c0:c1, :, :], (name, c0 * 256, c1 * 256, 1))
+
+    def line(name, rho):
+        return (T[name][:, :, rho, :], (name, 0, 2048, 1))
+
+    bank = [0]
+
+    def plan(s):
+        return [(q, 64 * k, 64) for k, q in enumerate(s)]
+
+    def absdiff(parts, win, off, raw, other, sub, dest, scale):
+        for (q, l0, n) in parts:
+            h, a, b = l0 // 128, (l0 % 128) * 16, (l0 % 128 + n) * 16
+            head[0] = HEAD * (1 - h)
+            o = A("%s%d" % (raw, h), a, b)
+            if q == "V":
+                gatop(o, win, A(off, l0, l0 + n), other(h, a, b), OP.subtract if sub else OP.add)
+                for x in range(a, b, 1024):
+                    act(quad("%s%d" % (dest, h), x // 256, min(x + 1024, b) // 256), A("%s%d" % (raw, h), x, min(x + 1024, b)), AF.Abs, scale)
+            else:
+                gat("S", o, win, A(off, l0, l0 + n))
+                for x in range(a, b, 512):
+                    y = min(x + 512, b)
+                    ps = A("ps%d" % bank[0], 0, y - x)
+                    bank[0] ^= 1
+                    pe(ps, [(ps, A("idb"), A("%s%d" % (raw, h), x, y)), (ps, A("nib" if sub else "idb"), other(h, x, y))])
+                    act(quad("%s%d" % (dest, h), x // 256, y // 256), ps, AF.Abs, scale)
+
+    def firsts(bc, own, eqn, lo_lo, small, extra=None):
+        bank7 = (None, ("ps7", 0, 512, 1))
+        O = lambda x, y: A("ps7", 256 + x, 256 + y)
+        E3 = lambda c, x, y: (T[eqn][:, c, x:y], (eqn, 256 * c + x, 256 * c + y, 1))
+        if extra:
+            pe(bank7, [(O(0, 256),) + extra], True, False)
+        else:
+            rest = []
+        for c0, c1 in ((0, 3), (3, 7), (7, 11), (11, 16)):
+            calls, w, r, cost = [], [], [], 0.0
+            for c in range(c0, c1):
+                o = E3(c, 0, 256 - 16 * c)
+                i = A(bc, 16 * c, 256)
+                s = A(own, c, c + 1)
+                calls.append(lambda o=o, i=i, s=s: g.vector.tensor_scalar(o[0], i[0], s[0], None, OP.is_equal))
+                w.append(o[1])
+                r += [i[1], s[1]]
+                cost += vcost(256 - 16 * c, 0.5)
+            add("V", calls, w, sorted(set(r)), cost)
+            terms = [(O(16 * c + 16, 256), A("bo4"), E3(c, 16, 256 - 16 * c)) for c in range(c0, min(c1, 15))]
+            if extra:
+                pe(bank7, terms, False, False)
+            else:
+                rest += terms
+        own_block = (O(0, 256), A("wd"), (T[eqn][:, :, 0:16], (eqn, 0, 4096, 1)))
+        if extra:
+            pe(bank7, [own_block], False, True)
+        else:
+            pe(bank7, [own_block] + rest)
+        tt(A("lo", lo_lo, lo_lo + 256), O(0, 256), A("thr"), OP.is_ge)
+        collect(A("ps5", small, small + 16), "lo", lo_lo)
+
+    def sel(k, own, t, dlt):
+        tt(A("dT", 16 * k, 16 * k + 16), t, dlt, OP.mult)
+        tt(A("oT", 16 * k, 16 * k + 16), A("dT", 16 * k, 16 * k + 16), own, OP.add)
+        cp(A("of", 16 * k, 16 * k + 16), A("oT", 16 * k, 16 * k + 16))
+
+    def scat(win, off, src, src2=None):
+        if src2 is None:
+            f = lambda: g.vector.tensor_copy(win[0].indirect(off[0]), src[0])
+        else:
+            f = lambda: g.vector.tensor_tensor(win[0].indirect(off[0]), src[0], src2[0], OP.add)
+        add("V", [f], [win[1]], [off[1], src[1]] + ([src2[1]] if src2 else []), 0.06 + 256 * SC * CY)
+
+    def cues(t):
+        head[0] = HC
+        z, cb, v16 = "zin%d" % t, "cmb%d" % (t & 1), "v16%d" % (t & 1)
+        u = A("ps6", 0, 16)
+        pe(u, [(u, A("SW", r * 128, r * 128 + 128), A(z, r, 256, 16)) for r in range(16)])
+        cp(A("ui", 0, 16), u)
+        ts(A("ui", 16, 32), A("ui", 0, 16), 4095, OP.bitwise_and)
+        tt(A("sq"), A("ui", 16, 32), A("ui", 16, 32), OP.mult)
+        ts(A(cb, 0, 16), A("ui", 0, 16), 2047, OP.bitwise_and)
+        ts(A(cb, 16, 32), A("sq"), 5, OP.logical_shift_right, 2047, OP.bitwise_and)
+        ts(A(cb, 32, 48), A("sq"), 4, OP.logical_shift_right, 1023, OP.bitwise_and)
+        cp(A("cf"), A(cb))
+        spread("ps6", 0, A("cf", 0, 32))
+        act(A("xe"), A("ps6", 0, 256), AF.Copy, A("hkf", 0, 1))
+        act(A("xq"), A("ps6", 0, 256), AF.Copy, A("hkf", 1, 2))
+        tt(A("ei" if t == 0 else "e0"), A("ps6", 256, 512), A("xe"), OP.add)
+        spread("ps6", 0, A("cf", 32, 48))
+        tt(A("vi"), A("ps6", 0, 256), A("xq"), OP.add)
+        ts(A("vj"), A("vi"), 1023, OP.bitwise_and)
+        gcp(A(v16), A("vj"))
+        zr = "zr%d" % (t & 1)
+        head[0] = 0.0
+        for k in range(0, 16, 4):
+            if ZPLAN[t][k // 4] == "S":
+                add("S", [lambda m=m: g.scalar.activation(T[zr][:, m::16], T[z][:], AF.Copy, 0.0, 1.0) for m in range(k, k + 4)],
+                    [(zr, m, 4096, 16) for m in range(k, k + 4)], [(z, 0, 256, 1)], 4 * (0.07 + 256 * CY))
+            elif ZPLAN[t][k // 4] == "G":
+                for m in range(k, k + 4):
+                    gcp(A(zr, m, 4096, 16), A(z))
+            else:
+                add("V", [lambda m=m: g.vector.tensor_copy(T[zr][:, m::16], T[z][:]) for m in range(k, k + 4)],
+                    [(zr, m, 4096, 16) for m in range(k, k + 4)], [(z, 0, 256, 1)], 4 * vcost(256, 0.5))
+
+    cues(0)
+    H = ((0, 0, 128), (1, 128, 256))
+    for t in range(RO):
+        z, zr, cb = "zin%d" % t, "zr%d" % (t & 1), "cmb%d" % (t & 1)
+        for (h, a, b) in H:
+            if t:
+                ts(A("ei", a, b), A("e0", a, b), A("acol"), OP.add)
+            ts(A("ej", a, b), A("ei", a, b), 2047, OP.bitwise_and)
+            cp(A("e16", a, b), A("ej", a, b))
+        if t:
+            ts(A("bs"), A(cb, 16, 32), A("acol"), OP.add)
+        base, boff = ("bs", 0) if t else (cb, 16)
+        absdiff(plan(GPLAN[t]), A("gist", 0, E), "e16", "gd", lambda h, x, y: A(zr, h * 2048 + x, h * 2048 + y), True, "aa", 32768.0)
+        for (h, a, b) in H:
+            head[0] = HEAD * (1 - h)
+            c0, c1 = 8 * h, 8 * h + 8
+            k = A("ps%d" % (2 + h), 0, 128)
+            pe(k, [(k, A("R", 0, 128), A("prow")), (k, A("r0k"), A("imr")), (k, A("r0k"), A("c8k"))]
+               + [(k, A("S", r * 128, r * 128 + 128), line("aa%d" % h, r)) for r in range(16)])
+            scan(A("km%d" % h), A("rmin"), k, 4.0e7, OP.max, OP.min)
+            i0, i1, i2, i3 = [A("ki", 32 * h + 8 * x, 32 * h + 8 * x + 8) for x in range(4)]
+            ts(i1, A("km%d" % h, 15, 128, 16), 2047, OP.bitwise_and)
+            tt(i2, i1, A(cb, c0, c1), OP.mult)
+            tt(i3, i2, A(base, boff + c0, boff + c1), OP.add)
+            ts(A("el", c0, c1), i3, 2047, OP.bitwise_and)
+            cp(A("elu", c0, c1), A("el", c0, c1))
+            gat("V", A("ju", a, b), A("nm", 0, E) if t else A("ixi"), A("elu", c0, c1))
+            for q in (0, 64):
+                gat("V", A("lg%d" % h, 16 * q, 16 * q + 1024), A("lkt", 0, W) if t else A("lki"), A("ju", a + q, a + q + 64))
+                gat("S", A("nx%d" % h, 16 * q, 16 * q + 1024), A("xcb"), A("ju", a + q, a + q + 64), -1.0)
+                n = A("ps%d" % (2 + h), 128 + q, 192 + q)
+                pe(n, [(n, A("D", r * 128, r * 128 + 128), A("lg%d" % h, 16 * q + r, 16 * q + 1024, 16)) for r in range(16)])
+                cp(A("nu", a + q, a + q + 64), n)
+            gcp(A("jh", a, b), A("ju", a, b))
+            gcp(A("nh", a, b), A("nu", a, b))
+            head[0] = HZ
+            scan(A("zs%d" % h), A("rz"), A("nx%d" % h, 0, 2048), 100.0, OP.max, OP.min)
+            zp = A("ps6", a, b)
+            pe(zp, [(zp, A("idb"), A(z, a, b)), (zp, A("nib"), A("zs%d" % h, 15, 2048, 16))])
+            act(A("ze", a, b), zp, AF.Copy, 0.5, 127.75)
+            act(A("zo%d" % t, a, b), A("ze", a, b), AF.Copy, 1.0, -128.0)
+        dst = T.cores[(rank + 1) % len(T.cores)] if t < RO - 1 else T.cores[(rank - t) % len(T.cores)]
+        land = "zin%d" % (t + 1) if t < RO - 1 else "zfin"
+        eng = topo.engines(core, dst)[:NENG]
+        rid, pid, _se = topo.addr(dst)
+        mask = sum(1 << e for e in eng)
+        add("G", [lambda land=land, rid=rid, pid=pid, mask=mask, t=t: g.remote_dma(
+            T[land][:], T["zo%d" % t][:], T.sem["arr%d" % (t + 1)], T.sem.snd, pid, rid, mask)],
+            [(land, 0, 256, 1)], [("zo%d" % t, 0, 256, 1)], 1.0, 3.0, "r", "arr%d" % (t + 1), len(eng))
+        head[0] = 0.0
+        for (h, a, b) in H:
+            x = A(zr, h * 2048, h * 2048 + 2048)
+            dma("G", x[0], T["nx%d" % h][:, 0:2048], 5.0, [x[1]], [x[1], ("nx%d" % h, 0, 2048, 1)], acc=True)
+        gcp(A("elh"), A("el"))
+        gcp(A("elf"), A("el"))
+        tt(A("dE", 0, 16), A("lane", 0, 16), A("elf"), OP.subtract)
+        spread("ps7", 0, A("elh"))
+        cp(A("eB"), A("ps7", 0, 256))
+        firsts("eB", "elf", "eq", 0, 32)
+        ts(A("loL"), A("ps5", 32, 48), 0.0625, OP.mult)
+        sel(0, A("elf"), A("loL", 0, 16), A("dE", 0, 16))
+        for (h, a, b) in H:
+            c0, c1 = 8 * h, 8 * h + 8
+            absdiff([p for p in plan(YPLAN[t]) if p[1] // 128 == h], A("xcb"), "nu", "yb", lambda h, x, y: A("nx%d" % h, x + 1, y + 1), False, "ya", 16.0)
+            k = A("ps%d" % (2 + h), 256, 384)
+            pe(k, [(k, A("R", 0, 128), A("ksr"))] + [(k, A("S", r * 128, r * 128 + 128), line("ya%d" % h, r)) for r in range(16)])
+            tt(A("cm%d" % h), k, A("akey"), OP.is_le)
+            scan(A("cn", a, b), A("rcnt"), A("cm%d" % h), 0.0, OP.mult, OP.add)
+            scan(A("kx", a, b), A("rmax"), k, -4.0e7, OP.min, OP.max)
+        ts(A("rec"), A("cn", 15, 256, 16), float(NEED), OP.is_ge)
+        cp(A("recb"), A("rec"))
+        ts(A("kj", 16, 32), A("kx", 15, 256, 16), 15, OP.bitwise_and)
+        head[0] = 0.0
+        if t < RO - 1:
+            cues(t + 1)
+            cnt = A("ps3", 384, 400)
+            pe(cnt, [(cnt, A("oneb"), A("recb"))])
+            total_of(A("acol"), cnt)
+            ts(A("nrec"), A("rec"), -1.0, OP.mult, 1.0, OP.add)
+            tt(A("gT"), A("loL", 0, 16), A("nrec"), OP.max)
+            sel(1, A("elf"), A("gT"), A("dE", 0, 16))
+            scat(A("gist"), A("of", 16, 32), A(z))
+        F = A("ps4", 0, 256)
+        jp = A("ps4", 256, 512)
+        pe(jp, [(jp, A("id16"), A("jh"))])
+        pe((None, ("ps4", 0, 512, 1)), [(F, A("nb16"), A("one16", 0, 256))], True, False)
+        for (h, a, b) in H:
+            fh = A("ps4", a, b)
+            terms = [(fh, A("S", r * 128, r * 128 + 128), A("fa%d" % h, r, 2048, 16)) for r in range(16)]
+            if FPLAN[h] == "S":
+                for x in (0, 1024):
+                    act(A("fa%d" % h, x, x + 1024), A(zr, h * 2048 + x, h * 2048 + x + 1024), AF.Abs)
+            else:
+                for x in (0, 1024):
+                    ts(A("fa%d" % h, x, x + 1024), A(zr, h * 2048 + x, h * 2048 + x + 1024), 0.0, OP.max, 2.0, OP.mult)
+                terms += [(fh, A("NS", r * 128, r * 128 + 128), A(zr, h * 2048 + r, h * 2048 + 2048, 16)) for r in range(16)]
+            pe(fh, terms, False, False)
+        ts(A("rec"), A("rec"), 16.0, OP.mult)
+        tt(A("jr"), A("kj", 16, 32), A("rec"), OP.add)
+        spread("ps5", 256, A("jr"))
+        act(A("rB"), A("ps5", 256, 512), AF.Relu, 1.0, -15.0)
+        ts(A("oh"), A("ps5", 256, 512), A("kcol"), OP.is_equal)
+        tt(A("pj"), A("ps4", 256, 512), A("oh"), OP.mult)
+        pe(F, [(F, A("k1b"), A("rB"))], False, True)
+        dp, ib = A("ps6", 0, 256), A("ps6", 256, 512)
+        pe(ib, [(ib, A("bo16"), A("pj")), (ib, A("k1b"), A("rB"))])
+        cp(A("IB"), ib)
+        pe(dp, [(dp, A("sh16"), A("jh")), (dp, A("ni16"), A("nh"))])
+        tt(A("dl"), dp, A("oh"), OP.mult)
+        v = A("v16%d" % (t & 1))
+        hp, hm = A("ps6", 0, 256), A("ps6", 256, 512)
+        pe(hp, [(hp, A("hi16"), v), (hp, A("hi16"), A("jh"))])
+        act(A("ja"), hp, AF.Copy)
+        pe(hm, [(hm, A("hi16"), v), (hm, A("nh16"), A("jh"))])
+        act(A("mk"), F, AF.Sign)
+        tt(A("pn"), hm, A("mk"), OP.mult)
+        if t == 0:
+            for x in range(0, E, 512):
+                gcp(A("nm", x, x + 512), A("ixi", x, x + 512))
+            for x in range(0, W, 512):
+                gcp(A("lkt", x, x + 512), A("lki", x, x + 512))
+        scat(A("nm"), A("of", 0, 16), A("pn"), A("ja"))
+        collect(A("ps5", 48, 64), "pj", 0)
+        cp(A("ILu"), A("ps5", 48, 64))
+        ts(A("dT", 48, 64), A("rec"), 128.0, OP.mult)
+        tt(A("IL"), A("ps5", 48, 64), A("dT", 48, 64), OP.add)
+        gatop(A("nl"), A("lkt", 0, W), A("ILu"), A("dl"), OP.add)
+        tt(A("dE", 16, 32), A("lane", 16, 32), A("IL"), OP.subtract)
+        ts(A("dE", 16, 32), A("dE", 16, 32), 0.0625, OP.mult)
+        firsts("IB", "IL", "eq2", 256, 96, (A("k1b"), A("rB")))
+        sel(2, A("IL"), A("ps5", 96, 112), A("dE", 16, 32))
+        scat(A("lkt"), A("of", 32, 48), A("nl"))
+    dma("Y", T.yz[:], T.zfin[:], 2.5, [], [("zfin", 0, 256, 1)])
+    dma("Y", T.yi[:], T.nm[:, 0:E], 5.0, [], [("nm", 0, E, 1)])
+    dma("Y", T.yl[:], T.lkt[:, 0:W], 3.5, [], [("lkt", 0, W, 1)])
+
+    n = len(ops)
+    users = [[] for _ in range(n)]
+    for o in ops:
+        for d in o["deps"]:
+            users[d].append(o["i"])
+    way = [0.0] * n
+    for i in range(n - 1, -1, -1):
+        o = ops[i]
+        way[i] = o["cost"] + o["lat"] + max([way[j] + WAKE for j in users[i]] + [0.0])
+    queue, cost = [o["q"] for o in ops], [o["cost"] for o in ops]
+    tail = [o["cost"] + o["lat"] for o in ops]
+    then = [[(j, tail[i] + WAKE if ops[j]["deps"][i] else 1e-6) for j in users[i]] for i in range(n)]
+    npre = [len(o["deps"]) for o in ops]
+
+    def place(key):
+        left, avail, start, order = list(npre), [0.0] * n, [0.0] * n, []
+        free, ready = {q: 0.0 for q in queues}, {q: [] for q in queues}
+        for i in range(n):
+            if left[i] == 0:
+                ready[queue[i]].append(i)
+        while len(order) < n:
+            m, q = 1e18, None
+            for x in ready:
+                if ready[x]:
+                    y = max(free[x], min(avail[i] for i in ready[x]))
+                    if y < m:
+                        m, q = y, x
+            i = max((j for j in ready[q] if avail[j] <= m + LOOK), key=lambda j: key[j])
+            s = start[i] = max(avail[i], free[q])
+            free[q] = s + cost[i]
+            ready[q].remove(i)
+            order.append(i)
+            for j, w in then[i]:
+                left[j] -= 1
+                if s + w > avail[j]:
+                    avail[j] = s + w
+                if left[j] == 0:
+                    ready[queue[j]].append(j)
+        return start, order, max(start[i] + tail[i] for i in range(n))
+
+    if n not in ORDER:
+        key = [way[i] + ops[i]["head"] for i in range(n)]
+        best = place(key)
+        rng = np.random.RandomState(5)
+        for k in range(TRIES):
+            nk = [float(x) for x in np.array(key) + (rng.rand(n) < (0.02, 0.1, 0.4)[k % 3]) * rng.randn(n) * (0.5, 2.0, 6.0)[(k // 3) % 3]]
+            new = place(nk)
+            if new[2] <= best[2]:
+                key, best = nk, new
+        ORDER[n] = best
+    start, order, _span = ORDER[n]
+    fin = [start[i] + tail[i] for i in range(n)]
+
+    know = {q: {} for q in queues}
+    clock = [None] * n
+    count = {q: 0 for q in queues}
+    total = {}
+    for i in order:
+        o = ops[i]
+        q = o["q"]
+        k = know[q]
+        for d in sorted(o["deps"]):
+            if not o["deps"][d]:
+                continue
+            sem, val, ck = clock[d]
+            if k.get(sem, 0) < val:
+                queues[q].wait_ge(T.sem[sem], val)
+                k[sem] = val
+                for s2, v2 in ck.items():
+                    if k.get(s2, 0) < v2:
+                        k[s2] = v2
+        ck = dict(k)
+        inst = None
+        for f in o["calls"]:
+            inst = f()
+        if o["kind"] == "c":
+            count[q] += 1
+            inst.then_inc(T.sem["e" + q], 1)
+            clock[i] = ("e" + q, count[q], ck)
+            total["e" + q] = count[q]
+        elif o["kind"] == "d":
+            inst.then_inc(T.sem[o["sem"]], 16)
+            clock[i] = (o["sem"], 16, ck)
+            total[o["sem"]] = 16
+        else:
+            clock[i] = (o["sem"], o["val"], {})
+            total[o["sem"]] = o["val"]
+            total["snd"] = total.get("snd", 0) + o["val"]
+    for sem in sorted(total):
+        if know["G"].get(sem, 0) < total[sem]:
+            g.wait_ge(T.sem[sem], total[sem])

@@ -1,44 +1,48 @@
 import numpy as np
-from concourse.mybir import AluOpType as OP, ActivationFunctionType as AF, AxisListType as AX
+from concourse.bass import DstId, RemoteDMATransfer
+from concourse.mybir import AluOpType as OP, ActivationFunctionType as AF
 
-W, E, B, RO, NEED = 1024, 2048, 256, 3, 11
-NENG = 4
-GPLAN = ("SVSV", "SVSV", "VSVS")
-YPLAN = ("SVSV", "SSSV", "SVSV")
-ZPLAN = ("VVVV", "VGVG", "VVVG")
-FPLAN = "SS"
-TRIES, ORDER = 2000, {}
-HEAD, HZ, HC, LOOK = 0.0, 2.0, 6.0, 0.04
+W, E, B, RO = 1024, 2048, 256, 3
+NENG = 8
+GPLAN = ("VSVSSVSV", "VSVSSVSV", "VSVSSVSV")
+PCUT = 32
+YPLAN = ("VVVV", "VVVV", "VVVV")
+YABS = ("SS", "SS", "SS")
+FABS = ("SS", "SS", "SS")
+ZMAX = ("pp", "pp", "dd")
+ZPLAN = ("VG", "G", "G")
+HENG, RENG, HLAT = 8, 16, 12.0
+FCUT = 1024
+TRIES, ORDER = 11000, {}
+HZ, HC, LEAN, SLACK, SEED = 0.0, 0.0, 1.5, 0.3, 5
 F32, BF, F16, I32, U16 = "float32", "bfloat16", "float16", "int32", "uint16"
 
 SCRATCH = {
-    "gist": ("sbuf", [128, E + B], BF), "nm": ("sbuf", [128, E + B], F32), "lkt": ("sbuf", [128, W + B], F32),
-    "xcb": ("sbuf", [128, W], BF), "ixi": ("sbuf", [128, E], I32), "lki": ("sbuf", [128, W], I32),
+    "gist": ("sbuf", [128, E + B], BF), "nm": ("sbuf", [128, E + B], F32), "ixi": ("sbuf", [128, E + B], I32),
+    "pt": ("sbuf", [128, W + B], F32), "lkt": ("sbuf", [128, W + B], F32), "xw": ("sbuf", [128, W], BF),
+    "xcb": ("sbuf", [128, W], BF), "lki": ("sbuf", [128, W], I32),
     "wti": ("sbuf", [128, 1], I32), "hki": ("sbuf", [128, 2], I32), "thi": ("sbuf", [128, 2], I32),
     "zin0": ("sbuf", [128, B], BF), "zin1": ("sbuf", [128, B], BF), "zin2": ("sbuf", [128, B], BF), "zfin": ("sbuf", [128, B], BF),
     "zo0": ("sbuf", [128, B], BF), "zo1": ("sbuf", [128, B], BF), "zo2": ("sbuf", [128, B], BF),
-    "S": ("sbuf", [128, 2048], BF), "SF": ("sbuf", [128, 2048], F16), "SW": ("sbuf", [128, 2048], BF), "D": ("sbuf", [128, 2048], F16), "R": ("sbuf", [128, 2048], F16),
-    "NS": ("sbuf", [128, 2048], BF), "rz": ("sbuf", [128, 2048], BF), "zr0": ("sbuf", [128, 4096], BF), "zr1": ("sbuf", [128, 4096], BF),
-    "eq": ("sbuf", [128, 16, 256], BF), "eq2": ("sbuf", [128, 16, 256], BF),
+    "R": ("sbuf", [128, 2048], F16), "DP": ("sbuf", [128, 2048], F16), "rz": ("sbuf", [128, 1024], BF),
+    "zr0": ("sbuf", [128, 4096], BF), "zr1": ("sbuf", [128, 4096], BF), "zq0": ("sbuf", [128, 2, 512], BF), "zq1": ("sbuf", [128, 2, 512], BF),
+    "eq": ("sbuf", [128, 16, 256], BF), "eq2": ("sbuf", [128, 16, 256], BF), "ei": ("sbuf", [128, 16, 16], I32),
+    "ksl": ("sbuf", [128, 2, 32], I32), "c192": ("sbuf", [128, FCUT], BF),
 }
 for _k in (0, 1):
-    for _n, _d, _w in (("gd", BF, 2048), ("fa", BF, 2048), ("nx", BF, 2064), ("lg", F16, 2048), ("yb", BF, 2048), ("zs", BF, 2048)):
+    for _n, _d, _w in (("gd", BF, 2048), ("ga", BF, 2048), ("px", F32, 2064), ("yd", BF, 2048), ("ya", BF, 2048), ("fa", BF, 2048), ("zs", F16, 2048),
+                       ("km", I32, 136), ("kc", F32, 136)):
         SCRATCH["%s%d" % (_n, _k)] = ("sbuf", [128, _w], _d)
-    SCRATCH["aa%d" % _k] = ("sbuf", [128, 8, 16, 16], BF)
-    SCRATCH["ya%d" % _k] = ("sbuf", [128, 8, 16, 16], BF)
 _SMALL = {
-    F32: (("wtf", 1), ("hkf", 2), ("thf", 2), ("one", 128), ("idf", 128), ("blk", 128), ("wblk", 128), ("zer", 128), ("pm64", 64), ("pm32", 32), ("pm", 16), ("im", 16),
-          ("half", 16), ("zero", 16), ("pw", 16), ("tw", 16), ("tr", 16), ("wcol", 1), ("rcol", 1), ("kcol", 1), ("thr", 256), ("lane", 32), ("lan0", 16),
-          ("pd", 32), ("akey", 128), ("rmin", 128), ("rmax", 128), ("xe", 256), ("xq", 256), ("e0", 256), ("elf", 16),
-          ("ja", 256), ("rec", 16), ("nrec", 16), ("acol", 1), ("loL", 16), ("dE", 32), ("dT", 64), ("oT", 64), ("gT", 16),
-          ("IL", 16), ("dl", 256), ("nl", 256), ("pn", 256)),
-    F16: (("id16", 128), ("ni16", 128), ("hi16", 128), ("nh16", 128), ("sh16", 128), ("bo16", 128), ("nb16", 128), ("one16", 512), ("r0k", 128), ("prow", 128), ("imr", 128), ("c8k", 128),
-          ("ksr", 128), ("cf", 48), ("v160", 256), ("v161", 256), ("elh", 16), ("jh", 256), ("nh", 256), ("jr", 16), ("eB", 256), ("IB", 256), ("lo", 512),
-          ("oh", 256), ("pj", 256)),
-    BF: (("idb", 128), ("nib", 128), ("k1b", 128), ("oneb", 128), ("wd", 128), ("bo4", 128), ("rcnt", 128), ("ze", 256), ("cm0", 128), ("cm1", 128), ("cn", 256),
-         ("recb", 16), ("rB", 256), ("mk", 256)),
-    I32: (("kx", 256), ("km0", 128), ("km1", 128), ("ui", 32), ("sq", 16), ("cmb0", 48), ("cmb1", 48), ("bs", 16), ("ei", 256), ("ej", 256), ("vi", 256), ("vj", 256), ("ki", 64), ("el", 16), ("kj", 32)),
-    U16: (("e16", 256), ("elu", 16), ("ju", 256), ("nu", 256), ("of", 64), ("ILu", 16)),
+    F32: (("wtf", 1), ("hkf", 2), ("thf", 2), ("one", 128), ("idf", 128), ("blk", 128), ("i4k", 128), ("bm4", 8), ("pd", 16), ("pB", 16), ("pw", 16), ("half", 16), ("zero", 16),
+          ("tw", 16), ("wcol", 1), ("rcol", 1), ("kcol", 1), ("ccol", 2), ("wb", 1), ("dmp", 32), ("lcol", 2), ("msk", 512), ("rmin", 128), ("rmax", 128), ("xq", 256),
+          ("X0", 256), ("X1", 256), ("elf", 16), ("of0", 16), ("oT", 32), ("own", 16), ("acol", 1), ("junk", 16), ("dl", 256), ("nl", 256), ("nn", 256), ("fr", 256)),
+    F16: (("id16", 128), ("ni16", 128), ("hi16", 128), ("nh16", 128), ("sh16", 128), ("one16", 512), ("z16", 128), ("dP", 128), ("dA", 128), ("dB", 256), ("dmh", 32),
+          ("cf0", 48), ("cf1", 48), ("v16", 256), ("elh", 16), ("jh", 256), ("nh", 256), ("sl", 32), ("eB", 256), ("IB", 256), ("oh", 256), ("pn", 256), ("Xh", 256), ("b16", 8)),
+    BF: (("idb", 128), ("nib", 128), ("n2b", 128), ("k2b", 128), ("n4k", 128), ("c2k", 128), ("oneb", 128), ("dM", 128), ("dC", 128), ("wd", 128), ("bo4", 128), ("rcnt", 128), ("thr", 256),
+         ("U", 144), ("UW", 144), ("cw", 48), ("zpl", 256), ("c24", 128), ("zn", 256), ("ze", 256), ("qx", 256), ("sg", 256), ("cn", 256), ("rT", 256), ("mk", 256), ("lo", 512)),
+    I32: (("pi", 256), ("pj", 256), ("ui", 32), ("sq", 16), ("cb0", 48), ("cb1", 48), ("bs", 16), ("ej", 256), ("vi", 256), ("vj", 256), ("ki", 64), ("el", 16), ("ij", 32)),
+    U16: (("xl", 16), ("e16", 256), ("elu", 16), ("ju", 256), ("nu", 256), ("of", 64), ("ILu", 16)),
 }
 PLACE = {}
 for _d, _a in ((F32, "fA"), (F16, "hA"), (BF, "bA"), (I32, "iA"), (U16, "uA")):
@@ -49,16 +53,32 @@ for _d, _a in ((F32, "fA"), (F16, "hA"), (BF, "bA"), (I32, "iA"), (U16, "uA")):
     SCRATCH[_a] = ("sbuf", [128, _at], _d)
 for _k in range(8):
     SCRATCH["ps%d" % _k] = ("psum", [128, 512], F32)
-NDMA = 20
-SEMAPHORES = ["eV", "eS", "eP", "eG", "snd", "arr1", "arr2", "arr3"] + ["d%d" % k for k in range(NDMA)]
+NDMA = 44
+SEMAPHORES = ["eV", "eS", "eP", "eG", "snd", "arr1", "arr2", "arr3"] + ["d%d" % k for k in range(NDMA)] + ["%s%d" % (s, k) for s in ("out", "ret") for k in range(12)]
 
-CY = 0.00083 * 1.15
-GA, SC, PEC, VO, WAKE = 1.4, 3.0, 0.0005, 0.03, 0.06
+CY = 0.00083 * 1.1
+GA, SC, PEC, VO, SO, WAKE, DL = 1.4, 3.0, 0.00052, 0.035, 0.08, 0.09, 1.2
+EST = []
 
 
 def rank_program(g, core, T, topo):
+    def helper_of(c):
+        mates = [x for x in topo.cores_of(c) if topo.die(x) == topo.die(c)]
+        return [x for x in mates if T.rank_of(x) is None][[x for x in mates if T.rank_of(x) is not None].index(c)]
+
+    def bits(src, dst, lo, hi):
+        return sum(1 << e for e in topo.engines(src, dst)[lo:hi])
+
+    folds = [(t, x) for t in range(RO) for x in range(0, 4096, FCUT) if FABS[t][x // 2048] == "H"]
     rank = T.rank_of(core)
     if rank is None:
+        for home in [c for c in T.cores if helper_of(c) == core]:
+            rid, pid, _se = topo.addr(home)
+            for k, (t, x) in enumerate(folds):
+                g.wait_ge(T.sem["out%d" % k], HENG)
+                g.remote_dma(T["fa%d" % (x // 2048)][:, x % 2048:x % 2048 + FCUT], T.zr0[:, x:x + FCUT], T.sem["ret%d" % k], T.sem.snd, pid, rid, bits(core, home, 0, RENG))
+            if folds:
+                g.wait_ge(T.sem.snd, RENG * len(folds))
         return
     ops, hist, head = [], {}, [0.0]
     queues = {"V": g.vector, "S": g.scalar, "P": g.tensor, "G": g, "Y": g.sync}
@@ -68,7 +88,12 @@ def rank_program(g, core, T, topo):
             name, at, w = PLACE[name]
             lo, hi = at + lo, at + (w if hi is None else hi)
         hi = T[name].shape[1] if hi is None else hi
-        return (T[name][:, lo:hi] if step == 1 else T[name][:, lo:hi:step], (name, lo, hi, step))
+        return (T[name][:, lo:hi] if step == 1 else T[name][:, lo:hi:step], (name, lo, hi, step), (hi - lo + step - 1) // step)
+
+    def A3(name, i0, i1, a, b):
+        w = SCRATCH[name][1][2]
+        ap = T[name][:, i0, a:b] if i1 == i0 + 1 else T[name][:, i0:i1, a:b]
+        return (ap, (name, i0 * w + a, (i1 - 1) * w + b, 1), (i1 - i0) * (b - a))
 
     def meets(a, b):
         if a[1] >= b[2] or b[1] >= a[2]:
@@ -76,40 +101,44 @@ def rank_program(g, core, T, topo):
         return not (a[3] == b[3] and a[3] > 1 and a[1] % a[3] != b[1] % b[3])
 
     def add(q, calls, w, r, cost, lat=0.0, kind="c", sem=None, val=1):
-        o = {"q": q, "calls": calls, "cost": cost, "lat": lat, "kind": kind, "sem": sem, "val": val, "deps": {}, "i": len(ops), "head": head[0]}
+        o = {"q": q, "calls": calls, "cost": cost, "lat": lat, "kind": kind, "sem": sem, "val": val, "deps": {}, "i": len(ops), "head": head[0], "w": w}
         for regs, isw in ((r, False), (w, True)):
             for reg in regs:
                 ps = reg[0][:2] == "ps"
                 for (p, preg, pw) in hist.setdefault(reg[0], []):
-                    same = p["q"] == q and p["kind"] == "c" and kind == "c"
+                    same = p["q"] == q and len(q) == 1 and p["kind"] == "c" and kind == "c"
                     if ps and not same:
                         o["deps"][p["i"]] = True
-                    elif meets(reg, preg) and (isw or pw):
+                    elif (ps and q == "P") or (meets(reg, preg) and (isw or pw)):
                         need = not (same and q == "P")
                         o["deps"][p["i"]] = o["deps"].get(p["i"], False) or need
         for regs, isw in ((r, False), (w, True)):
             for reg in regs:
                 h = hist[reg[0]]
-                if isw and reg[3] == 1 and reg[0][:2] != "ps":
+                if reg[0][:2] == "ps":
+                    if q == "P":
+                        h[:] = []
+                elif isw and reg[3] == 1 and len(reg) == 4:
                     h[:] = [x for x in h if not (x[0] is not o and x[1][1] >= reg[1] and x[1][2] <= reg[2])]
                 h.append((o, reg, isw))
         ops.append(o)
 
-    def vcost(n, f=1.0):
+    def dty(x):
+        return SCRATCH[x[1][0]][2]
+
+    def vcost(n, *xs):
+        f = 0.5 if xs and all(dty(x) in (BF, F16, U16) for x in xs) else 1.0
         return VO + max(64.0, n * f) * CY
 
-    def width(x):
-        return (x[1][2] - x[1][1] + x[1][3] - 1) // x[1][3]
-
-    def fast(*xs):
-        return 0.5 if all(SCRATCH[x[1][0]][2] in (BF, F16, U16) for x in xs) else 1.0
+    def part(o):
+        return o[1] if o[1][3] > 1 or o[1][2] - o[1][1] == o[2] else o[1] + (0,)
 
     def cp(o, i):
-        add("V", [lambda: g.vector.tensor_copy(o[0], i[0])], [o[1]], [i[1]], vcost(width(i), fast(o, i)))
+        add("V", [lambda: g.vector.tensor_copy(o[0], i[0])], [part(o)], [i[1]], vcost(i[2], o, i))
 
     def tt(o, a, b, op):
-        f = 1.0 if a[1][0][:2] == "ps" or b[1][0][:2] == "ps" else 2.0
-        add("V", [lambda: g.vector.tensor_tensor(o[0], a[0], b[0], op)], [o[1]], [a[1], b[1]], vcost(width(a), f))
+        f = 1 if a[1][0][:2] == "ps" or b[1][0][:2] == "ps" else 2
+        add("V", [lambda: g.vector.tensor_tensor(o[0], a[0], b[0], op)], [part(o)], [a[1], b[1]], vcost(a[2] * f))
 
     def ts(o, a, s1, op0, s2=None, op1=None):
         r = [a[1]] + [s[1] for s in (s1, s2) if isinstance(s, tuple)]
@@ -119,52 +148,71 @@ def rank_program(g, core, T, topo):
             f = lambda: g.vector.tensor_scalar(o[0], a[0], x1, None, op0)
         else:
             f = lambda: g.vector.tensor_scalar(o[0], a[0], x1, x2, op0, op1)
-        add("V", [f], [o[1]], r, vcost(width(a), fast(o, a)))
+        add("V", [f], [part(o)], r, vcost(a[2], o, a))
 
     def ms(o, v):
-        add("V", [lambda: g.vector.memset(o[0], v)], [o[1]], [], vcost(width(o), fast(o)))
+        add("V", [lambda: g.vector.memset(o[0], v)], [o[1]], [], vcost(o[2], o))
 
     def scan(o, d0, d1, init, op0, op1):
-        add("V", [lambda: g.vector.tensor_tensor_scan(o[0], d0[0], d1[0], init, op0, op1)], [o[1]], [d0[1], d1[1]], vcost(width(d1), fast(o, d0, d1)))
+        add("V", [lambda: g.vector.tensor_tensor_scan(o[0], d0[0], d1[0], init, op0, op1)], [o[1]], [d0[1], d1[1]], vcost(d1[2], o, d0, d1))
 
-    def total_of(o, i):
-        add("V", [lambda: g.vector.tensor_reduce(o[0], i[0], AX.X, OP.add)], [o[1]], [i[1]], vcost(width(i)))
-
-    def act(o, i, func, scale=1.0, bias=0.0):
-        r = [i[1]] + ([scale[1]] if isinstance(scale, tuple) else [])
+    def act(o, i, func=AF.Copy, scale=1.0, bias=0.0, total=None):
+        r = [i[1]] + [s[1] for s in (scale, bias) if isinstance(s, tuple)]
         sc = scale[0] if isinstance(scale, tuple) else scale
-        add("S", [lambda: g.scalar.activation(o[0], i[0], func, bias, sc)], [o[1]], r, 0.07 + width(i) * CY)
-
-    def gat(q, o, win, off, scale=1.0):
-        if q == "V":
-            f = lambda: g.vector.tensor_copy(o[0], win[0].indirect(off[0]))
+        bi = bias[0] if isinstance(bias, tuple) else bias
+        if total is None:
+            f = lambda: g.scalar.activation(o[0], i[0], func, bi, sc)
         else:
-            f = lambda: g.scalar.activation(o[0], win[0].indirect(off[0]), AF.Copy, 0.0, scale)
-        add(q, [f], [o[1]], [win[1], off[1]], 0.07 + 16 * width(off) * GA * CY)
+            f = lambda: g.scalar.activation(o[0], i[0], func, bi, sc, accum_out=total[0])
+        add("S", [f], [part(o)] + ([total[1]] if total else []), r, SO + i[2] * CY + (0.02 if total else 0.0))
+
+    def either(alts, w, r):
+        add("".join(alts), None, w, r, min(c for _f, c in alts.values()))
+        ops[-1]["alts"] = alts
+
+    def conv(o, i, scale=1.0, bias=0.0, qs="VS"):
+        r = [i[1]] + [s[1] for s in (scale, bias) if isinstance(s, tuple)]
+        sc = scale[0] if isinstance(scale, tuple) else scale
+        bi = bias[0] if isinstance(bias, tuple) else bias
+        plain = not isinstance(scale, tuple) and not isinstance(bias, tuple) and scale == 1.0 and bias == 0.0
+        alts = {"V": ((lambda: g.vector.tensor_copy(o[0], i[0])) if plain else (lambda: g.vector.tensor_scalar(o[0], i[0], sc, bi, OP.mult, OP.add)), vcost(i[2], o, i)),
+                "S": (lambda: g.scalar.activation(o[0], i[0], AF.Identity if isinstance(bias, tuple) else AF.Copy, bi, sc), SO + i[2] * CY),
+                "G": (lambda: g.affine_select(o[0], i[0], [[1, o[2]]], OP.is_ge, 0.0, 1, 0), 0.2 + 2 * o[2] * CY)}
+        either({q: alts[q] for q in qs}, [part(o)], r)
+
+    def gcp(o, i):
+        conv(o, i, qs="VSG")
+
+    def gat(qs, o, win, off, scale=1.0, bias=0.0):
+        c = 0.07 + 16 * off[2] * GA * CY
+        alts = {"V": (lambda: g.vector.tensor_copy(o[0], win[0].indirect(off[0])), c),
+                "S": (lambda: g.scalar.activation(o[0], win[0].indirect(off[0]), AF.Copy, bias, scale), c)}
+        either({q: alts[q] for q in qs}, [o[1]], [win[1], off[1]])
 
     def gatop(o, win, off, b, op):
-        add("V", [lambda: g.vector.tensor_tensor(o[0], win[0].indirect(off[0]), b[0], op)], [o[1]], [win[1], off[1], b[1]], 0.07 + 16 * width(off) * GA * CY)
+        add("V", [lambda: g.vector.tensor_tensor(o[0], win[0].indirect(off[0]), b[0], op)], [o[1]], [win[1], off[1], b[1]], 0.07 + 16 * off[2] * GA * CY)
 
-    def pe(out, terms, first=True, last=True):
-        calls, regs, n, c = [], [], len(terms), 0.05
+    def scat(win, off, src, src2=None):
+        if src2 is None:
+            f = lambda: g.vector.tensor_copy(win[0].indirect(off[0]), src[0])
+        else:
+            f = lambda: g.vector.tensor_tensor(win[0].indirect(off[0]), src[0], src2[0], OP.add)
+        add("V", [f], [win[1] + (0,)], [off[1], src[1]] + ([src2[1]] if src2 else []), 0.06 + src[2] * SC * CY)
+
+    def pe(terms, first=True, last=True, each=False):
+        calls, regs, n, c = [], [], len(terms), 0.0
         for k, (po, l, r) in enumerate(terms):
-            calls.append(lambda po=po, l=l, r=r, k=k: g.tensor.matmul(po[0], l[0], r[0], first and k == 0, last and k == n - 1))
+            go, end = (k % each == 0, k % each == each - 1) if each else (first and k == 0, last and k == n - 1)
+            calls.append(lambda po=po, l=l, r=r, go=go, end=end: g.tensor.matmul(po[0], l[0], r[0], go, end))
             regs += [l[1], r[1]]
-            c += max(64, width(po)) * PEC
-        add("P", calls, [out[1]], sorted(set(regs)), c)
+            c += max(64, po[2]) * PEC * (4 if dty(l) == F32 else 1)
+        add("P", calls, [terms[0][0][1]], sorted(set(regs)), c, 0.05)
 
-    def spread(out_name, lo, src):
-        calls, regs = [], [src[1]]
-        w = 16 * width(src)
-        for rho in range(16):
-            po = A(out_name, lo + rho, lo + w, 16)
-            l = A("R", rho * 128, rho * 128 + 128)
-            calls.append(lambda po=po, l=l: g.tensor.matmul(po[0], l[0], src[0], True, True))
-            regs.append(l[1])
-        add("P", calls, [(out_name, lo, lo + w, 1)], regs, 0.05 + 16 * 64 * PEC)
+    def spread(bank, lo, src):
+        return [(A(bank, lo + r, lo + 16 * src[2], 16), A("R", r * 128, r * 128 + 128), src) for r in range(16)]
 
-    def collect(out, src, lo):
-        pe(out, [(out, A("SF", rho * 128, rho * 128 + 128), A(src, lo + rho, lo + 256, 16)) for rho in range(16)])
+    def shifted(name, r):
+        return A(name, 15 - r, 143 - r)
 
     dn = [0]
 
@@ -172,7 +220,7 @@ def rank_program(g, core, T, topo):
         sem = "d%d" % dn[0]
         dn[0] += 1
         if acc:
-            f = lambda: g.dma_start(o, i, accum_op=OP.add, max_dma_last_dim=4096)
+            f = lambda: g.dma_start(o, i, accum_op=OP.add)
         else:
             f = lambda: queues[q].dma_start(o, i)
         add(q, [f], regs_w, regs_r, 1.0 if q == "G" else 0.1, lat, "d", sem, 16)
@@ -181,263 +229,246 @@ def rank_program(g, core, T, topo):
         a = A(name, 0, hi)
         dma(q, a[0], T[src][:], lat, [a[1]], [])
 
+    def addto(o, i, lat):
+        dma("G", o[0], i[0], lat * DL, [o[1]], [o[1], i[1]], acc=True)
+
+    def aff(o, i, pat, op, base, cm, fill=0.0):
+        add("G", [lambda: g.affine_select(o[0], i[0], pat, op, fill, base, cm)], [o[1]], [i[1]], 0.2 + 2 * i[2] * CY)
+
+    def iot(o, pat, base, cm):
+        if dty(o) == I32:
+            f = lambda: g.iota(o[0], pat, base, cm)
+        else:
+            f = lambda: g.iota(o[0], pat, base, cm, allow_small_or_imprecise_dtypes=True)
+        add("G", [f], [o[1]], [], 0.16 + 2 * o[2] * CY)
+
     load("Y", "hki", "hk", 2.2)
     load("S", "wti", "wt", 2.2)
     load("Y", "zin0", "zc", 2.4)
     load("S", "thi", "th", 2.4)
-    load("Y", "gist", "gi", 4.0, E)
-    load("Y", "ixi", "ix", 6.0)
-    load("Y", "lki", "lk", 7.0)
-    load("Y", "xcb", "xc", 8.0)
+    load("Y", "lki", "lk", 4.0)
+    load("Y", "gist", "gi", 5.3, E)
+    load("Y", "ixi", "ix", 7.5, E)
+    load("Y", "xcb", "xc", 8.5)
 
-    def aff(o, i, pat, op, base, cm, fill=0.0):
-        add("G", [lambda: g.affine_select(o[0], i[0], pat, op, fill, base, cm)], [o[1]], [i[1]], 0.2 + 2 * width(i) * CY)
-
-    def gcp(o, i):
-        add("G", [lambda: g.affine_select(o[0], i[0], [[1, width(o)]], OP.is_ge, 0.0, 1, 0)], [o[1]], [i[1]], 0.2 + 2 * width(o) * CY)
-
-    def iot(o, pat, base, cm):
-        add("G", [lambda: g.iota(o[0], pat, base, cm, allow_small_or_imprecise_dtypes=True)], [o[1]], [], 0.16 + 2 * width(o) * CY)
-
-    def rep(name, n, w, cp=cp):
-        k = w
-        while k < n:
-            cp(A(name, k, 2 * k), A(name, 0, k))
-            k *= 2
-
-    head[0] = 80.0
+    blk8 = A("blk", 0, 128, 16)
     ms(A("one"), 1.0)
-    head[0] = 70.0
-    ms(A("one16"), 1.0)
-    ms(A("SW"), 0.0)
-    head[0] = 0.0
-    for k in range(0, 2048, 512):
-        ms(A("S", k, k + 512), 0.0)
-    head[0] = 60.0
+    ms(A("UW"), 0.0)
     aff(A("blk"), A("one"), [[-16, 8], [0, 16]], OP.is_ge, 0, 1)
     aff(A("blk"), A("blk"), [[16, 8], [0, 16]], OP.is_ge, 15, -1)
+    iot(A("pi", 0, 16), [[-1, 16]], 16, 1)
     aff(A("idf"), A("one"), [[-1, 128]], OP.is_equal, 0, 1)
-    tt(A("pm64"), A("idf", 0, 64), A("idf", 64, 128), OP.add)
-    tt(A("pm32"), A("pm64", 0, 32), A("pm64", 32, 64), OP.add)
-    tt(A("pm"), A("pm32", 0, 16), A("pm32", 16, 32), OP.add)
     cp(A("wtf"), A("wti"))
-    ts(A("wblk"), A("blk"), A("wtf"), OP.mult)
-    for k in range(0, 16, 2):
-        cp(A("SW", k * 129, k * 128 + 128, 16), A("wblk", 0, 128, 16))
-        act(A("SW", k * 129 + 129, k * 128 + 256, 16), A("blk", 0, 128, 16), AF.Copy, A("wtf"))
-    head[0] = 0.0
-    for k in range(16):
-        act(A("S", k * 129, k * 128 + 128, 16), A("blk", 0, 128, 16), AF.Copy)
+    ts(A("UW", 15, 143, 16), blk8, A("wtf"), OP.mult)
     cp(A("hkf"), A("hki"))
-    cp(A("thf"), A("thi"))
-    head[0] = 60.0
+    ts(A("pj", 0, 16), A("pi", 0, 16), 15, OP.bitwise_and)
+    ts(A("pd"), A("pj", 0, 16), 0.0, OP.is_equal, A("hkf", 0, 1), OP.mult)
+    pe([(A("ps5", 0, 16), A("blk"), A("pd"))])
+    conv(A("pB"), A("ps5", 0, 16))
+    conv(A("id16"), A("idf"))
+    for m in range(16):
+        conv(A("DP", m * 128, m * 128 + 128), A("id16"), A("pB", m, m + 1))
+    ms(A("one16"), 1.0)
+    ms(A("z16"), 0.0)
     for k in range(0, 16, 4):
         aff(A("R", k * 128, k * 128 + 512), A("one16"), [[-1, 4], [-16, 8], [0, 16]], OP.is_equal, -k, 1)
-    head[0] = 0.0
-    iot(A("im"), [[1, 16]], 0, 0)
-    ts(A("pd", 0, 16), A("pm"), A("hkf", 0, 1), OP.mult)
-    ts(A("pd", 16, 32), A("pm"), A("thf", 0, 1), OP.mult)
-    pe(A("ps5", 64, 96), [(A("ps5", 64, 96), A("blk"), A("pd"))])
-    cp(A("prow", 0, 16), A("ps5", 64, 80))
-    rep("prow", 128, 16)
-    cp(A("imr", 0, 16), A("im"))
-    rep("imr", 128, 16)
-    ms(A("c8k"), -8192.0)
-    ts(A("r0k"), A("R", 0, 128), 2048.0, OP.mult)
+    cp(A("rcol"), A("pj", 0, 1))
+    cp(A("thf"), A("thi"))
+    for name, c in (("idb", 1.0), ("nib", -1.0), ("n2b", -2.0), ("k2b", 2048.0), ("n4k", -4096.0), ("ni16", -1.0), ("hi16", 0.5), ("nh16", -0.5), ("i4k", 4096.0)):
+        conv(A(name), A("id16"), c)
+    aff(A("sh16"), A("one16", 0, 128), [[-1, 128]], OP.is_equal, -1, 1)
+    for k, c in enumerate((16384.0, 1.0, -32768.0, -2.0, 32768.0, -65536.0)):
+        conv(A("cw", 8 * k, 8 * k + 8), blk8, c)
+    conv(A("b16"), blk8)
+    conv(A("bm4"), blk8, -4.0)
+    conv(A("dP"), A("id16"), A("hkf", 0, 1))
+    conv(A("dM"), A("id16"), A("rcol"), -64.0)
+    ms(A("c2k"), 2048.0)
+    ms(A("oneb"), 1.0)
     ms(A("rmin"), -4.0e7)
     ms(A("rmin", 0, 128, 16), 4.0e7)
-    ms(A("zer"), 0.0)
-    for name, c, off in (("idb", 1.0, 0), ("nib", -1.0, 0), ("id16", 1.0, 0), ("ni16", -1.0, 0), ("hi16", 0.5, 0), ("nh16", -0.5, 0), ("k1b", 1024.0, 0), ("sh16", 1.0, -1)):
-        aff(A(name), A("zer"), [[-1, 128]], OP.not_equal, off, 1, c)
-    aff(A("D"), A("R"), [[1, 16], [0, 8], [-1, 16]], OP.is_equal, 0, 0)
-    ms(A("nx0", 2048, 2064), 0.0)
-    ms(A("nx1", 2048, 2064), 0.0)
-    for k in range(0, 2048, 512):
-        ms(A("rz", k, k + 512), -100.0)
-        ms(A("rz", k, k + 512, 16), 100.0)
+    iot(A("pi", 16, 32), [[16, 16]], 15, 0)
+    iot(A("pi", 24, 32), [[1, 8]], 128, 0)
+    cp(A("xl"), A("pi", 16, 32))
+    iot(A("vi", 0, 128), [[0, 8], [-1, 16]], 16, 1)
+    ts(A("vj", 0, 128), A("vi", 0, 128), 15, OP.bitwise_and)
+    ts(A("msk", 0, 128), A("vj", 0, 128), 0.0, OP.is_equal)
+    iot(A("lcol"), [[128, 2]], W, 1)
+    gcp(A("msk", 256, 384), A("msk", 0, 128))
+    for h in (0, 1):
+        conv(A("msk", 256 * h + 128, 256 * h + 256), A("msk", 0, 128), A("lcol", h, h + 1))
+    ms(A("U"), 0.0)
+    conv(A("U", 15, 143, 16), blk8, 128.0)
+    ms(A("px0", 2048, 2064), 0.0)
+    ms(A("px1", 2048, 2064), 0.0)
+    ms(A("rz"), 1000.0)
+    ms(A("rz", 0, 1024, 16), 0.0)
     ms(A("half"), 0.5)
     ms(A("zero"), 0.0)
     scan(A("pw"), A("half"), A("zero"), 2.0, OP.mult, OP.add)
-    tt(A("tw"), A("pw"), A("pm"), OP.mult)
-    total_of(A("wcol"), A("tw"))
-    tt(A("tr"), A("im"), A("pm"), OP.mult)
-    total_of(A("rcol"), A("tr"))
-    act(A("wd"), A("blk"), AF.Copy, A("wcol"))
-    act(A("bo4"), A("blk"), AF.Copy, 4.0)
-    ts(A("thr", 0, 16), A("pw"), 2.0, OP.mult)
-    rep("thr", 256, 16, gcp)
-    iot(A("lan0"), [[16, 16]], E, 0)
-    ts(A("lane", 0, 16), A("lan0"), A("rcol"), OP.add)
-    ts(A("lane", 16, 32), A("lane", 0, 16), float(E - W), OP.subtract)
+    tt(A("tw"), A("pw"), A("msk", 0, 16), OP.mult)
+    act(A("junk"), A("tw"), AF.Copy, total=A("wcol"))
+    conv(A("wd"), A("blk"), A("wcol"))
+    conv(A("bo4"), A("blk"), 4.0)
+    conv(A("thr", 0, 16), A("pw"), -2.5 / 128)
+    for k in (16, 32, 64, 128):
+        gcp(A("thr", k, 2 * k), A("thr", 0, k))
+    iot(A("dmp", 16, 32), [[16, 16]], W, 0)
+    ts(A("dmp", 16, 32), A("dmp", 16, 32), A("rcol"), OP.add)
+    ts(A("dmp", 0, 16), A("dmp", 16, 32), float(E - W), OP.add)
+    ts(A("dmh"), A("dmp"), -2048.0, OP.add)
     ts(A("kcol"), A("rcol"), -1.0, OP.mult, 15.0, OP.add)
-    for k in range(0, 2048, 512):
-        gcp(A("SF", k, k + 512), A("S", k, k + 512))
-    if "V" in FPLAN:
-        for k in range(0, 2048, 1024):
-            act(A("NS", k, k + 1024), A("S", k, k + 1024), AF.Copy, -1.0)
-    ts(A("ksr", 0, 16), A("im"), -1.0, OP.mult, 15.0, OP.add)
-    ts(A("akey", 0, 16), A("ps5", 80, 96), 16.0, OP.mult)
-    tt(A("akey", 0, 16), A("akey", 0, 16), A("ksr", 0, 16), OP.add)
-    ms(A("ksr", 15, 16), -32768.0)
-    ms(A("akey", 15, 16), -1.0e6)
-    rep("ksr", 128, 16, gcp)
-    rep("akey", 128, 16, gcp)
+    ts(A("ccol", 0, 1), A("rcol"), 15.0, OP.is_equal, -16384.0, OP.mult)
+    tt(A("ccol", 1, 2), A("ccol", 0, 1), A("kcol"), OP.add)
+    ts(A("dC"), A("idf"), A("ccol", 1, 2), OP.mult, 1024.0, OP.mult)
+    ts(A("ccol", 0, 1), A("ccol", 0, 1), 0.125, OP.mult, A("thf", 0, 1), OP.add)
+    ts(A("ccol", 0, 1), A("ccol", 0, 1), -1.0, OP.mult, -0.5, OP.add)
+    ts(A("ccol", 0, 1), A("ccol", 0, 1), 1000.0, OP.min)
+    ts(A("dA"), A("idf"), A("ccol", 0, 1), OP.mult)
+    ts(A("thf", 1, 2), A("thf", 1, 2), -1.0, OP.mult, -0.5, OP.add)
+    ts(A("dB", 0, 128), A("idf"), A("thf", 1, 2), OP.mult)
+    gcp(A("dB", 128, 256), A("dB", 0, 128))
     ms(A("rmax"), 4.0e7)
     ms(A("rmax", 0, 128, 16), -4.0e7)
     ms(A("rcnt"), 1.0)
     ms(A("rcnt", 0, 128, 16), 0.0)
-    ms(A("oneb"), 1.0)
-    gcp(A("bo16"), A("blk"))
-    ts(A("thf", 1, 2), A("thf", 1, 2), -1.0, OP.mult, -0.5, OP.add)
-    ts(A("nb16"), A("idf"), A("thf", 1, 2), OP.mult)
-
-    def quad(name, c0, c1):
-        return (T[name][:, c0:c1, :, :], (name, c0 * 256, c1 * 256, 1))
-
-    def line(name, rho):
-        return (T[name][:, :, rho, :], (name, 0, 2048, 1))
+    pe([(A("ps5", 32, 33), A("blk"), A("wtf"))])
+    conv(A("wb"), A("ps5", 32, 33), 192.0)
+    conv(A("pt", 0, W), A("lki"), 1.0 / 4096)
+    dma("G", T.pt[:, 0:W], T.xc[:], 4.0, [("pt", 0, W, 1)], [("pt", 0, W, 1)], acc=True)
+    conv(A("xw"), A("xcb"), 1.0, 192.0)
+    conv(A("zn"), A("zin0"), -1.0, 192.0)
 
     bank = [0]
+    helper = helper_of(core)
+    hrid, hpid, _se = topo.addr(helper)
+    if folds:
+        iot(A("c192"), [[0, FCUT]], 192, 0)
+        ms(A("c24"), 24.0)
 
-    def plan(s):
-        return [(q, 64 * k, 64) for k, q in enumerate(s)]
+    def sums(out, src, lo, w, step):
+        return [(out(k), src(k), w) for k in range(lo, lo + step)]
 
-    def absdiff(parts, win, off, raw, other, sub, dest, scale):
-        for (q, l0, n) in parts:
-            h, a, b = l0 // 128, (l0 % 128) * 16, (l0 % 128 + n) * 16
-            head[0] = HEAD * (1 - h)
-            o = A("%s%d" % (raw, h), a, b)
-            if q == "V":
-                gatop(o, win, A(off, l0, l0 + n), other(h, a, b), OP.subtract if sub else OP.add)
-                for x in range(a, b, 1024):
-                    act(quad("%s%d" % (dest, h), x // 256, min(x + 1024, b) // 256), A("%s%d" % (raw, h), x, min(x + 1024, b)), AF.Abs, scale)
-            else:
-                gat("S", o, win, A(off, l0, l0 + n))
-                for x in range(a, b, 512):
-                    y = min(x + 512, b)
-                    ps = A("ps%d" % bank[0], 0, y - x)
-                    bank[0] ^= 1
-                    pe(ps, [(ps, A("idb"), A("%s%d" % (raw, h), x, y)), (ps, A("nib" if sub else "idb"), other(h, x, y))])
-                    act(quad("%s%d" % (dest, h), x // 256, y // 256), ps, AF.Abs, scale)
-
-    def firsts(bc, own, eqn, lo_lo, small, extra=None):
-        bank7 = (None, ("ps7", 0, 512, 1))
-        O = lambda x, y: A("ps7", 256 + x, 256 + y)
-        E3 = lambda c, x, y: (T[eqn][:, c, x:y], (eqn, 256 * c + x, 256 * c + y, 1))
-        if extra:
-            pe(bank7, [(O(0, 256),) + extra], True, False)
-        else:
-            rest = []
+    def firsts(bc, own, eqn, lo, ps, dump):
+        O = lambda x, y: A(ps, 256 + x, 256 + y)
+        pe([(O(0, 256), A("oneb"), A("thr"))], True, False)
         for c0, c1 in ((0, 3), (3, 7), (7, 11), (11, 16)):
             calls, w, r, cost = [], [], [], 0.0
             for c in range(c0, c1):
-                o = E3(c, 0, 256 - 16 * c)
-                i = A(bc, 16 * c, 256)
-                s = A(own, c, c + 1)
+                o, i, s = A3(eqn, c, c + 1, 0, 256 - 16 * c), A(bc, 16 * c, 256), A(own, c, c + 1)
                 calls.append(lambda o=o, i=i, s=s: g.vector.tensor_scalar(o[0], i[0], s[0], None, OP.is_equal))
                 w.append(o[1])
                 r += [i[1], s[1]]
-                cost += vcost(256 - 16 * c, 0.5)
+                cost += vcost(i[2], o, i)
             add("V", calls, w, sorted(set(r)), cost)
-            terms = [(O(16 * c + 16, 256), A("bo4"), E3(c, 16, 256 - 16 * c)) for c in range(c0, min(c1, 15))]
-            if extra:
-                pe(bank7, terms, False, False)
-            else:
-                rest += terms
-        own_block = (O(0, 256), A("wd"), (T[eqn][:, :, 0:16], (eqn, 0, 4096, 1)))
-        if extra:
-            pe(bank7, [own_block], False, True)
-        else:
-            pe(bank7, [own_block] + rest)
-        tt(A("lo", lo_lo, lo_lo + 256), O(0, 256), A("thr"), OP.is_ge)
-        collect(A("ps5", small, small + 16), "lo", lo_lo)
-
-    def sel(k, own, t, dlt):
-        tt(A("dT", 16 * k, 16 * k + 16), t, dlt, OP.mult)
-        tt(A("oT", 16 * k, 16 * k + 16), A("dT", 16 * k, 16 * k + 16), own, OP.add)
-        cp(A("of", 16 * k, 16 * k + 16), A("oT", 16 * k, 16 * k + 16))
-
-    def scat(win, off, src, src2=None):
-        if src2 is None:
-            f = lambda: g.vector.tensor_copy(win[0].indirect(off[0]), src[0])
-        else:
-            f = lambda: g.vector.tensor_tensor(win[0].indirect(off[0]), src[0], src2[0], OP.add)
-        add("V", [f], [win[1]], [off[1], src[1]] + ([src2[1]] if src2 else []), 0.06 + 256 * SC * CY)
+            pe([(O(16 * c + 16, 256), A("bo4"), A3(eqn, c, c + 1, 16, 256 - 16 * c)) for c in range(c0, min(c1, 15))], False, False)
+        pe([(O(0, 256), A("wd"), A3(eqn, 0, 16, 0, 16))], False, True)
+        act(A("lo", lo, lo + 256), O(0, 256), AF.Sign)
+        out = A(ps, 0, 16)
+        pe([(out, A("id16"), dump)] + [(out, shifted("U", r), A("lo", lo + r, lo + 256, 16)) for r in range(16)])
+        return out
 
     def cues(t):
         head[0] = HC
-        z, cb, v16 = "zin%d" % t, "cmb%d" % (t & 1), "v16%d" % (t & 1)
-        u = A("ps6", 0, 16)
-        pe(u, [(u, A("SW", r * 128, r * 128 + 128), A(z, r, 256, 16)) for r in range(16)])
-        cp(A("ui", 0, 16), u)
+        z, cb, cf, zq = "zin%d" % t, "cb%d" % (t & 1), "cf%d" % (t & 1), "zq%d" % (t & 1)
+        u = A("ps6", 256, 272)
+        pe([(u, shifted("UW", r), A(z, r, 256, 16)) for r in range(16)])
+        if t:
+            conv(A("ui", 0, 16), u, -1.0, A("wb"))
+        else:
+            conv(A("ui", 0, 16), u)
         ts(A("ui", 16, 32), A("ui", 0, 16), 4095, OP.bitwise_and)
         tt(A("sq"), A("ui", 16, 32), A("ui", 16, 32), OP.mult)
         ts(A(cb, 0, 16), A("ui", 0, 16), 2047, OP.bitwise_and)
         ts(A(cb, 16, 32), A("sq"), 5, OP.logical_shift_right, 2047, OP.bitwise_and)
         ts(A(cb, 32, 48), A("sq"), 4, OP.logical_shift_right, 1023, OP.bitwise_and)
-        cp(A("cf"), A(cb))
-        spread("ps6", 0, A("cf", 0, 32))
-        act(A("xe"), A("ps6", 0, 256), AF.Copy, A("hkf", 0, 1))
-        act(A("xq"), A("ps6", 0, 256), AF.Copy, A("hkf", 1, 2))
-        tt(A("ei" if t == 0 else "e0"), A("ps6", 256, 512), A("xe"), OP.add)
-        spread("ps6", 0, A("cf", 32, 48))
-        tt(A("vi"), A("ps6", 0, 256), A("xq"), OP.add)
-        ts(A("vj"), A("vi"), 1023, OP.bitwise_and)
-        gcp(A(v16), A("vj"))
+        conv(A(cf), A(cb))
+        for m0 in range(0, 16, 4):
+            terms = []
+            for m in range(m0, m0 + 4):
+                o = A("ps6", 16 * m, 16 * m + 16)
+                terms += [(o, A("DP", m * 128, m * 128 + 128), A(cf, 0, 16)), (o, A("id16"), A(cf, 16, 32))]
+            pe(terms, each=2)
+        for x in range(0, 512, 128):
+            gcp(A3(zq, 0, 2, x, x + 128), A(z if t else "zn"))
+        if 0 < t < RO - 1:
+            conv(A("zpl"), A(z), -1.0, 192.0)
         zr = "zr%d" % (t & 1)
-        head[0] = 0.0
-        for k in range(0, 16, 4):
-            if ZPLAN[t][k // 4] == "S":
-                add("S", [lambda m=m: g.scalar.activation(T[zr][:, m::16], T[z][:], AF.Copy, 0.0, 1.0) for m in range(k, k + 4)],
-                    [(zr, m, 4096, 16) for m in range(k, k + 4)], [(z, 0, 256, 1)], 4 * (0.07 + 256 * CY))
-            elif ZPLAN[t][k // 4] == "G":
-                for m in range(k, k + 4):
-                    gcp(A(zr, m, 4096, 16), A(z))
-            else:
-                add("V", [lambda m=m: g.vector.tensor_copy(T[zr][:, m::16], T[z][:]) for m in range(k, k + 4)],
-                    [(zr, m, 4096, 16) for m in range(k, k + 4)], [(z, 0, 256, 1)], 4 * vcost(256, 0.5))
+        for m in range(16):
+            conv(A(zr, m, 4096, 16), A(z if t else "zn"), qs=ZPLAN[t])
 
     cues(0)
     H = ((0, 0, 128), (1, 128, 256))
     for t in range(RO):
-        z, zr, cb = "zin%d" % t, "zr%d" % (t & 1), "cmb%d" % (t & 1)
-        for (h, a, b) in H:
-            if t:
-                ts(A("ei", a, b), A("e0", a, b), A("acol"), OP.add)
-            ts(A("ej", a, b), A("ei", a, b), 2047, OP.bitwise_and)
-            cp(A("e16", a, b), A("ej", a, b))
+        z, zr, cb, cf, zq = "zin%d" % t if t else "zn", "zr%d" % (t & 1), "cb%d" % (t & 1), "cf%d" % (t & 1), "zq%d" % (t & 1)
         if t:
-            ts(A("bs"), A(cb, 16, 32), A("acol"), OP.add)
-        base, boff = ("bs", 0) if t else (cb, 16)
-        absdiff(plan(GPLAN[t]), A("gist", 0, E), "e16", "gd", lambda h, x, y: A(zr, h * 2048 + x, h * 2048 + y), True, "aa", 32768.0)
+            conv(A3("ei", 0, 16, 0, 16), A("ps6", 0, 256), 1.0, A("acol"))
+            conv(A("bs"), A(cb, 16, 32), 1.0, A("acol"))
+        else:
+            conv(A3("ei", 0, 16, 0, 16), A("ps6", 0, 256))
         for (h, a, b) in H:
-            head[0] = HEAD * (1 - h)
-            c0, c1 = 8 * h, 8 * h + 8
-            k = A("ps%d" % (2 + h), 0, 128)
-            pe(k, [(k, A("R", 0, 128), A("prow")), (k, A("r0k"), A("imr")), (k, A("r0k"), A("c8k"))]
-               + [(k, A("S", r * 128, r * 128 + 128), line("aa%d" % h, r)) for r in range(16)])
-            scan(A("km%d" % h), A("rmin"), k, 4.0e7, OP.max, OP.min)
-            i0, i1, i2, i3 = [A("ki", 32 * h + 8 * x, 32 * h + 8 * x + 8) for x in range(4)]
-            ts(i1, A("km%d" % h, 15, 128, 16), 2047, OP.bitwise_and)
-            tt(i2, i1, A(cb, c0, c1), OP.mult)
+            ts(A("ej", a, b), A3("ei", 0, 16, 8 * h, 8 * h + 8), 2047, OP.bitwise_and)
+            conv(A("e16", a, b), A("ej", a, b))
+        base, boff = ("bs", 0) if t else (cb, 16)
+        for (h, a, b) in H:
+            c0, c1, ps, X = 8 * h, 8 * h + 8, "ps%d" % (2 + h), "X%d" % h
+            gd, ga, px, yd, ya, fa = ["%s%d" % (n, h) for n in ("gd", "ga", "px", "yd", "ya", "fa")]
+            key = lambda k: A(ps, k, 128, 16)
+            pe([(A(ps, 0, 128), A("z16"), A("one16", 0, 128))], True, False)
+            for j in range(4):
+                x, y, q = 512 * j, 512 * j + 512, GPLAN[t][4 * h + j]
+                lst, zz = A("e16", a + 32 * j, a + 32 * j + 32), A3(zq, h, h + 1, 0, 512)
+                if q == "S":
+                    gat("S", A(gd, x, y), A("gist", 0, E), lst)
+                    d = A("ps%d" % bank[0])
+                    bank[0] ^= 1
+                    pe([(d, A("idb"), A(gd, x, y))] + [(A(d[1][0], v, v + 128), A("idb"), A(z, a, b)) for v in range(0, 512, 128)])
+                    act(A(ga, x, y), d, AF.Abs, 1.0, -192.0)
+                else:
+                    gatop(A(gd, x, y), A("gist", 0, E), lst, zz, OP.add)
+                    if q == "A":
+                        act(A(ga, x, y), A(gd, x, y), AF.Abs, 1.0, -192.0)
+                    else:
+                        ts(A(ga, x, y), A(gd, x, y), 192.0, OP.min, -96.0, OP.add)
+                        pe(sums(key, lambda m: A(gd, 128 * m, 128 * m + 128), 4 * j, A("cw", 32, 40), 4), False, False)
+                pe(sums(key, lambda m: A(ga, 128 * m, 128 * m + 128), 4 * j, A("cw", 40, 48) if q == "V" else A("cw", 32, 40), 4), False, False)
+            pe([(A(ps, 0, 128), A("c2k"), A("dM")), (A(ps, 0, 128), A("one16", 0, 128), A("dP"))], False, True)
+            km = "km%d" % h
+            scan(A(km, 0, 128), A("rmin"), A(ps, 0, 128), 4.0e7, OP.max, OP.min)
+            ts(A(km, 128, 136), A(km, 15, 128, 16), 2047, OP.bitwise_and)
+            gatop(A("Xh", a, b), A(km), A("xl", 8, 16), A("msk", 0, 128), OP.mult)
+            pe([(A(ps, 0, 8), A("Xh", a, b), A("b16"))])
+            i2, i3 = [A("ki", 32 * h + 8 * x, 32 * h + 8 * x + 8) for x in range(2)]
+            tt(i2, A(ps, 0, 8), A(cb, c0, c1), OP.mult)
             tt(i3, i2, A(base, boff + c0, boff + c1), OP.add)
             ts(A("el", c0, c1), i3, 2047, OP.bitwise_and)
-            cp(A("elu", c0, c1), A("el", c0, c1))
-            gat("V", A("ju", a, b), A("nm", 0, E) if t else A("ixi"), A("elu", c0, c1))
-            for q in (0, 64):
-                gat("V", A("lg%d" % h, 16 * q, 16 * q + 1024), A("lkt", 0, W) if t else A("lki"), A("ju", a + q, a + q + 64))
-                gat("S", A("nx%d" % h, 16 * q, 16 * q + 1024), A("xcb"), A("ju", a + q, a + q + 64), -1.0)
-                n = A("ps%d" % (2 + h), 128 + q, 192 + q)
-                pe(n, [(n, A("D", r * 128, r * 128 + 128), A("lg%d" % h, 16 * q + r, 16 * q + 1024, 16)) for r in range(16)])
-                cp(A("nu", a + q, a + q + 64), n)
+            conv(A("elu", c0, c1), A("el", c0, c1))
+            gat("VS", A("ju", a, b), A("ixi", 0, E), A("elu", c0, c1))
+            for q in range(0, 128, PCUT):
+                gat("VS", A(px, 16 * q, 16 * (q + PCUT)), A("pt", 0, W), A("ju", a + q, a + q + PCUT))
             gcp(A("jh", a, b), A("ju", a, b))
+            nT = A(ps, 128, 256)
+            pe([(A(ps, 128 + k, 256, 16), A(px, k, 2048, 16), A("idf", k, 128, 16)) for k in range(16)], each=True)
+            conv(A("qx", a, b), nT, 1.0, 128.0)
+            conv(A("fr", a, b), nT)
+            pe([(A(ps, 0, 128), A("fr", a, b), A("i4k")), (A(ps, 0, 128), A("qx", a, b), A("n4k"))])
+            conv(A("nu", a, b), A(ps, 0, 128), 1.0, 128.0 * 4096)
             gcp(A("nh", a, b), A("nu", a, b))
+            for x in range(0, 2048, FCUT):
+                addto(A(zr, 2048 * h + x, 2048 * h + x + FCUT), A(px, x, x + FCUT), 2.0 + 3.0 * FCUT / 2048)
+        for (h, a, b) in H:
             head[0] = HZ
-            scan(A("zs%d" % h), A("rz"), A("nx%d" % h, 0, 2048), 100.0, OP.max, OP.min)
-            zp = A("ps6", a, b)
-            pe(zp, [(zp, A("idb"), A(z, a, b)), (zp, A("nib"), A("zs%d" % h, 15, 2048, 16))])
-            act(A("ze", a, b), zp, AF.Copy, 0.5, 127.75)
-            act(A("zo%d" % t, a, b), A("ze", a, b), AF.Copy, 1.0, -128.0)
+            diff = ZMAX[t][h] == "d"
+            for x in (0, 1024):
+                src = A(zr, 2048 * h + x, 2048 * h + x + 1024) if diff else A("px%d" % h, x, x + 1024)
+                scan(A("zs%d" % h, x, x + 1024), A("rz"), src, 0.0, OP.min, OP.max)
+            zp = A("ps6", 256 + a, 256 + b)
+            pe([(zp, A("n2b" if diff else "nib"), A(z, a, b)), (zp, A("id16"), A("zs%d" % h, 15, 2048, 16))])
+            if t < RO - 1:
+                conv(A("zo%d" % t, a, b), zp, -0.5, 96.25)
+            else:
+                conv(A("ze", a, b), zp, -0.5, 96.25)
+                conv(A("zo%d" % t, a, b), A("ze", a, b), -1.0, 192.0)
         dst = T.cores[(rank + 1) % len(T.cores)] if t < RO - 1 else T.cores[(rank - t) % len(T.cores)]
         land = "zin%d" % (t + 1) if t < RO - 1 else "zfin"
         eng = topo.engines(core, dst)[:NENG]
@@ -445,90 +476,116 @@ def rank_program(g, core, T, topo):
         mask = sum(1 << e for e in eng)
         add("G", [lambda land=land, rid=rid, pid=pid, mask=mask, t=t: g.remote_dma(
             T[land][:], T["zo%d" % t][:], T.sem["arr%d" % (t + 1)], T.sem.snd, pid, rid, mask)],
-            [(land, 0, 256, 1)], [("zo%d" % t, 0, 256, 1)], 1.0, 3.0, "r", "arr%d" % (t + 1), len(eng))
+            [(land, 0, 256, 1)], [("zo%d" % t, 0, 256, 1)], 1.0, 3.0 * DL, "r", "arr%d" % (t + 1), len(eng))
         head[0] = 0.0
-        for (h, a, b) in H:
-            x = A(zr, h * 2048, h * 2048 + 2048)
-            dma("G", x[0], T["nx%d" % h][:, 0:2048], 5.0, [x[1]], [x[1], ("nx%d" % h, 0, 2048, 1)], acc=True)
         gcp(A("elh"), A("el"))
         gcp(A("elf"), A("el"))
-        tt(A("dE", 0, 16), A("lane", 0, 16), A("elf"), OP.subtract)
-        spread("ps7", 0, A("elh"))
-        cp(A("eB"), A("ps7", 0, 256))
-        firsts("eB", "elf", "eq", 0, 32)
-        ts(A("loL"), A("ps5", 32, 48), 0.0625, OP.mult)
-        sel(0, A("elf"), A("loL", 0, 16), A("dE", 0, 16))
-        for (h, a, b) in H:
-            c0, c1 = 8 * h, 8 * h + 8
-            absdiff([p for p in plan(YPLAN[t]) if p[1] // 128 == h], A("xcb"), "nu", "yb", lambda h, x, y: A("nx%d" % h, x + 1, y + 1), False, "ya", 16.0)
-            k = A("ps%d" % (2 + h), 256, 384)
-            pe(k, [(k, A("R", 0, 128), A("ksr"))] + [(k, A("S", r * 128, r * 128 + 128), line("ya%d" % h, r)) for r in range(16)])
-            tt(A("cm%d" % h), k, A("akey"), OP.is_le)
-            scan(A("cn", a, b), A("rcnt"), A("cm%d" % h), 0.0, OP.mult, OP.add)
-            scan(A("kx", a, b), A("rmax"), k, -4.0e7, OP.min, OP.max)
-        ts(A("rec"), A("cn", 15, 256, 16), float(NEED), OP.is_ge)
-        cp(A("recb"), A("rec"))
-        ts(A("kj", 16, 32), A("kx", 15, 256, 16), 15, OP.bitwise_and)
-        head[0] = 0.0
+        pe(spread("ps7", 0, A("elh")), each=True)
+        conv(A("eB"), A("ps7", 0, 256))
+        tt(A("of0"), firsts("eB", "elf", "eq", 0, "ps7", A("dmh", 0, 16)), A("elf"), OP.max)
+        gcp(A("of", 0, 16), A("of0"))
+        pe(spread("ps5", 0, A(cf, 0, 16)), each=True)
+        conv(A("xq"), A("ps5", 0, 256), A("hkf", 1, 2))
+        pe([(A("ps5", 256, 512), A("idf"), A("xq"))] + spread("ps5", 256, A(cf, 32, 48)))
+        conv(A("vi"), A("ps5", 256, 512))
+        ts(A("vj"), A("vi"), 1023, OP.bitwise_and)
+        gcp(A("v16"), A("vj"))
         if t < RO - 1:
             cues(t + 1)
-            cnt = A("ps3", 384, 400)
-            pe(cnt, [(cnt, A("oneb"), A("recb"))])
-            total_of(A("acol"), cnt)
-            ts(A("nrec"), A("rec"), -1.0, OP.mult, 1.0, OP.add)
-            tt(A("gT"), A("loL", 0, 16), A("nrec"), OP.max)
-            sel(1, A("elf"), A("gT"), A("dE", 0, 16))
-            scat(A("gist"), A("of", 16, 32), A(z))
-        F = A("ps4", 0, 256)
-        jp = A("ps4", 256, 512)
-        pe(jp, [(jp, A("id16"), A("jh"))])
-        pe((None, ("ps4", 0, 512, 1)), [(F, A("nb16"), A("one16", 0, 256))], True, False)
         for (h, a, b) in H:
-            fh = A("ps4", a, b)
-            terms = [(fh, A("S", r * 128, r * 128 + 128), A("fa%d" % h, r, 2048, 16)) for r in range(16)]
-            if FPLAN[h] == "S":
-                for x in (0, 1024):
-                    act(A("fa%d" % h, x, x + 1024), A(zr, h * 2048 + x, h * 2048 + x + 1024), AF.Abs)
+            c0, c1, ps, X, kc = 8 * h, 8 * h + 8, "ps%d" % (2 + h), "X%d" % h, "kc%d" % h
+            px, yd, ya = "px%d" % h, "yd%d" % h, "ya%d" % h
+            for q in (0, 64):
+                x, y, lst = 16 * q, 16 * q + 1024, A("nu", a + q, a + q + 64)
+                if YPLAN[t][2 * h + q // 64] == "V":
+                    gatop(A(yd, x, y), A("xw"), lst, A(px, x + 1, y + 1), OP.subtract)
+                else:
+                    gat("S", A(yd, x, y), A("xcb"), lst, -1.0, 192.0)
+                    addto(A(yd, x, y), A(px, x + 1, y + 1), 3.5)
+                if YABS[t][h] == "S":
+                    act(A(ya, x, y), A(yd, x, y), AF.Abs, 1.0, -192.0)
+                else:
+                    ts(A(ya, x, y), A(yd, x, y), 192.0, OP.min, -96.0, OP.add)
+            key = lambda k: A(ps, 256 + k, 512, 16)
+            pe([(A(ps, 256, 512), A("z16"), A("one16", 0, 256)), (A(ps, 384, 512), A("one16", 0, 128), A("dA"))], True, False)
+            if YABS[t][h] == "S":
+                pe(sums(key, lambda k: A(ya, k, 2048, 16), 0, A("cw", 0, 16), 16), False, False)
             else:
-                for x in (0, 1024):
-                    ts(A("fa%d" % h, x, x + 1024), A(zr, h * 2048 + x, h * 2048 + x + 1024), 0.0, OP.max, 2.0, OP.mult)
-                terms += [(fh, A("NS", r * 128, r * 128 + 128), A(zr, h * 2048 + r, h * 2048 + 2048, 16)) for r in range(16)]
-            pe(fh, terms, False, False)
-        ts(A("rec"), A("rec"), 16.0, OP.mult)
-        tt(A("jr"), A("kj", 16, 32), A("rec"), OP.add)
-        spread("ps5", 256, A("jr"))
-        act(A("rB"), A("ps5", 256, 512), AF.Relu, 1.0, -15.0)
-        ts(A("oh"), A("ps5", 256, 512), A("kcol"), OP.is_equal)
-        tt(A("pj"), A("ps4", 256, 512), A("oh"), OP.mult)
-        pe(F, [(F, A("k1b"), A("rB"))], False, True)
-        dp, ib = A("ps6", 0, 256), A("ps6", 256, 512)
-        pe(ib, [(ib, A("bo16"), A("pj")), (ib, A("k1b"), A("rB"))])
-        cp(A("IB"), ib)
-        pe(dp, [(dp, A("sh16"), A("jh")), (dp, A("ni16"), A("nh"))])
-        tt(A("dl"), dp, A("oh"), OP.mult)
-        v = A("v16%d" % (t & 1))
-        hp, hm = A("ps6", 0, 256), A("ps6", 256, 512)
-        pe(hp, [(hp, A("hi16"), v), (hp, A("hi16"), A("jh"))])
-        act(A("ja"), hp, AF.Copy)
-        pe(hm, [(hm, A("hi16"), v), (hm, A("nh16"), A("jh"))])
-        act(A("mk"), F, AF.Sign)
-        tt(A("pn"), hm, A("mk"), OP.mult)
-        if t == 0:
+                pe(sums(key, lambda k: A(yd, k, 2048, 16), 0, A("cw", 0, 16), 16), False, False)
+                pe(sums(key, lambda k: A(ya, k, 2048, 16), 0, A("cw", 16, 32), 16), False, False)
+            pe([(A(ps, 256, 384), A("oneb"), A("dC")), (A(ps, 256, 384), A("jh", a, b), A("id16"))], False, True)
+            act(A("sg", a, b), A(ps, 384, 512), AF.Sign)
+            scan(A("cn", a, b), A("rcnt"), A("sg", a, b), 0.0, OP.mult, OP.add)
+            ts(A(kc, 128, 136), A("cn", a + 15, b, 16), -6.0, OP.is_le)
+            scan(A(kc, 0, 128), A("rmax"), A(ps, 256, 384), -4.0e7, OP.min, OP.max)
+            gatop(A(X), A(kc), A("xl"), A("msk", 2 * a, 2 * b), OP.mult)
+            pe([(A(ps, 0, 8), A(X, 0, 128), blk8), (A(ps, 8, 16), A(X, 128, 256), blk8)], each=True)
+            if t < RO - 1:
+                pe([(A(ps, 16, 24), A("idf"), A("dmp", c0, c1)), (A(ps, 16, 24), A(X, 128, 256), A("bm4"))])
+                tt(A("oT", c0, c1), A(ps, 16, 24), A("of0", c0, c1), OP.max)
+                conv(A("of", 16 + c0, 16 + c1), A("oT", c0, c1))
+                scat(A("gist"), A("of", 16 + c0, 16 + c1), A("zpl" if t else "zin0", a, b))
+            conv(A3("ksl", h, h + 1, 0, 16), A(ps, 0, 16))
+            gat("VS", A("rT", a, b), A(kc), A("xl", 8, 16))
+        if t < RO - 1:
+            cnt = A("ps6", 272, 280)
+            pe([(cnt, A("one"), A("kc0", 128, 136)), (cnt, A("one"), A("kc1", 128, 136))])
+            act(A("junk", 0, 8), cnt, AF.Copy, total=A("acol"))
+        pe([(A("ps4"), A("z16"), A("one16")), (A("ps4", 0, 256), A("one16", 0, 128), A("dB"))], True, False)
+        for (h, a, b) in H:
+            fa, far = "fa%d" % h, lambda k: A("ps4", a + k, b, 16)
+            pe([(A("ps4", 256 + a, 256 + b), A("v16", a, b), A("hi16")), (A("ps4", 256 + a, 256 + b), A("jh", a, b), A("nh16"))], False, False)
+            for x in range(0, 2048, FCUT):
+                d = A(zr, 2048 * h + x, 2048 * h + x + FCUT)
+                if FABS[t][h] == "S":
+                    act(A(fa, x, x + FCUT), d, AF.Abs, 1.0, -192.0)
+                elif FABS[t][h] == "V":
+                    ts(A(fa, x, x + FCUT), d, 192.0, OP.min, -96.0, OP.add)
+                else:
+                    k, y = folds.index((t, 2048 * h + x)), 2048 * h + x
+                    tr = RemoteDMATransfer(dst_ids=[DstId(rid=hrid, pnc=hpid)], dma_engine_mask=bits(core, helper, 16 - HENG, 16), remote_sem=T.sem["out%d" % k],
+                                           srcs=[d[0], T.c192[:]], dsts=[T.zr0[:, y:y + FCUT]], alu_op=3)
+                    add("G", [lambda tr=tr: g.remote_dma_fused([tr], local_sem=T.sem.snd)], [A(fa, x, x + FCUT)[1], ("fold", 0, 1, 1)], [d[1], A("c192")[1]],
+                        1.0, HLAT, "r", "ret%d" % k, RENG)
+                    ops[-1]["sent"], ops[-1]["deps"] = HENG, {i: (w if ops[i]["w"][:1] == [A(fa, x, x + FCUT)[1]] or ops[i]["w"][1:] != [("fold", 0, 1, 1)] else False)
+                                                              for i, w in ops[-1]["deps"].items()}
+            if FABS[t][h] == "H":
+                pe([(A("ps4", a, b), A("oneb"), A("c24"))], False, False)
+            if FABS[t][h] == "S":
+                pe(sums(far, lambda k: A(fa, k, 2048, 16), 0, A("cw", 8, 16), 16), False, False)
+            else:
+                pe(sums(far, lambda k: A(zr, 2048 * h + k, 2048 * h + 2048, 16), 0, A("cw", 8, 16), 16), False, False)
+                pe(sums(far, lambda k: A(fa, k, 2048, 16), 0, A("cw", 24, 32), 16), False, False)
+        pe([(A("ps4", a, b), A("k2b"), A("rT", a, b)) for (h, a, b) in H], False, True)
+        act(A("mk"), A("ps4", 0, 256), AF.Sign)
+        tt(A("pn"), A("ps4", 256, 512), A("mk"), OP.mult)
+        nn = A("ps4", 0, 256)
+        pe([(nn, A("hi16"), A("v16")), (nn, A("hi16"), A("jh"))] + [(A("ps4", a, b), A("pn", a, b), A("id16")) for (h, a, b) in H])
+        conv(A("nn"), nn)
+        if t == RO - 1:
             for x in range(0, E, 512):
                 gcp(A("nm", x, x + 512), A("ixi", x, x + 512))
-            for x in range(0, W, 512):
-                gcp(A("lkt", x, x + 512), A("lki", x, x + 512))
-        scat(A("nm"), A("of", 0, 16), A("pn"), A("ja"))
-        collect(A("ps5", 48, 64), "pj", 0)
-        cp(A("ILu"), A("ps5", 48, 64))
-        ts(A("dT", 48, 64), A("rec"), 128.0, OP.mult)
-        tt(A("IL"), A("ps5", 48, 64), A("dT", 48, 64), OP.add)
-        gatop(A("nl"), A("lkt", 0, W), A("ILu"), A("dl"), OP.add)
-        tt(A("dE", 16, 32), A("lane", 16, 32), A("IL"), OP.subtract)
-        ts(A("dE", 16, 32), A("dE", 16, 32), 0.0625, OP.mult)
-        firsts("IB", "IL", "eq2", 256, 96, (A("k1b"), A("rB")))
-        sel(2, A("IL"), A("ps5", 96, 112), A("dE", 16, 32))
-        scat(A("lkt"), A("of", 32, 48), A("nl"))
+        scat(A("ixi" if t < RO - 1 else "nm"), A("of", 0, 16), A("nn"))
+        ts(A("ij", 0, 16), A3("ksl", 0, 2, 0, 8), 1023, OP.bitwise_and)
+        ts(A("ij", 16, 32), A3("ksl", 0, 2, 0, 8), 10, OP.logical_shift_right, 15, OP.bitwise_and)
+        conv(A("sl"), A("ij"))
+        gcp(A("ILu"), A("ij", 0, 16))
+        tt(A("own"), A("ij", 0, 16), A3("ksl", 0, 2, 8, 16), OP.max)
+        pe(spread("ps7", 0, A("sl")), each=True)
+        conv(A("IB"), A("ps7", 0, 256))
+        ts(A("oh"), A("ps7", 256, 512), A("kcol"), OP.is_equal, 1.0 / 4096 if t < RO - 1 else 1.0, OP.mult)
+        dp = A("ps5", 256, 512)
+        pe([(dp, A("sh16"), A("jh")), (dp, A("ni16"), A("nh"))])
+        tt(A("dl"), dp, A("oh"), OP.mult)
+        tab = "pt" if t < RO - 1 else "lkt"
+        gat("VS", A("nl"), A(tab, 0, W), A("ILu"))
+        tt(A("oT", 16, 32), firsts("IB", "own", "eq2", 256, "ps5" if t < RO - 1 else "ps0", A("dmh", 16, 32)), A("own"), OP.max)
+        conv(A("of", 32, 48), A("oT", 16, 32))
+        scat(A(tab), A("of", 32, 48), A("nl"), A("dl"))
+        if t == RO - 2:
+            for x, ps in ((0, "ps5"), (512, "ps7")):
+                pe([(A(ps), A("i4k"), A("pt", x, x + 512)), (A(ps), A("n4k"), A("xcb", x, x + 512))])
+                conv(A("lkt", x, x + 512), A(ps))
     dma("Y", T.yz[:], T.zfin[:], 2.5, [], [("zfin", 0, 256, 1)])
     dma("Y", T.yi[:], T.nm[:, 0:E], 5.0, [], [("nm", 0, E, 1)])
     dma("Y", T.yl[:], T.lkt[:, 0:W], 3.5, [], [("lkt", 0, W, 1)])
@@ -541,50 +598,85 @@ def rank_program(g, core, T, topo):
     way = [0.0] * n
     for i in range(n - 1, -1, -1):
         o = ops[i]
-        way[i] = o["cost"] + o["lat"] + max([way[j] + WAKE for j in users[i]] + [0.0])
-    queue, cost = [o["q"] for o in ops], [o["cost"] for o in ops]
-    tail = [o["cost"] + o["lat"] for o in ops]
-    then = [[(j, tail[i] + WAKE if ops[j]["deps"][i] else 1e-6) for j in users[i]] for i in range(n)]
-    npre = [len(o["deps"]) for o in ops]
+        way[i] = o["cost"] + max([way[j] + (o["lat"] + WAKE if ops[j]["deps"][i] else 0.0) for j in users[i]] + [o["lat"]])
+    choice = [[(q, o["alts"][q][1]) for q in o["q"]] if "alts" in o else [(o["q"], o["cost"])] for o in ops]
+    lat = [o["lat"] for o in ops]
+    ahead = ([[(j, lat[i] + WAKE if ops[j]["deps"][i] else None) for j in users[i]] for i in range(n)], [len(o["deps"]) for o in ops], [0.0] * n, lat)
+    back = ([[(d, lat[d] + WAKE if w else None) for d, w in o["deps"].items()] for o in ops], [len(u) for u in users], lat, [0.0] * n)
 
-    def place(key):
-        left, avail, start, order = list(npre), [0.0] * n, [0.0] * n, []
-        free, ready = {q: 0.0 for q in queues}, {q: [] for q in queues}
-        for i in range(n):
-            if left[i] == 0:
-                ready[queue[i]].append(i)
-        while len(order) < n:
-            m, q = 1e18, None
-            for x in ready:
-                if ready[x]:
-                    y = max(free[x], min(avail[i] for i in ready[x]))
-                    if y < m:
-                        m, q = y, x
-            i = max((j for j in ready[q] if avail[j] <= m + LOOK), key=lambda j: key[j])
-            s = start[i] = max(avail[i], free[q])
-            free[q] = s + cost[i]
-            ready[q].remove(i)
-            order.append(i)
-            for j, w in then[i]:
+    def place(key, lean, way):
+        then, left, avail, after = way[0], list(way[1]), list(way[2]), way[3]
+        start, on, span, end = [0.0] * n, [""] * n, 0.0, [0.0] * n
+        begins, ends = {q: [] for q in queues}, {q: [] for q in queues}
+        ready = sorted((key[i], i) for i in range(n) if left[i] == 0)
+        while ready:
+            i = ready.pop()[1]
+            top = None
+            for q, c in choice[i]:
+                b, e, s = begins[q], ends[q], avail[i]
+                k = len(e)
+                if k and e[-1] > s:
+                    lo, hi = 0, k
+                    while lo < hi:
+                        mid = (lo + hi) >> 1
+                        if e[mid] > s:
+                            hi = mid
+                        else:
+                            lo = mid + 1
+                    while lo < k and b[lo] < s + c:
+                        s = e[lo]
+                        lo += 1
+                    k = lo
+                v = s + c + (lean[i] if q == "V" else 0.0)
+                if top is None or v < top[0]:
+                    top = (v, q, s, c, k)
+            _v, q, s, c, k = top
+            begins[q].insert(k, s)
+            ends[q].insert(k, s + c)
+            f = s + c
+            start[i], on[i], end[i] = s, q, f
+            if f + after[i] > span:
+                span = f + after[i]
+            for j, wait in then[i]:
+                w = s + 1e-6 if wait is None else f + wait
+                if w > avail[j]:
+                    avail[j] = w
                 left[j] -= 1
-                if s + w > avail[j]:
-                    avail[j] = s + w
                 if left[j] == 0:
-                    ready[queue[j]].append(j)
-        return start, order, max(start[i] + tail[i] for i in range(n))
+                    x, lo, hi = (key[j], j), 0, len(ready)
+                    while lo < hi:
+                        mid = (lo + hi) >> 1
+                        if ready[mid] < x:
+                            lo = mid + 1
+                        else:
+                            hi = mid
+                    ready.insert(lo, x)
+        return start, on, span, end
 
     if n not in ORDER:
-        key = [way[i] + ops[i]["head"] for i in range(n)]
-        best = place(key)
-        rng = np.random.RandomState(5)
+        key, lean = np.array([way[i] + ops[i]["head"] for i in range(n)]), np.full(n, LEAN)
+        best = top = place(key.tolist(), lean.tolist(), ahead)
+        rng = np.random.RandomState(SEED)
         for k in range(TRIES):
-            nk = [float(x) for x in np.array(key) + (rng.rand(n) < (0.02, 0.1, 0.4)[k % 3]) * rng.randn(n) * (0.5, 2.0, 6.0)[(k // 3) % 3]]
-            new = place(nk)
-            if new[2] <= best[2]:
-                key, best = nk, new
-        ORDER[n] = best
-    start, order, _span = ORDER[n]
-    fin = [start[i] + tail[i] for i in range(n)]
+            near = (np.abs(np.array(best[0]) - rng.rand() * best[2]) < 5.0) * (rng.rand(n) < (0.05, 0.2, 0.5)[k % 3])
+            nl = lean + near * (rng.rand(n) < 0.3) * rng.randn(n)
+            if k % 4 == 3:
+                nk = np.array(place((np.array(best[3]) + near * rng.randn(n)).tolist(), nl.tolist(), back)[3])
+            else:
+                nk = key + near * rng.randn(n) * (0.5, 1.5, 4.0)[(k // 4) % 3]
+            new = place(nk.tolist(), nl.tolist(), ahead)
+            if new[2] <= best[2] + SLACK * (1.0 - k / TRIES) * rng.rand():
+                key, lean, best = nk, nl, new
+                if best[2] < top[2]:
+                    top = best
+        ORDER[n] = top
+    start, on, _span, _end = ORDER[n]
+    order = sorted(range(n), key=lambda i: (start[i], i))
+    for o in ops:
+        if "alts" in o:
+            o["q"] = on[o["i"]]
+            o["calls"], o["cost"] = [o["alts"][o["q"]][0]], o["alts"][o["q"]][1]
+    EST.append((ops, (start, order, _span), way))
 
     know = {q: {} for q in queues}
     clock = [None] * n
@@ -620,7 +712,7 @@ def rank_program(g, core, T, topo):
         else:
             clock[i] = (o["sem"], o["val"], {})
             total[o["sem"]] = o["val"]
-            total["snd"] = total.get("snd", 0) + o["val"]
+            total["snd"] = total.get("snd", 0) + o.get("sent", o["val"])
     for sem in sorted(total):
         if know["G"].get(sem, 0) < total[sem]:
             g.wait_ge(T.sem[sem], total[sem])

@@ -4,17 +4,22 @@ from concourse.mybir import AluOpType as OP, ActivationFunctionType as AF
 
 W, E, B, RO = 1024, 2048, 256, 3
 NENG = 8
-GPLAN = ("VSVSSVSV", "VSVSSVSV", "VSVSSVSV")
+GPLAN = ("VSVSVSVS", "VSVSSVSS", "VSVSSVSS")
+LSPLIT = (False, False, False)
+FAST0 = FAST = True
+SPLIT = False
+YCUT = (((0, 128),), ((0, 64), (64, 96), (96, 128)))
 PCUT = 32
 YPLAN = ("VVVV", "VVVV", "VVVV")
 YABS = ("SS", "SS", "SS")
 FABS = ("SS", "SS", "SS")
-ZMAX = ("pp", "pp", "dd")
+ZMAX = ("pppp", "pppp", "dddd")
 ZPLAN = ("VG", "G", "G")
 HENG, RENG, HLAT = 8, 16, 12.0
 FCUT = 1024
-TRIES, ORDER = 11000, {}
-HZ, HC, LEAN, SLACK, SEED = 0.0, 0.0, 1.5, 0.3, 5
+TRIES, ORDER = 600, {}
+MOVES, HEAT = 150000, 0.1
+HZ, HC, LEAN, SLACK, SEED = 0.0, 0.0, 1.5, 0.5, 4
 F32, BF, F16, I32, U16 = "float32", "bfloat16", "float16", "int32", "uint16"
 
 SCRATCH = {
@@ -27,6 +32,7 @@ SCRATCH = {
     "R": ("sbuf", [128, 2048], F16), "DP": ("sbuf", [128, 2048], F16), "rz": ("sbuf", [128, 1024], BF),
     "zr0": ("sbuf", [128, 4096], BF), "zr1": ("sbuf", [128, 4096], BF), "zq0": ("sbuf", [128, 2, 512], BF), "zq1": ("sbuf", [128, 2, 512], BF),
     "eq": ("sbuf", [128, 16, 256], BF), "eq2": ("sbuf", [128, 16, 256], BF), "ei": ("sbuf", [128, 16, 16], I32),
+    "cb0": ("sbuf", [128, 3, 16], I32), "cb1": ("sbuf", [128, 3, 16], I32), "cf0": ("sbuf", [128, 3, 16], F16), "cf1": ("sbuf", [128, 3, 16], F16),
     "ksl": ("sbuf", [128, 2, 32], I32), "c192": ("sbuf", [128, FCUT], BF),
 }
 for _k in (0, 1):
@@ -34,15 +40,15 @@ for _k in (0, 1):
                        ("km", I32, 136), ("kc", F32, 136)):
         SCRATCH["%s%d" % (_n, _k)] = ("sbuf", [128, _w], _d)
 _SMALL = {
-    F32: (("wtf", 1), ("hkf", 2), ("thf", 2), ("one", 128), ("idf", 128), ("blk", 128), ("i4k", 128), ("bm4", 8), ("pd", 16), ("pB", 16), ("pw", 16), ("half", 16), ("zero", 16),
+    F32: (("wtf", 1), ("hkf", 2), ("thf", 2), ("one", 128), ("idf", 128), ("blk", 128), ("dCA", 256), ("prow", 256), ("e0", 256), ("bm4", 8), ("pd", 16), ("pB", 16), ("pw", 16), ("half", 16), ("zero", 16),
           ("tw", 16), ("wcol", 1), ("rcol", 1), ("kcol", 1), ("ccol", 2), ("wb", 1), ("dmp", 32), ("lcol", 2), ("msk", 512), ("rmin", 128), ("rmax", 128), ("xq", 256),
-          ("X0", 256), ("X1", 256), ("elf", 16), ("of0", 16), ("oT", 32), ("own", 16), ("acol", 1), ("junk", 16), ("dl", 256), ("nl", 256), ("nn", 256), ("fr", 256)),
+          ("X0", 256), ("X1", 256), ("elf", 16), ("of0", 16), ("oT", 32), ("own", 16), ("acol", 2), ("hlf", 128), ("junk", 16), ("dl", 256), ("nl", 256), ("nn", 256), ("fr", 256)),
     F16: (("id16", 128), ("ni16", 128), ("hi16", 128), ("nh16", 128), ("sh16", 128), ("one16", 512), ("z16", 128), ("dP", 128), ("dA", 128), ("dB", 256), ("dmh", 32),
-          ("cf0", 48), ("cf1", 48), ("v16", 256), ("elh", 16), ("jh", 256), ("nh", 256), ("sl", 32), ("eB", 256), ("IB", 256), ("oh", 256), ("pn", 256), ("Xh", 256), ("b16", 8)),
+          ("v16", 256), ("elh", 16), ("jh", 256), ("nh", 256), ("sl", 32), ("eB", 256), ("IB", 256), ("oh", 256), ("pn", 256), ("Xh", 256), ("b16", 8)),
     BF: (("idb", 128), ("nib", 128), ("n2b", 128), ("k2b", 128), ("n4k", 128), ("c2k", 128), ("oneb", 128), ("dM", 128), ("dC", 128), ("wd", 128), ("bo4", 128), ("rcnt", 128), ("thr", 256),
          ("U", 144), ("UW", 144), ("cw", 48), ("zpl", 256), ("c24", 128), ("zn", 256), ("ze", 256), ("qx", 256), ("sg", 256), ("cn", 256), ("rT", 256), ("mk", 256), ("lo", 512)),
-    I32: (("pi", 256), ("pj", 256), ("ui", 32), ("sq", 16), ("cb0", 48), ("cb1", 48), ("bs", 16), ("ej", 256), ("vi", 256), ("vj", 256), ("ki", 64), ("el", 16), ("ij", 32)),
-    U16: (("xl", 16), ("e16", 256), ("elu", 16), ("ju", 256), ("nu", 256), ("of", 64), ("ILu", 16)),
+    I32: (("pi", 256), ("pj", 256), ("ui", 32), ("sq", 16), ("bs", 16), ("ej", 256), ("vi", 256), ("vj", 256), ("ki", 64), ("el", 16), ("ij", 32)),
+    U16: (("xl", 48), ("e16", 256), ("elu", 16), ("ju", 256), ("nu", 256), ("of", 64), ("ILu", 16)),
 }
 PLACE = {}
 for _d, _a in ((F32, "fA"), (F16, "hA"), (BF, "bA"), (I32, "iA"), (U16, "uA")):
@@ -54,10 +60,10 @@ for _d, _a in ((F32, "fA"), (F16, "hA"), (BF, "bA"), (I32, "iA"), (U16, "uA")):
 for _k in range(8):
     SCRATCH["ps%d" % _k] = ("psum", [128, 512], F32)
 NDMA = 44
-SEMAPHORES = ["eV", "eS", "eP", "eG", "snd", "arr1", "arr2", "arr3"] + ["d%d" % k for k in range(NDMA)] + ["%s%d" % (s, k) for s in ("out", "ret") for k in range(12)]
+SEMAPHORES = ["eV", "eS", "eP", "eG", "snd", ] + ["arr%d" % k for k in range(5)] + ["d%d" % k for k in range(NDMA)] + ["%s%d" % (s, k) for s in ("out", "ret") for k in range(12)]
 
 CY = 0.00083 * 1.1
-GA, SC, PEC, VO, SO, WAKE, DL = 1.4, 3.0, 0.00052, 0.035, 0.08, 0.09, 1.2
+GA, SC, PEC, VO, SO, WAKE, DL, RLAT = 1.4, 3.0, 0.00052, 0.035, 0.08, 0.09, 1.45, 3.6
 EST = []
 
 
@@ -266,30 +272,34 @@ def rank_program(g, core, T, topo):
     pe([(A("ps5", 0, 16), A("blk"), A("pd"))])
     conv(A("pB"), A("ps5", 0, 16))
     conv(A("id16"), A("idf"))
-    for m in range(16):
+    for m in range(0 if FAST else 16):
         conv(A("DP", m * 128, m * 128 + 128), A("id16"), A("pB", m, m + 1))
     ms(A("one16"), 1.0)
-    ms(A("z16"), 0.0)
     for k in range(0, 16, 4):
         aff(A("R", k * 128, k * 128 + 512), A("one16"), [[-1, 4], [-16, 8], [0, 16]], OP.is_equal, -k, 1)
     cp(A("rcol"), A("pj", 0, 1))
-    cp(A("thf"), A("thi"))
-    for name, c in (("idb", 1.0), ("nib", -1.0), ("n2b", -2.0), ("k2b", 2048.0), ("n4k", -4096.0), ("ni16", -1.0), ("hi16", 0.5), ("nh16", -0.5), ("i4k", 4096.0)):
+    conv(A("thf"), A("thi"), -1.0, -0.5)
+    for name, c in (("k2b", 2048.0), ("ni16", -1.0)):
         conv(A(name), A("id16"), c)
     aff(A("sh16"), A("one16", 0, 128), [[-1, 128]], OP.is_equal, -1, 1)
     for k, c in enumerate((16384.0, 1.0, -32768.0, -2.0, 32768.0, -65536.0)):
         conv(A("cw", 8 * k, 8 * k + 8), blk8, c)
-    conv(A("b16"), blk8)
     conv(A("bm4"), blk8, -4.0)
     conv(A("dP"), A("id16"), A("hkf", 0, 1))
     conv(A("dM"), A("id16"), A("rcol"), -64.0)
     ms(A("c2k"), 2048.0)
-    ms(A("oneb"), 1.0)
+    conv(A("hlf"), A("one"), 0.5)
     ms(A("rmin"), -4.0e7)
     ms(A("rmin", 0, 128, 16), 4.0e7)
     iot(A("pi", 16, 32), [[16, 16]], 15, 0)
     iot(A("pi", 24, 32), [[1, 8]], 128, 0)
-    cp(A("xl"), A("pi", 16, 32))
+    cp(A("xl", 0, 16), A("pi", 16, 32))
+    if FAST0:
+        iot(A("pi", 32, 48), [[1, 16]], 0, 0)
+        iot(A("pi", 48, 64), [[0, 16]], 0, 1)
+        ts(A("pj", 48, 64), A("pi", 48, 64), 15, OP.bitwise_and)
+        conv(A("xl", 16, 32), A("pi", 32, 48))
+        conv(A("xl", 32, 48), A("pj", 48, 64))
     iot(A("vi", 0, 128), [[0, 8], [-1, 16]], 16, 1)
     ts(A("vj", 0, 128), A("vi", 0, 128), 15, OP.bitwise_and)
     ts(A("msk", 0, 128), A("vj", 0, 128), 0.0, OP.is_equal)
@@ -320,13 +330,10 @@ def rank_program(g, core, T, topo):
     ts(A("kcol"), A("rcol"), -1.0, OP.mult, 15.0, OP.add)
     ts(A("ccol", 0, 1), A("rcol"), 15.0, OP.is_equal, -16384.0, OP.mult)
     tt(A("ccol", 1, 2), A("ccol", 0, 1), A("kcol"), OP.add)
-    ts(A("dC"), A("idf"), A("ccol", 1, 2), OP.mult, 1024.0, OP.mult)
-    ts(A("ccol", 0, 1), A("ccol", 0, 1), 0.125, OP.mult, A("thf", 0, 1), OP.add)
-    ts(A("ccol", 0, 1), A("ccol", 0, 1), -1.0, OP.mult, -0.5, OP.add)
-    ts(A("ccol", 0, 1), A("ccol", 0, 1), 1000.0, OP.min)
-    ts(A("dA"), A("idf"), A("ccol", 0, 1), OP.mult)
-    ts(A("thf", 1, 2), A("thf", 1, 2), -1.0, OP.mult, -0.5, OP.add)
-    ts(A("dB", 0, 128), A("idf"), A("thf", 1, 2), OP.mult)
+    ts(A("dCA", 0, 128), A("idf"), A("ccol", 1, 2), OP.mult, 1024.0, OP.mult)
+    tt(A("ccol", 0, 1), A("thf", 0, 1), A("ccol", 0, 1), OP.subtract)
+    conv(A("dCA", 128, 256), A("idf"), A("ccol", 0, 1))
+    conv(A("dB", 0, 128), A("id16"), A("thf", 1, 2))
     gcp(A("dB", 128, 256), A("dB", 0, 128))
     ms(A("rmax"), 4.0e7)
     ms(A("rmax", 0, 128, 16), -4.0e7)
@@ -335,7 +342,7 @@ def rank_program(g, core, T, topo):
     pe([(A("ps5", 32, 33), A("blk"), A("wtf"))])
     conv(A("wb"), A("ps5", 32, 33), 192.0)
     conv(A("pt", 0, W), A("lki"), 1.0 / 4096)
-    dma("G", T.pt[:, 0:W], T.xc[:], 4.0, [("pt", 0, W, 1)], [("pt", 0, W, 1)], acc=True)
+    dma("G", T.pt[:, 0:W], T.xc[:], 5.5, [("pt", 0, W, 1)], [("pt", 0, W, 1)], acc=True)
     conv(A("xw"), A("xcb"), 1.0, 192.0)
     conv(A("zn"), A("zin0"), -1.0, 192.0)
 
@@ -349,72 +356,96 @@ def rank_program(g, core, T, topo):
     def sums(out, src, lo, w, step):
         return [(out(k), src(k), w) for k in range(lo, lo + step)]
 
-    def firsts(bc, own, eqn, lo, ps, dump):
+    def firsts(bc, own, eqn, lo, ps, dump, a=0, b=256):
         O = lambda x, y: A(ps, 256 + x, 256 + y)
-        pe([(O(0, 256), A("oneb"), A("thr"))], True, False)
-        for c0, c1 in ((0, 3), (3, 7), (7, 11), (11, 16)):
-            calls, w, r, cost = [], [], [], 0.0
-            for c in range(c0, c1):
-                o, i, s = A3(eqn, c, c + 1, 0, 256 - 16 * c), A(bc, 16 * c, 256), A(own, c, c + 1)
+        pe([(O(a, b), A("one16", 0, 128), A("thr", a, b))], True, False)
+        for c0 in range(0, b // 16, 4):
+            calls, w, r, cost, terms = [], [], [], 0.0, []
+            for c in range(c0, c0 + 4):
+                x, y = max(a, 16 * c), max(a, 16 * c + 16)
+                o, i, s = A3(eqn, c, c + 1, x - 16 * c, b - 16 * c), A(bc, x, b), A(own, c, c + 1)
                 calls.append(lambda o=o, i=i, s=s: g.vector.tensor_scalar(o[0], i[0], s[0], None, OP.is_equal))
                 w.append(o[1])
                 r += [i[1], s[1]]
                 cost += vcost(i[2], o, i)
+                if y < b:
+                    terms.append((O(y, b), A("bo4"), A3(eqn, c, c + 1, y - 16 * c, b - 16 * c)))
             add("V", calls, w, sorted(set(r)), cost)
-            pe([(O(16 * c + 16, 256), A("bo4"), A3(eqn, c, c + 1, 16, 256 - 16 * c)) for c in range(c0, min(c1, 15))], False, False)
-        pe([(O(0, 256), A("wd"), A3(eqn, 0, 16, 0, 16))], False, True)
-        act(A("lo", lo, lo + 256), O(0, 256), AF.Sign)
-        out = A(ps, 0, 16)
-        pe([(out, A("id16"), dump)] + [(out, shifted("U", r), A("lo", lo + r, lo + 256, 16)) for r in range(16)])
+            pe(terms, False, False)
+        pe([(O(a, b), A("wd"), A3(eqn, a // 16, b // 16, 0, 16))], False, True)
+        act(A("lo", lo + a, lo + b), O(a, b), AF.Sign)
+        out = A(ps, a // 16, b // 16)
+        pe([(out, A("id16"), A("dmh", dump + a // 16, dump + b // 16))] + [(out, shifted("U", r), A("lo", lo + a + r, lo + b, 16)) for r in range(16)])
         return out
 
-    def cues(t):
-        head[0] = HC
+    def cues(t, h0, h1):
         z, cb, cf, zq = "zin%d" % t, "cb%d" % (t & 1), "cf%d" % (t & 1), "zq%d" % (t & 1)
-        u = A("ps6", 256, 272)
-        pe([(u, shifted("UW", r), A(z, r, 256, 16)) for r in range(16)])
+        a, b, c0, c1 = 128 * h0, 128 * h1, 8 * h0, 8 * h1
+        u, n = A("ps6", 256 + c0, 256 + c1), A(z if t else "zn", a, b)
+        pe([(u, shifted("UW", r), A(z, a + r, b, 16)) for r in range(16)])
         if t:
-            conv(A("ui", 0, 16), u, -1.0, A("wb"))
+            conv(A("ui", c0, c1), u, -1.0, A("wb"))
         else:
-            conv(A("ui", 0, 16), u)
-        ts(A("ui", 16, 32), A("ui", 0, 16), 4095, OP.bitwise_and)
-        tt(A("sq"), A("ui", 16, 32), A("ui", 16, 32), OP.mult)
-        ts(A(cb, 0, 16), A("ui", 0, 16), 2047, OP.bitwise_and)
-        ts(A(cb, 16, 32), A("sq"), 5, OP.logical_shift_right, 2047, OP.bitwise_and)
-        ts(A(cb, 32, 48), A("sq"), 4, OP.logical_shift_right, 1023, OP.bitwise_and)
-        conv(A(cf), A(cb))
-        for m0 in range(0, 16, 4):
-            terms = []
-            for m in range(m0, m0 + 4):
-                o = A("ps6", 16 * m, 16 * m + 16)
-                terms += [(o, A("DP", m * 128, m * 128 + 128), A(cf, 0, 16)), (o, A("id16"), A(cf, 16, 32))]
-            pe(terms, each=2)
+            conv(A("ui", c0, c1), u)
+        ts(A3(cb, 0, 1, c0, c1), A("ui", c0, c1), 2047, OP.bitwise_and)
+        if not FAST:
+            conv(A3(cf, 0, 1, c0, c1), A3(cb, 0, 1, c0, c1))
+        ts(A("ui", 16 + c0, 16 + c1), A("ui", c0, c1), 4095, OP.bitwise_and)
+        tt(A("sq", c0, c1), A("ui", 16 + c0, 16 + c1), A("ui", 16 + c0, 16 + c1), OP.mult)
+        ts(A3(cb, 2, 3, c0, c1), A("sq", c0, c1), 5, OP.logical_shift_right, 2047, OP.bitwise_and)
+        ts(A3(cb, 1, 2, c0, c1), A("sq", c0, c1), 4, OP.logical_shift_right, 1023, OP.bitwise_and)
+        if FAST:
+            gcp(A3(cf, 0, 2, c0, c1), A3(cb, 0, 2, c0, c1))
+        else:
+            conv(A3(cf, 1, 3, c0, c1), A3(cb, 1, 3, c0, c1))
+        w = c1 - c0
+        if t == 0 and FAST0:
+            gat("VS", A("prow"), A("pB"), A("xl", 16, 32))
+        if (t == 0 and FAST0) or FAST:
+            gatop(A("e0"), A3(cb, 0, 1, 0, 16), A("xl", 32, 48), A("prow"), OP.mult)
+        if t == 0 and FAST0:
+            gatop(A("ej"), A3(cb, 2, 3, 0, 16), A("xl", 32, 48), A("e0"), OP.add)
+            ts(A3("ei", 0, 16, 0, 16), A("ej"), 2047, OP.bitwise_and)
+        for row in () if (t == 0 and FAST0) or FAST else (0, 2):
+            for m0 in (0, 8):
+                pe([(A("ps6", a + w * m, a + w * m + w), A("id16") if row else A("DP", m * 128, m * 128 + 128), A3(cf, row, row + 1, c0, c1))
+                    for m in range(m0, m0 + 8)], row + m0 == 0, row + m0 == 10)
         for x in range(0, 512, 128):
-            gcp(A3(zq, 0, 2, x, x + 128), A(z if t else "zn"))
+            gcp(A3(zq, h0, h1, x, x + 128), n)
         if 0 < t < RO - 1:
-            conv(A("zpl"), A(z), -1.0, 192.0)
-        zr = "zr%d" % (t & 1)
+            conv(A("zpl", a, b), n, -1.0, 192.0)
         for m in range(16):
-            conv(A(zr, m, 4096, 16), A(z if t else "zn"), qs=ZPLAN[t])
+            conv(A("zr%d" % (t & 1), 16 * a + m, 16 * b, 16), n, qs=ZPLAN[t])
 
-    cues(0)
     H = ((0, 0, 128), (1, 128, 256))
     for t in range(RO):
         z, zr, cb, cf, zq = "zin%d" % t if t else "zn", "zr%d" % (t & 1), "cb%d" % (t & 1), "cf%d" % (t & 1), "zq%d" % (t & 1)
-        if t:
-            conv(A3("ei", 0, 16, 0, 16), A("ps6", 0, 256), 1.0, A("acol"))
-            conv(A("bs"), A(cb, 16, 32), 1.0, A("acol"))
-        else:
-            conv(A3("ei", 0, 16, 0, 16), A("ps6", 0, 256))
+        acol = A("ps6", 272, 273)
+        if t == 0:
+            cues(0, 0, 2)
+            if not FAST0:
+                conv(A3("ei", 0, 16, 0, 16), A("ps6", 0, 256))
+        elif FAST:
+            ts(A("bs"), A3(cb, 2, 3, 0, 16), acol, OP.add, 1024.0, OP.add)
+            gatop(A("ej"), A("bs"), A("xl", 32, 48), A("e0"), OP.add)
+            ts(A3("ei", 0, 16, 0, 16), A("ej"), 2047, OP.bitwise_and)
+        elif not SPLIT:
+            ts(A3("ei", 0, 16, 0, 16), A("ps6", 0, 256), acol, OP.add, 1024.0, OP.add)
+            ts(A("bs"), A3(cb, 2, 3, 0, 16), acol, OP.add, 1024.0, OP.add)
         for (h, a, b) in H:
-            ts(A("ej", a, b), A3("ei", 0, 16, 8 * h, 8 * h + 8), 2047, OP.bitwise_and)
-            conv(A("e16", a, b), A("ej", a, b))
-        base, boff = ("bs", 0) if t else (cb, 16)
+            if t and SPLIT:
+                if h:
+                    cues(t, 1, 2)
+                ts(A3("ei", 8 * h, 8 * h + 8, 0, 16), A("ps6", a, b), acol, OP.add, 1024.0, OP.add)
+                ts(A("bs", 8 * h, 8 * h + 8), A3(cb, 2, 3, 8 * h, 8 * h + 8), acol, OP.add, 1024.0, OP.add)
+                ts(A("ej", a, b), A3("ei", 8 * h, 8 * h + 8, 0, 16), 2047, OP.bitwise_and)
+            elif not FAST and (t or not FAST0):
+                ts(A("ej", a, b), A3("ei", 0, 16, 8 * h, 8 * h + 8), 2047, OP.bitwise_and)
+            conv(A("e16", a, b), A("ej", a, b) if not FAST and (t or not FAST0) else A3("ei", 0, 16, 8 * h, 8 * h + 8))
         for (h, a, b) in H:
             c0, c1, ps, X = 8 * h, 8 * h + 8, "ps%d" % (2 + h), "X%d" % h
             gd, ga, px, yd, ya, fa = ["%s%d" % (n, h) for n in ("gd", "ga", "px", "yd", "ya", "fa")]
             key = lambda k: A(ps, k, 128, 16)
-            pe([(A(ps, 0, 128), A("z16"), A("one16", 0, 128))], True, False)
             for j in range(4):
                 x, y, q = 512 * j, 512 * j + 512, GPLAN[t][4 * h + j]
                 lst, zz = A("e16", a + 32 * j, a + 32 * j + 32), A3(zq, h, h + 1, 0, 512)
@@ -422,7 +453,7 @@ def rank_program(g, core, T, topo):
                     gat("S", A(gd, x, y), A("gist", 0, E), lst)
                     d = A("ps%d" % bank[0])
                     bank[0] ^= 1
-                    pe([(d, A("idb"), A(gd, x, y))] + [(A(d[1][0], v, v + 128), A("idb"), A(z, a, b)) for v in range(0, 512, 128)])
+                    pe([(d, A("id16"), A(gd, x, y))] + [(A(d[1][0], v, v + 128), A("id16"), A(z, a, b)) for v in range(0, 512, 128)])
                     act(A(ga, x, y), d, AF.Abs, 1.0, -192.0)
                 else:
                     gatop(A(gd, x, y), A("gist", 0, E), lst, zz, OP.add)
@@ -430,17 +461,17 @@ def rank_program(g, core, T, topo):
                         act(A(ga, x, y), A(gd, x, y), AF.Abs, 1.0, -192.0)
                     else:
                         ts(A(ga, x, y), A(gd, x, y), 192.0, OP.min, -96.0, OP.add)
-                        pe(sums(key, lambda m: A(gd, 128 * m, 128 * m + 128), 4 * j, A("cw", 32, 40), 4), False, False)
-                pe(sums(key, lambda m: A(ga, 128 * m, 128 * m + 128), 4 * j, A("cw", 40, 48) if q == "V" else A("cw", 32, 40), 4), False, False)
+                        pe(sums(key, lambda m: A(gd, 128 * m, 128 * m + 128), 4 * j, A("cw", 32, 40), 4), j == 0, False)
+                pe(sums(key, lambda m: A(ga, 128 * m, 128 * m + 128), 4 * j, A("cw", 40, 48) if q == "V" else A("cw", 32, 40), 4), j == 0 and q != "V", False)
             pe([(A(ps, 0, 128), A("c2k"), A("dM")), (A(ps, 0, 128), A("one16", 0, 128), A("dP"))], False, True)
             km = "km%d" % h
             scan(A(km, 0, 128), A("rmin"), A(ps, 0, 128), 4.0e7, OP.max, OP.min)
             ts(A(km, 128, 136), A(km, 15, 128, 16), 2047, OP.bitwise_and)
             gatop(A("Xh", a, b), A(km), A("xl", 8, 16), A("msk", 0, 128), OP.mult)
-            pe([(A(ps, 0, 8), A("Xh", a, b), A("b16"))])
+            pe([(A(ps, 0, 8), A("Xh", a, b), A("cw", 8, 16))])
             i2, i3 = [A("ki", 32 * h + 8 * x, 32 * h + 8 * x + 8) for x in range(2)]
-            tt(i2, A(ps, 0, 8), A(cb, c0, c1), OP.mult)
-            tt(i3, i2, A(base, boff + c0, boff + c1), OP.add)
+            tt(i2, A(ps, 0, 8), A3(cb, 0, 1, c0, c1), OP.mult)
+            tt(i3, i2, A("bs", c0, c1) if t else A3(cb, 2, 3, c0, c1), OP.add)
             ts(A("el", c0, c1), i3, 2047, OP.bitwise_and)
             conv(A("elu", c0, c1), A("el", c0, c1))
             gat("VS", A("ju", a, b), A("ixi", 0, E), A("elu", c0, c1))
@@ -451,19 +482,22 @@ def rank_program(g, core, T, topo):
             pe([(A(ps, 128 + k, 256, 16), A(px, k, 2048, 16), A("idf", k, 128, 16)) for k in range(16)], each=True)
             conv(A("qx", a, b), nT, 1.0, 128.0)
             conv(A("fr", a, b), nT)
-            pe([(A(ps, 0, 128), A("fr", a, b), A("i4k")), (A(ps, 0, 128), A("qx", a, b), A("n4k"))])
-            conv(A("nu", a, b), A(ps, 0, 128), 1.0, 128.0 * 4096)
+            pe([(A(ps, 0, 128), A("fr", a, b), A("idf")), (A(ps, 0, 128), A("qx", a, b), A("ni16"))])
+            conv(A("nu", a, b), A(ps, 0, 128), 4096.0, 128.0 * 4096)
             gcp(A("nh", a, b), A("nu", a, b))
             for x in range(0, 2048, FCUT):
                 addto(A(zr, 2048 * h + x, 2048 * h + x + FCUT), A(px, x, x + FCUT), 2.0 + 3.0 * FCUT / 2048)
         for (h, a, b) in H:
             head[0] = HZ
-            diff = ZMAX[t][h] == "d"
+            terms = []
             for x in (0, 1024):
+                diff, l = ZMAX[t][2 * h + x // 1024] == "d", a + x // 16
                 src = A(zr, 2048 * h + x, 2048 * h + x + 1024) if diff else A("px%d" % h, x, x + 1024)
                 scan(A("zs%d" % h, x, x + 1024), A("rz"), src, 0.0, OP.min, OP.max)
+                zp = A("ps6", 256 + l, 320 + l)
+                terms += [(zp, A("ni16"), A(z, l, l + 64))] * (2 if diff else 1) + [(zp, A("id16"), A("zs%d" % h, x + 15, x + 1024, 16))]
+            pe(terms)
             zp = A("ps6", 256 + a, 256 + b)
-            pe([(zp, A("n2b" if diff else "nib"), A(z, a, b)), (zp, A("id16"), A("zs%d" % h, 15, 2048, 16))])
             if t < RO - 1:
                 conv(A("zo%d" % t, a, b), zp, -0.5, 96.25)
             else:
@@ -474,67 +508,57 @@ def rank_program(g, core, T, topo):
         eng = topo.engines(core, dst)[:NENG]
         rid, pid, _se = topo.addr(dst)
         mask = sum(1 << e for e in eng)
-        add("G", [lambda land=land, rid=rid, pid=pid, mask=mask, t=t: g.remote_dma(
-            T[land][:], T["zo%d" % t][:], T.sem["arr%d" % (t + 1)], T.sem.snd, pid, rid, mask)],
-            [(land, 0, 256, 1)], [("zo%d" % t, 0, 256, 1)], 1.0, 3.0 * DL, "r", "arr%d" % (t + 1), len(eng))
-        head[0] = 0.0
+        for a, b in ((0, 128), (128, 256)) if SPLIT and t < RO - 1 else ((0, 256),):
+            sem = "arr%d" % (2 * t + a // 128)
+            add("G", [lambda land=land, rid=rid, pid=pid, mask=mask, t=t, a=a, b=b, sem=sem: g.remote_dma(
+                T[land][:, a:b], T["zo%d" % t][:, a:b], T.sem[sem], T.sem.snd, pid, rid, mask)],
+                [(land, a, b, 1)], [("zo%d" % t, a, b, 1)], 1.0, RLAT, "r", sem, len(eng))
         gcp(A("elh"), A("el"))
         gcp(A("elf"), A("el"))
         pe(spread("ps7", 0, A("elh")), each=True)
         conv(A("eB"), A("ps7", 0, 256))
-        tt(A("of0"), firsts("eB", "elf", "eq", 0, "ps7", A("dmh", 0, 16)), A("elf"), OP.max)
-        gcp(A("of", 0, 16), A("of0"))
-        pe(spread("ps5", 0, A(cf, 0, 16)), each=True)
+        tt(A("of", 0, 16), firsts("eB", "elf", "eq", 0, "ps7", 0), A("elf"), OP.max)
+        pe(spread("ps5", 0, A3(cf, 0, 2, 0, 16)), each=True)
         conv(A("xq"), A("ps5", 0, 256), A("hkf", 1, 2))
-        pe([(A("ps5", 256, 512), A("idf"), A("xq"))] + spread("ps5", 256, A(cf, 32, 48)))
-        conv(A("vi"), A("ps5", 256, 512))
+        tt(A("vi"), A("ps5", 256, 512), A("xq"), OP.add)
         ts(A("vj"), A("vi"), 1023, OP.bitwise_and)
         gcp(A("v16"), A("vj"))
         if t < RO - 1:
-            cues(t + 1)
+            cues(t + 1, 0, 1 if SPLIT else 2)
         for (h, a, b) in H:
             c0, c1, ps, X, kc = 8 * h, 8 * h + 8, "ps%d" % (2 + h), "X%d" % h, "kc%d" % h
             px, yd, ya = "px%d" % h, "yd%d" % h, "ya%d" % h
-            for q in (0, 64):
-                x, y, lst = 16 * q, 16 * q + 1024, A("nu", a + q, a + q + 64)
+            pe([(A(ps, 256, 512), A("one"), A("dCA")), (A(ps, 256, 384), A("jh", a, b), A("id16"))], True, False)
+            for q, r in YCUT[h]:
+                x, y, lst = 16 * q, 16 * r, A("nu", a + q, a + r)
                 if YPLAN[t][2 * h + q // 64] == "V":
                     gatop(A(yd, x, y), A("xw"), lst, A(px, x + 1, y + 1), OP.subtract)
                 else:
                     gat("S", A(yd, x, y), A("xcb"), lst, -1.0, 192.0)
                     addto(A(yd, x, y), A(px, x + 1, y + 1), 3.5)
-                if YABS[t][h] == "S":
-                    act(A(ya, x, y), A(yd, x, y), AF.Abs, 1.0, -192.0)
-                else:
-                    ts(A(ya, x, y), A(yd, x, y), 192.0, OP.min, -96.0, OP.add)
-            key = lambda k: A(ps, 256 + k, 512, 16)
-            pe([(A(ps, 256, 512), A("z16"), A("one16", 0, 256)), (A(ps, 384, 512), A("one16", 0, 128), A("dA"))], True, False)
-            if YABS[t][h] == "S":
-                pe(sums(key, lambda k: A(ya, k, 2048, 16), 0, A("cw", 0, 16), 16), False, False)
-            else:
-                pe(sums(key, lambda k: A(yd, k, 2048, 16), 0, A("cw", 0, 16), 16), False, False)
-                pe(sums(key, lambda k: A(ya, k, 2048, 16), 0, A("cw", 16, 32), 16), False, False)
-            pe([(A(ps, 256, 384), A("oneb"), A("dC")), (A(ps, 256, 384), A("jh", a, b), A("id16"))], False, True)
+                act(A(ya, x, y), A(yd, x, y), AF.Abs, 1.0, -192.0)
+            pe(sums(lambda k: A(ps, 256 + k, 512, 16), lambda k: A(ya, k, 2048, 16), 0, A("cw", 0, 16), 16), False, True)
             act(A("sg", a, b), A(ps, 384, 512), AF.Sign)
             scan(A("cn", a, b), A("rcnt"), A("sg", a, b), 0.0, OP.mult, OP.add)
             ts(A(kc, 128, 136), A("cn", a + 15, b, 16), -6.0, OP.is_le)
+            if t < RO - 1:
+                act(A("junk", c0, c1), A("cn", a + 15, b, 16), AF.Sign, -1.0, -5.0, total=A("acol", h, h + 1))
             scan(A(kc, 0, 128), A("rmax"), A(ps, 256, 384), -4.0e7, OP.min, OP.max)
-            gatop(A(X), A(kc), A("xl"), A("msk", 2 * a, 2 * b), OP.mult)
+            gatop(A(X), A(kc), A("xl", 0, 16), A("msk", 2 * a, 2 * b), OP.mult)
             pe([(A(ps, 0, 8), A(X, 0, 128), blk8), (A(ps, 8, 16), A(X, 128, 256), blk8)], each=True)
             if t < RO - 1:
                 pe([(A(ps, 16, 24), A("idf"), A("dmp", c0, c1)), (A(ps, 16, 24), A(X, 128, 256), A("bm4"))])
-                tt(A("oT", c0, c1), A(ps, 16, 24), A("of0", c0, c1), OP.max)
-                conv(A("of", 16 + c0, 16 + c1), A("oT", c0, c1))
+                tt(A("of", 16 + c0, 16 + c1), A(ps, 16, 24), A("of", c0, c1), OP.max)
                 scat(A("gist"), A("of", 16 + c0, 16 + c1), A("zpl" if t else "zin0", a, b))
             conv(A3("ksl", h, h + 1, 0, 16), A(ps, 0, 16))
             gat("VS", A("rT", a, b), A(kc), A("xl", 8, 16))
         if t < RO - 1:
-            cnt = A("ps6", 272, 280)
-            pe([(cnt, A("one"), A("kc0", 128, 136)), (cnt, A("one"), A("kc1", 128, 136))])
-            act(A("junk", 0, 8), cnt, AF.Copy, total=A("acol"))
-        pe([(A("ps4"), A("z16"), A("one16")), (A("ps4", 0, 256), A("one16", 0, 128), A("dB"))], True, False)
+            cnt = A("ps6", 272, 273)
+            pe([(cnt, A("hlf"), A("acol", h, h + 1)) for h in (0, 1)])
+        pe([(A("ps4", 0, 256), A("one16", 0, 128), A("dB"))], True, False)
         for (h, a, b) in H:
             fa, far = "fa%d" % h, lambda k: A("ps4", a + k, b, 16)
-            pe([(A("ps4", 256 + a, 256 + b), A("v16", a, b), A("hi16")), (A("ps4", 256 + a, 256 + b), A("jh", a, b), A("nh16"))], False, False)
+            pe([(A("ps4", 256 + a, 256 + b), A("v16", a, b), A("id16")), (A("ps4", 256 + a, 256 + b), A("jh", a, b), A("ni16"))], False, False)
             for x in range(0, 2048, FCUT):
                 d = A(zr, 2048 * h + x, 2048 * h + x + FCUT)
                 if FABS[t][h] == "S":
@@ -550,7 +574,7 @@ def rank_program(g, core, T, topo):
                     ops[-1]["sent"], ops[-1]["deps"] = HENG, {i: (w if ops[i]["w"][:1] == [A(fa, x, x + FCUT)[1]] or ops[i]["w"][1:] != [("fold", 0, 1, 1)] else False)
                                                               for i, w in ops[-1]["deps"].items()}
             if FABS[t][h] == "H":
-                pe([(A("ps4", a, b), A("oneb"), A("c24"))], False, False)
+                pe([(A("ps4", a, b), A("one16", 0, 128), A("c24"))], False, False)
             if FABS[t][h] == "S":
                 pe(sums(far, lambda k: A(fa, k, 2048, 16), 0, A("cw", 8, 16), 16), False, False)
             else:
@@ -560,38 +584,47 @@ def rank_program(g, core, T, topo):
         act(A("mk"), A("ps4", 0, 256), AF.Sign)
         tt(A("pn"), A("ps4", 256, 512), A("mk"), OP.mult)
         nn = A("ps4", 0, 256)
-        pe([(nn, A("hi16"), A("v16")), (nn, A("hi16"), A("jh"))] + [(A("ps4", a, b), A("pn", a, b), A("id16")) for (h, a, b) in H])
-        conv(A("nn"), nn)
+        pe([(nn, A("id16"), A("v16")), (nn, A("id16"), A("jh"))] + [(A("ps4", a, b), A("pn", a, b), A("id16")) for (h, a, b) in H])
+        conv(A("nn"), nn, 0.5)
         if t == RO - 1:
             for x in range(0, E, 512):
                 gcp(A("nm", x, x + 512), A("ixi", x, x + 512))
         scat(A("ixi" if t < RO - 1 else "nm"), A("of", 0, 16), A("nn"))
-        ts(A("ij", 0, 16), A3("ksl", 0, 2, 0, 8), 1023, OP.bitwise_and)
-        ts(A("ij", 16, 32), A3("ksl", 0, 2, 0, 8), 10, OP.logical_shift_right, 15, OP.bitwise_and)
-        conv(A("sl"), A("ij"))
-        gcp(A("ILu"), A("ij", 0, 16))
-        tt(A("own"), A("ij", 0, 16), A3("ksl", 0, 2, 8, 16), OP.max)
-        pe(spread("ps7", 0, A("sl")), each=True)
-        conv(A("IB"), A("ps7", 0, 256))
-        ts(A("oh"), A("ps7", 256, 512), A("kcol"), OP.is_equal, 1.0 / 4096 if t < RO - 1 else 1.0, OP.mult)
-        dp = A("ps5", 256, 512)
-        pe([(dp, A("sh16"), A("jh")), (dp, A("ni16"), A("nh"))])
-        tt(A("dl"), dp, A("oh"), OP.mult)
-        tab = "pt" if t < RO - 1 else "lkt"
-        gat("VS", A("nl"), A(tab, 0, W), A("ILu"))
-        tt(A("oT", 16, 32), firsts("IB", "own", "eq2", 256, "ps5" if t < RO - 1 else "ps0", A("dmh", 16, 32)), A("own"), OP.max)
-        conv(A("of", 32, 48), A("oT", 16, 32))
-        scat(A(tab), A("of", 32, 48), A("nl"), A("dl"))
+        tab, writes = "pt" if t < RO - 1 else "lkt", []
+        for h0, h1 in ((0, 1), (1, 2)) if LSPLIT[t] else ((0, 2),):
+            a, b, c0, c1 = 128 * h0, 128 * h1, 8 * h0, 8 * h1
+            w = c1 - c0
+            ij, sl = 2 * c0, A("sl", 2 * c0, 2 * c1)
+            ts(A("ij", ij, ij + w), A3("ksl", h0, h1, 0, 8), 1023, OP.bitwise_and)
+            ts(A("ij", ij + w, ij + 2 * w), A3("ksl", h0, h1, 0, 8), 10, OP.logical_shift_right, 15, OP.bitwise_and)
+            conv(sl, A("ij", ij, ij + 2 * w))
+            gcp(A("ILu", c0, c1), A("ij", ij, ij + w))
+            tt(A("own", c0, c1), A("ij", ij, ij + w), A3("ksl", h0, h1, 8, 16), OP.max)
+            pe(spread("ps7", 0, sl), each=True)
+            conv(A("IB", a, b), A("ps7", 0, b - a))
+            ts(A("oh", a, b), A("ps7", b - a, 2 * (b - a)), A("kcol"), OP.is_equal, 1.0 / 4096 if t < RO - 1 else 1.0, OP.mult)
+            dp = A("ps5", 256 + a, 256 + b)
+            pe([(dp, A("sh16"), A("jh", a, b)), (dp, A("ni16"), A("nh", a, b))])
+            tt(A("dl", a, b), dp, A("oh", a, b), OP.mult)
+            gat("VS", A("nl", a, b), A(tab, 0, W), A("ILu", c0, c1))
+            tt(A("of", 32 + c0, 32 + c1), firsts("IB", "own", "eq2", 256, "ps5" if t < RO - 1 else "ps%d" % h0, 16, a, b), A("own", c0, c1), OP.max)
+            scat(A(tab), A("of", 32 + c0, 32 + c1), A("nl", a, b), A("dl", a, b))
         if t == RO - 2:
             for x, ps in ((0, "ps5"), (512, "ps7")):
-                pe([(A(ps), A("i4k"), A("pt", x, x + 512)), (A(ps), A("n4k"), A("xcb", x, x + 512))])
-                conv(A("lkt", x, x + 512), A(ps))
+                pe([(A(ps), A("idf"), A("pt", x, x + 512)), (A(ps), A("ni16"), A("xcb", x, x + 512))])
+                conv(A("lkt", x, x + 512), A(ps), 4096.0)
     dma("Y", T.yz[:], T.zfin[:], 2.5, [], [("zfin", 0, 256, 1)])
     dma("Y", T.yi[:], T.nm[:, 0:E], 5.0, [], [("nm", 0, E, 1)])
     dma("Y", T.yl[:], T.lkt[:, 0:W], 3.5, [], [("lkt", 0, W, 1)])
 
     n = len(ops)
-    users = [[] for _ in range(n)]
+    users, done = [[] for _ in range(n)], []
+    for o in ops:
+        seen = 0
+        for d in o["deps"]:
+            seen |= done[d]
+        o["deps"] = {d: w for d, w in o["deps"].items() if not seen >> d & 1}
+        done.append(seen | sum(1 << d for d, w in o["deps"].items() if w))
     for o in ops:
         for d in o["deps"]:
             users[d].append(o["i"])
@@ -653,6 +686,109 @@ def rank_program(g, core, T, topo):
                     ready.insert(lo, x)
         return start, on, span, end
 
+    def timed(lines, on, old=None, t0=-1.0):
+        then, before = ahead[0], back[0]
+        avail, end, why = (list(old[0]), list(old[3]), list(old[4])) if old else ([0.0] * n, [0.0] * n, [-1] * n)
+        left, nxt, todo, count = [-1] * n, [-1] * n, [], 0
+        new = [s >= t0 for s in avail]
+        for line in lines.values():
+            a, k = -1, len(line)
+            while k and new[line[k - 1]]:
+                k -= 1
+            if k:
+                a = line[k - 1]
+            for j in line[k:]:
+                s, cause, c = 0.0, -1, 0
+                for d, wait in before[j]:
+                    if new[d]:
+                        c += 1
+                    else:
+                        w = avail[d] + 1e-6 if wait is None else end[d] + wait
+                        if w > s:
+                            s, cause = w, d
+                if a >= 0:
+                    if new[a]:
+                        nxt[a] = j
+                        c += 1
+                    elif end[a] >= s:
+                        s, cause = end[a], a
+                left[j], why[j], a = c, cause, j
+                end[j] = s
+                count += 1
+                if c == 0:
+                    todo.append(j)
+        while todo:
+            i = todo.pop()
+            count -= 1
+            s = avail[i] = end[i]
+            f = end[i] = s + price[i][on[i]]
+            for j, wait in then[i]:
+                w = s + 1e-6 if wait is None else f + wait
+                if w > end[j]:
+                    end[j], why[j] = w, i
+                left[j] -= 1
+                if left[j] == 0:
+                    todo.append(j)
+            j = nxt[i]
+            if j >= 0:
+                if f >= end[j]:
+                    end[j], why[j] = f, i
+                left[j] -= 1
+                if left[j] == 0:
+                    todo.append(j)
+        if count:
+            return None
+        span, last = max((end[i] + lat[i], i) for i in final)
+        chain = [last]
+        while why[chain[-1]] >= 0:
+            chain.append(why[chain[-1]])
+        return avail, span, chain, end, why
+
+    def polish(start, on, rng):
+        on = list(on)
+        lines = {q: sorted((i for i in range(n) if on[i] == q), key=lambda i: (start[i], i)) for q in queues}
+        now = timed(lines, on)
+        top = (now[0], list(on), now[1])
+        for k in range(MOVES):
+            chain = now[2]
+            x = int(rng.randint(len(chain) - 1))
+            v, u, kind = chain[x], chain[x + 1], rng.rand()
+            if kind < 0.1:
+                v = int(rng.randint(n))
+            q = on[v]
+            if kind < 0.3:
+                if len(choice[v]) < 2:
+                    continue
+                r = [c for c, _p in choice[v] if c != q][int(rng.randint(len(choice[v]) - 1))]
+                at = now[0][v] - rng.rand()
+                new = dict(lines)
+                new[q] = [i for i in lines[q] if i != v]
+                p = sum(1 for i in lines[r] if now[0][i] < at)
+                new[r] = lines[r][:p] + [v] + lines[r][p:]
+                on[v], t0 = r, at
+            else:
+                if on[u] != q or u in ops[v]["deps"]:
+                    continue
+                line, far = lines[q], int(rng.randint(4))
+                p = line.index(u)
+                if kind < 0.65:
+                    a = max(0, p - far)
+                    new = dict(lines)
+                    new[q], t0 = line[:a] + [v] + line[a:p + 1] + line[p + 2:], now[0][line[a]]
+                else:
+                    b = min(len(line), p + 2 + far)
+                    new = dict(lines)
+                    new[q], t0 = line[:p] + line[p + 1:b] + [u] + line[b:], now[0][u]
+            got = timed(new, on, now, t0)
+            if got is not None and got[1] <= now[1] - HEAT * (1.0 - k / MOVES) * np.log(rng.rand()):
+                lines, now = new, got
+                if now[1] < top[2]:
+                    top = (now[0], list(on), now[1])
+            else:
+                on[v] = q
+        return top
+
+    price, final = [dict(c) for c in choice], [i for i in range(n) if not users[i]]
     if n not in ORDER:
         key, lean = np.array([way[i] + ops[i]["head"] for i in range(n)]), np.full(n, LEAN)
         best = top = place(key.tolist(), lean.tolist(), ahead)
@@ -660,7 +796,7 @@ def rank_program(g, core, T, topo):
         for k in range(TRIES):
             near = (np.abs(np.array(best[0]) - rng.rand() * best[2]) < 5.0) * (rng.rand(n) < (0.05, 0.2, 0.5)[k % 3])
             nl = lean + near * (rng.rand(n) < 0.3) * rng.randn(n)
-            if k % 4 == 3:
+            if k % 2 == 1:
                 nk = np.array(place((np.array(best[3]) + near * rng.randn(n)).tolist(), nl.tolist(), back)[3])
             else:
                 nk = key + near * rng.randn(n) * (0.5, 1.5, 4.0)[(k // 4) % 3]
@@ -669,8 +805,8 @@ def rank_program(g, core, T, topo):
                 key, lean, best = nk, nl, new
                 if best[2] < top[2]:
                     top = best
-        ORDER[n] = top
-    start, on, _span, _end = ORDER[n]
+        ORDER[n] = polish(top[0], top[1], rng)
+    start, on, _span = ORDER[n]
     order = sorted(range(n), key=lambda i: (start[i], i))
     for o in ops:
         if "alts" in o:

import numpy as np
from concourse.bass import DstId, RemoteDMATransfer
from concourse.mybir import AluOpType as OP, ActivationFunctionType as AF

W, E, B, RO = 1024, 2048, 256, 3
NENG = 8
GPLAN = ("VSVSVSVS", "VSVSSVSS", "VSVSSVSS")
LSPLIT = (False, False, False)
FAST0 = FAST = True
SPLIT = False
YCUT = (((0, 128),), ((0, 64), (64, 96), (96, 128)))
PCUT = 32
YPLAN = ("VVVV", "VVVV", "VVVV")
YABS = ("SS", "SS", "SS")
FABS = ("SS", "SS", "SS")
ZMAX = ("pppp", "pppp", "dddd")
ZPLAN = ("VG", "G", "G")
HENG, RENG, HLAT = 8, 16, 12.0
FCUT = 1024
TRIES, ORDER = 600, {}
MOVES, HEAT = 150000, 0.1
HZ, HC, LEAN, SLACK, SEED = 0.0, 0.0, 1.5, 0.5, 4
F32, BF, F16, I32, U16 = "float32", "bfloat16", "float16", "int32", "uint16"

SCRATCH = {
    "gist": ("sbuf", [128, E + B], BF), "nm": ("sbuf", [128, E + B], F32), "ixi": ("sbuf", [128, E + B], I32),
    "pt": ("sbuf", [128, W + B], F32), "lkt": ("sbuf", [128, W + B], F32), "xw": ("sbuf", [128, W], BF),
    "xcb": ("sbuf", [128, W], BF), "lki": ("sbuf", [128, W], I32),
    "wti": ("sbuf", [128, 1], I32), "hki": ("sbuf", [128, 2], I32), "thi": ("sbuf", [128, 2], I32),
    "zin0": ("sbuf", [128, B], BF), "zin1": ("sbuf", [128, B], BF), "zin2": ("sbuf", [128, B], BF), "zfin": ("sbuf", [128, B], BF),
    "zo0": ("sbuf", [128, B], BF), "zo1": ("sbuf", [128, B], BF), "zo2": ("sbuf", [128, B], BF),
    "R": ("sbuf", [128, 2048], F16), "DP": ("sbuf", [128, 2048], F16), "rz": ("sbuf", [128, 1024], BF),
    "zr0": ("sbuf", [128, 4096], BF), "zr1": ("sbuf", [128, 4096], BF), "zq0": ("sbuf", [128, 2, 512], BF), "zq1": ("sbuf", [128, 2, 512], BF),
    "eq": ("sbuf", [128, 16, 256], BF), "eq2": ("sbuf", [128, 16, 256], BF), "ei": ("sbuf", [128, 16, 16], I32),
    "cb0": ("sbuf", [128, 3, 16], I32), "cb1": ("sbuf", [128, 3, 16], I32), "cf0": ("sbuf", [128, 3, 16], F16), "cf1": ("sbuf", [128, 3, 16], F16),
    "ksl": ("sbuf", [128, 2, 32], I32), "c192": ("sbuf", [128, FCUT], BF),
}
for _k in (0, 1):
    for _n, _d, _w in (("gd", BF, 2048), ("ga", BF, 2048), ("px", F32, 2064), ("yd", BF, 2048), ("ya", BF, 2048), ("fa", BF, 2048), ("zs", F16, 2048),
                       ("km", I32, 136), ("kc", F32, 136)):
        SCRATCH["%s%d" % (_n, _k)] = ("sbuf", [128, _w], _d)
_SMALL = {
    F32: (("wtf", 1), ("hkf", 2), ("thf", 2), ("one", 128), ("idf", 128), ("blk", 128), ("dCA", 256), ("prow", 256), ("e0", 256), ("bm4", 8), ("pd", 16), ("pB", 16), ("pw", 16), ("half", 16), ("zero", 16),
          ("tw", 16), ("wcol", 1), ("rcol", 1), ("kcol", 1), ("ccol", 2), ("wb", 1), ("dmp", 32), ("lcol", 2), ("msk", 512), ("rmin", 128), ("rmax", 128), ("xq", 256),
          ("X0", 256), ("X1", 256), ("elf", 16), ("of0", 16), ("oT", 32), ("own", 16), ("acol", 2), ("hlf", 128), ("junk", 16), ("dl", 256), ("nl", 256), ("nn", 256), ("fr", 256)),
    F16: (("id16", 128), ("ni16", 128), ("hi16", 128), ("nh16", 128), ("sh16", 128), ("one16", 512), ("z16", 128), ("dP", 128), ("dA", 128), ("dB", 256), ("dmh", 32),
          ("v16", 256), ("elh", 16), ("jh", 256), ("nh", 256), ("sl", 32), ("eB", 256), ("IB", 256), ("oh", 256), ("pn", 256), ("Xh", 256), ("b16", 8)),
    BF: (("idb", 128), ("nib", 128), ("n2b", 128), ("k2b", 128), ("n4k", 128), ("c2k", 128), ("oneb", 128), ("dM", 128), ("dC", 128), ("wd", 128), ("bo4", 128), ("rcnt", 128), ("thr", 256),
         ("U", 144), ("UW", 144), ("cw", 48), ("zpl", 256), ("c24", 128), ("zn", 256), ("ze", 256), ("qx", 256), ("sg", 256), ("cn", 256), ("rT", 256), ("mk", 256), ("lo", 512)),
    I32: (("pi", 256), ("pj", 256), ("ui", 32), ("sq", 16), ("bs", 16), ("ej", 256), ("vi", 256), ("vj", 256), ("ki", 64), ("el", 16), ("ij", 32)),
    U16: (("xl", 48), ("e16", 256), ("elu", 16), ("ju", 256), ("nu", 256), ("of", 64), ("ILu", 16)),
}
PLACE = {}
for _d, _a in ((F32, "fA"), (F16, "hA"), (BF, "bA"), (I32, "iA"), (U16, "uA")):
    _at = 0
    for _n, _w in _SMALL[_d]:
        PLACE[_n] = (_a, _at, _w)
        _at += -(-_w // 32) * 32
    SCRATCH[_a] = ("sbuf", [128, _at], _d)
for _k in range(8):
    SCRATCH["ps%d" % _k] = ("psum", [128, 512], F32)
NDMA = 44
SEMAPHORES = ["eV", "eS", "eP", "eG", "snd", ] + ["arr%d" % k for k in range(5)] + ["d%d" % k for k in range(NDMA)] + ["%s%d" % (s, k) for s in ("out", "ret") for k in range(12)]

CY = 0.00083 * 1.1
GA, SC, PEC, VO, SO, WAKE, DL, RLAT = 1.4, 3.0, 0.00052, 0.035, 0.08, 0.09, 1.45, 3.6
EST = []


def rank_program(g, core, T, topo):
    def helper_of(c):
        mates = [x for x in topo.cores_of(c) if topo.die(x) == topo.die(c)]
        return [x for x in mates if T.rank_of(x) is None][[x for x in mates if T.rank_of(x) is not None].index(c)]

    def bits(src, dst, lo, hi):
        return sum(1 << e for e in topo.engines(src, dst)[lo:hi])

    folds = [(t, x) for t in range(RO) for x in range(0, 4096, FCUT) if FABS[t][x // 2048] == "H"]
    rank = T.rank_of(core)
    if rank is None:
        for home in [c for c in T.cores if helper_of(c) == core]:
            rid, pid, _se = topo.addr(home)
            for k, (t, x) in enumerate(folds):
                g.wait_ge(T.sem["out%d" % k], HENG)
                g.remote_dma(T["fa%d" % (x // 2048)][:, x % 2048:x % 2048 + FCUT], T.zr0[:, x:x + FCUT], T.sem["ret%d" % k], T.sem.snd, pid, rid, bits(core, home, 0, RENG))
            if folds:
                g.wait_ge(T.sem.snd, RENG * len(folds))
        return
    ops, hist, head = [], {}, [0.0]
    queues = {"V": g.vector, "S": g.scalar, "P": g.tensor, "G": g, "Y": g.sync}

    def A(name, lo=0, hi=None, step=1):
        if name in PLACE:
            name, at, w = PLACE[name]
            lo, hi = at + lo, at + (w if hi is None else hi)
        hi = T[name].shape[1] if hi is None else hi
        return (T[name][:, lo:hi] if step == 1 else T[name][:, lo:hi:step], (name, lo, hi, step), (hi - lo + step - 1) // step)

    def A3(name, i0, i1, a, b):
        w = SCRATCH[name][1][2]
        ap = T[name][:, i0, a:b] if i1 == i0 + 1 else T[name][:, i0:i1, a:b]
        return (ap, (name, i0 * w + a, (i1 - 1) * w + b, 1), (i1 - i0) * (b - a))

    def meets(a, b):
        if a[1] >= b[2] or b[1] >= a[2]:
            return False
        return not (a[3] == b[3] and a[3] > 1 and a[1] % a[3] != b[1] % b[3])

    def add(q, calls, w, r, cost, lat=0.0, kind="c", sem=None, val=1):
        o = {"q": q, "calls": calls, "cost": cost, "lat": lat, "kind": kind, "sem": sem, "val": val, "deps": {}, "i": len(ops), "head": head[0], "w": w}
        for regs, isw in ((r, False), (w, True)):
            for reg in regs:
                ps = reg[0][:2] == "ps"
                for (p, preg, pw) in hist.setdefault(reg[0], []):
                    same = p["q"] == q and len(q) == 1 and p["kind"] == "c" and kind == "c"
                    if ps and not same:
                        o["deps"][p["i"]] = True
                    elif (ps and q == "P") or (meets(reg, preg) and (isw or pw)):
                        need = not (same and q == "P")
                        o["deps"][p["i"]] = o["deps"].get(p["i"], False) or need
        for regs, isw in ((r, False), (w, True)):
            for reg in regs:
                h = hist[reg[0]]
                if reg[0][:2] == "ps":
                    if q == "P":
                        h[:] = []
                elif isw and reg[3] == 1 and len(reg) == 4:
                    h[:] = [x for x in h if not (x[0] is not o and x[1][1] >= reg[1] and x[1][2] <= reg[2])]
                h.append((o, reg, isw))
        ops.append(o)

    def dty(x):
        return SCRATCH[x[1][0]][2]

    def vcost(n, *xs):
        f = 0.5 if xs and all(dty(x) in (BF, F16, U16) for x in xs) else 1.0
        return VO + max(64.0, n * f) * CY

    def part(o):
        return o[1] if o[1][3] > 1 or o[1][2] - o[1][1] == o[2] else o[1] + (0,)

    def cp(o, i):
        add("V", [lambda: g.vector.tensor_copy(o[0], i[0])], [part(o)], [i[1]], vcost(i[2], o, i))

    def tt(o, a, b, op):
        f = 1 if a[1][0][:2] == "ps" or b[1][0][:2] == "ps" else 2
        add("V", [lambda: g.vector.tensor_tensor(o[0], a[0], b[0], op)], [part(o)], [a[1], b[1]], vcost(a[2] * f))

    def ts(o, a, s1, op0, s2=None, op1=None):
        r = [a[1]] + [s[1] for s in (s1, s2) if isinstance(s, tuple)]
        x1 = s1[0] if isinstance(s1, tuple) else s1
        x2 = s2[0] if isinstance(s2, tuple) else s2
        if op1 is None:
            f = lambda: g.vector.tensor_scalar(o[0], a[0], x1, None, op0)
        else:
            f = lambda: g.vector.tensor_scalar(o[0], a[0], x1, x2, op0, op1)
        add("V", [f], [part(o)], r, vcost(a[2], o, a))

    def ms(o, v):
        add("V", [lambda: g.vector.memset(o[0], v)], [o[1]], [], vcost(o[2], o))

    def scan(o, d0, d1, init, op0, op1):
        add("V", [lambda: g.vector.tensor_tensor_scan(o[0], d0[0], d1[0], init, op0, op1)], [o[1]], [d0[1], d1[1]], vcost(d1[2], o, d0, d1))

    def act(o, i, func=AF.Copy, scale=1.0, bias=0.0, total=None):
        r = [i[1]] + [s[1] for s in (scale, bias) if isinstance(s, tuple)]
        sc = scale[0] if isinstance(scale, tuple) else scale
        bi = bias[0] if isinstance(bias, tuple) else bias
        if total is None:
            f = lambda: g.scalar.activation(o[0], i[0], func, bi, sc)
        else:
            f = lambda: g.scalar.activation(o[0], i[0], func, bi, sc, accum_out=total[0])
        add("S", [f], [part(o)] + ([total[1]] if total else []), r, SO + i[2] * CY + (0.02 if total else 0.0))

    def either(alts, w, r):
        add("".join(alts), None, w, r, min(c for _f, c in alts.values()))
        ops[-1]["alts"] = alts

    def conv(o, i, scale=1.0, bias=0.0, qs="VS"):
        r = [i[1]] + [s[1] for s in (scale, bias) if isinstance(s, tuple)]
        sc = scale[0] if isinstance(scale, tuple) else scale
        bi = bias[0] if isinstance(bias, tuple) else bias
        plain = not isinstance(scale, tuple) and not isinstance(bias, tuple) and scale == 1.0 and bias == 0.0
        alts = {"V": ((lambda: g.vector.tensor_copy(o[0], i[0])) if plain else (lambda: g.vector.tensor_scalar(o[0], i[0], sc, bi, OP.mult, OP.add)), vcost(i[2], o, i)),
                "S": (lambda: g.scalar.activation(o[0], i[0], AF.Identity if isinstance(bias, tuple) else AF.Copy, bi, sc), SO + i[2] * CY),
                "G": (lambda: g.affine_select(o[0], i[0], [[1, o[2]]], OP.is_ge, 0.0, 1, 0), 0.2 + 2 * o[2] * CY)}
        either({q: alts[q] for q in qs}, [part(o)], r)

    def gcp(o, i):
        conv(o, i, qs="VSG")

    def gat(qs, o, win, off, scale=1.0, bias=0.0):
        c = 0.07 + 16 * off[2] * GA * CY
        alts = {"V": (lambda: g.vector.tensor_copy(o[0], win[0].indirect(off[0])), c),
                "S": (lambda: g.scalar.activation(o[0], win[0].indirect(off[0]), AF.Copy, bias, scale), c)}
        either({q: alts[q] for q in qs}, [o[1]], [win[1], off[1]])

    def gatop(o, win, off, b, op):
        add("V", [lambda: g.vector.tensor_tensor(o[0], win[0].indirect(off[0]), b[0], op)], [o[1]], [win[1], off[1], b[1]], 0.07 + 16 * off[2] * GA * CY)

    def scat(win, off, src, src2=None):
        if src2 is None:
            f = lambda: g.vector.tensor_copy(win[0].indirect(off[0]), src[0])
        else:
            f = lambda: g.vector.tensor_tensor(win[0].indirect(off[0]), src[0], src2[0], OP.add)
        add("V", [f], [win[1] + (0,)], [off[1], src[1]] + ([src2[1]] if src2 else []), 0.06 + src[2] * SC * CY)

    def pe(terms, first=True, last=True, each=False):
        calls, regs, n, c = [], [], len(terms), 0.0
        for k, (po, l, r) in enumerate(terms):
            go, end = (k % each == 0, k % each == each - 1) if each else (first and k == 0, last and k == n - 1)
            calls.append(lambda po=po, l=l, r=r, go=go, end=end: g.tensor.matmul(po[0], l[0], r[0], go, end))
            regs += [l[1], r[1]]
            c += max(64, po[2]) * PEC * (4 if dty(l) == F32 else 1)
        add("P", calls, [terms[0][0][1]], sorted(set(regs)), c, 0.05)

    def spread(bank, lo, src):
        return [(A(bank, lo + r, lo + 16 * src[2], 16), A("R", r * 128, r * 128 + 128), src) for r in range(16)]

    def shifted(name, r):
        return A(name, 15 - r, 143 - r)

    dn = [0]

    def dma(q, o, i, lat, regs_w, regs_r, acc=False):
        sem = "d%d" % dn[0]
        dn[0] += 1
        if acc:
            f = lambda: g.dma_start(o, i, accum_op=OP.add)
        else:
            f = lambda: queues[q].dma_start(o, i)
        add(q, [f], regs_w, regs_r, 1.0 if q == "G" else 0.1, lat, "d", sem, 16)

    def load(q, name, src, lat, hi=None):
        a = A(name, 0, hi)
        dma(q, a[0], T[src][:], lat, [a[1]], [])

    def addto(o, i, lat):
        dma("G", o[0], i[0], lat * DL, [o[1]], [o[1], i[1]], acc=True)

    def aff(o, i, pat, op, base, cm, fill=0.0):
        add("G", [lambda: g.affine_select(o[0], i[0], pat, op, fill, base, cm)], [o[1]], [i[1]], 0.2 + 2 * i[2] * CY)

    def iot(o, pat, base, cm):
        if dty(o) == I32:
            f = lambda: g.iota(o[0], pat, base, cm)
        else:
            f = lambda: g.iota(o[0], pat, base, cm, allow_small_or_imprecise_dtypes=True)
        add("G", [f], [o[1]], [], 0.16 + 2 * o[2] * CY)

    load("Y", "hki", "hk", 2.2)
    load("S", "wti", "wt", 2.2)
    load("Y", "zin0", "zc", 2.4)
    load("S", "thi", "th", 2.4)
    load("Y", "lki", "lk", 4.0)
    load("Y", "gist", "gi", 5.3, E)
    load("Y", "ixi", "ix", 7.5, E)
    load("Y", "xcb", "xc", 8.5)

    blk8 = A("blk", 0, 128, 16)
    ms(A("one"), 1.0)
    ms(A("UW"), 0.0)
    aff(A("blk"), A("one"), [[-16, 8], [0, 16]], OP.is_ge, 0, 1)
    aff(A("blk"), A("blk"), [[16, 8], [0, 16]], OP.is_ge, 15, -1)
    iot(A("pi", 0, 16), [[-1, 16]], 16, 1)
    aff(A("idf"), A("one"), [[-1, 128]], OP.is_equal, 0, 1)
    cp(A("wtf"), A("wti"))
    ts(A("UW", 15, 143, 16), blk8, A("wtf"), OP.mult)
    cp(A("hkf"), A("hki"))
    ts(A("pj", 0, 16), A("pi", 0, 16), 15, OP.bitwise_and)
    ts(A("pd"), A("pj", 0, 16), 0.0, OP.is_equal, A("hkf", 0, 1), OP.mult)
    pe([(A("ps5", 0, 16), A("blk"), A("pd"))])
    conv(A("pB"), A("ps5", 0, 16))
    conv(A("id16"), A("idf"))
    for m in range(0 if FAST else 16):
        conv(A("DP", m * 128, m * 128 + 128), A("id16"), A("pB", m, m + 1))
    ms(A("one16"), 1.0)
    for k in range(0, 16, 4):
        aff(A("R", k * 128, k * 128 + 512), A("one16"), [[-1, 4], [-16, 8], [0, 16]], OP.is_equal, -k, 1)
    cp(A("rcol"), A("pj", 0, 1))
    conv(A("thf"), A("thi"), -1.0, -0.5)
    for name, c in (("k2b", 2048.0), ("ni16", -1.0)):
        conv(A(name), A("id16"), c)
    aff(A("sh16"), A("one16", 0, 128), [[-1, 128]], OP.is_equal, -1, 1)
    for k, c in enumerate((16384.0, 1.0, -32768.0, -2.0, 32768.0, -65536.0)):
        conv(A("cw", 8 * k, 8 * k + 8), blk8, c)
    conv(A("bm4"), blk8, -4.0)
    conv(A("dP"), A("id16"), A("hkf", 0, 1))
    conv(A("dM"), A("id16"), A("rcol"), -64.0)
    ms(A("c2k"), 2048.0)
    conv(A("hlf"), A("one"), 0.5)
    ms(A("rmin"), -4.0e7)
    ms(A("rmin", 0, 128, 16), 4.0e7)
    iot(A("pi", 16, 32), [[16, 16]], 15, 0)
    iot(A("pi", 24, 32), [[1, 8]], 128, 0)
    cp(A("xl", 0, 16), A("pi", 16, 32))
    if FAST0:
        iot(A("pi", 32, 48), [[1, 16]], 0, 0)
        iot(A("pi", 48, 64), [[0, 16]], 0, 1)
        ts(A("pj", 48, 64), A("pi", 48, 64), 15, OP.bitwise_and)
        conv(A("xl", 16, 32), A("pi", 32, 48))
        conv(A("xl", 32, 48), A("pj", 48, 64))
    iot(A("vi", 0, 128), [[0, 8], [-1, 16]], 16, 1)
    ts(A("vj", 0, 128), A("vi", 0, 128), 15, OP.bitwise_and)
    ts(A("msk", 0, 128), A("vj", 0, 128), 0.0, OP.is_equal)
    iot(A("lcol"), [[128, 2]], W, 1)
    gcp(A("msk", 256, 384), A("msk", 0, 128))
    for h in (0, 1):
        conv(A("msk", 256 * h + 128, 256 * h + 256), A("msk", 0, 128), A("lcol", h, h + 1))
    ms(A("U"), 0.0)
    conv(A("U", 15, 143, 16), blk8, 128.0)
    ms(A("px0", 2048, 2064), 0.0)
    ms(A("px1", 2048, 2064), 0.0)
    ms(A("rz"), 1000.0)
    ms(A("rz", 0, 1024, 16), 0.0)
    ms(A("half"), 0.5)
    ms(A("zero"), 0.0)
    scan(A("pw"), A("half"), A("zero"), 2.0, OP.mult, OP.add)
    tt(A("tw"), A("pw"), A("msk", 0, 16), OP.mult)
    act(A("junk"), A("tw"), AF.Copy, total=A("wcol"))
    conv(A("wd"), A("blk"), A("wcol"))
    conv(A("bo4"), A("blk"), 4.0)
    conv(A("thr", 0, 16), A("pw"), -2.5 / 128)
    for k in (16, 32, 64, 128):
        gcp(A("thr", k, 2 * k), A("thr", 0, k))
    iot(A("dmp", 16, 32), [[16, 16]], W, 0)
    ts(A("dmp", 16, 32), A("dmp", 16, 32), A("rcol"), OP.add)
    ts(A("dmp", 0, 16), A("dmp", 16, 32), float(E - W), OP.add)
    ts(A("dmh"), A("dmp"), -2048.0, OP.add)
    ts(A("kcol"), A("rcol"), -1.0, OP.mult, 15.0, OP.add)
    ts(A("ccol", 0, 1), A("rcol"), 15.0, OP.is_equal, -16384.0, OP.mult)
    tt(A("ccol", 1, 2), A("ccol", 0, 1), A("kcol"), OP.add)
    ts(A("dCA", 0, 128), A("idf"), A("ccol", 1, 2), OP.mult, 1024.0, OP.mult)
    tt(A("ccol", 0, 1), A("thf", 0, 1), A("ccol", 0, 1), OP.subtract)
    conv(A("dCA", 128, 256), A("idf"), A("ccol", 0, 1))
    conv(A("dB", 0, 128), A("id16"), A("thf", 1, 2))
    gcp(A("dB", 128, 256), A("dB", 0, 128))
    ms(A("rmax"), 4.0e7)
    ms(A("rmax", 0, 128, 16), -4.0e7)
    ms(A("rcnt"), 1.0)
    ms(A("rcnt", 0, 128, 16), 0.0)
    pe([(A("ps5", 32, 33), A("blk"), A("wtf"))])
    conv(A("wb"), A("ps5", 32, 33), 192.0)
    conv(A("pt", 0, W), A("lki"), 1.0 / 4096)
    dma("G", T.pt[:, 0:W], T.xc[:], 5.5, [("pt", 0, W, 1)], [("pt", 0, W, 1)], acc=True)
    conv(A("xw"), A("xcb"), 1.0, 192.0)
    conv(A("zn"), A("zin0"), -1.0, 192.0)

    bank = [0]
    helper = helper_of(core)
    hrid, hpid, _se = topo.addr(helper)
    if folds:
        iot(A("c192"), [[0, FCUT]], 192, 0)
        ms(A("c24"), 24.0)

    def sums(out, src, lo, w, step):
        return [(out(k), src(k), w) for k in range(lo, lo + step)]

    def firsts(bc, own, eqn, lo, ps, dump, a=0, b=256):
        O = lambda x, y: A(ps, 256 + x, 256 + y)
        pe([(O(a, b), A("one16", 0, 128), A("thr", a, b))], True, False)
        for c0 in range(0, b // 16, 4):
            calls, w, r, cost, terms = [], [], [], 0.0, []
            for c in range(c0, c0 + 4):
                x, y = max(a, 16 * c), max(a, 16 * c + 16)
                o, i, s = A3(eqn, c, c + 1, x - 16 * c, b - 16 * c), A(bc, x, b), A(own, c, c + 1)
                calls.append(lambda o=o, i=i, s=s: g.vector.tensor_scalar(o[0], i[0], s[0], None, OP.is_equal))
                w.append(o[1])
                r += [i[1], s[1]]
                cost += vcost(i[2], o, i)
                if y < b:
                    terms.append((O(y, b), A("bo4"), A3(eqn, c, c + 1, y - 16 * c, b - 16 * c)))
            add("V", calls, w, sorted(set(r)), cost)
            pe(terms, False, False)
        pe([(O(a, b), A("wd"), A3(eqn, a // 16, b // 16, 0, 16))], False, True)
        act(A("lo", lo + a, lo + b), O(a, b), AF.Sign)
        out = A(ps, a // 16, b // 16)
        pe([(out, A("id16"), A("dmh", dump + a // 16, dump + b // 16))] + [(out, shifted("U", r), A("lo", lo + a + r, lo + b, 16)) for r in range(16)])
        return out

    def cues(t, h0, h1):
        z, cb, cf, zq = "zin%d" % t, "cb%d" % (t & 1), "cf%d" % (t & 1), "zq%d" % (t & 1)
        a, b, c0, c1 = 128 * h0, 128 * h1, 8 * h0, 8 * h1
        u, n = A("ps6", 256 + c0, 256 + c1), A(z if t else "zn", a, b)
        pe([(u, shifted("UW", r), A(z, a + r, b, 16)) for r in range(16)])
        if t:
            conv(A("ui", c0, c1), u, -1.0, A("wb"))
        else:
            conv(A("ui", c0, c1), u)
        ts(A3(cb, 0, 1, c0, c1), A("ui", c0, c1), 2047, OP.bitwise_and)
        if not FAST:
            conv(A3(cf, 0, 1, c0, c1), A3(cb, 0, 1, c0, c1))
        ts(A("ui", 16 + c0, 16 + c1), A("ui", c0, c1), 4095, OP.bitwise_and)
        tt(A("sq", c0, c1), A("ui", 16 + c0, 16 + c1), A("ui", 16 + c0, 16 + c1), OP.mult)
        ts(A3(cb, 2, 3, c0, c1), A("sq", c0, c1), 5, OP.logical_shift_right, 2047, OP.bitwise_and)
        ts(A3(cb, 1, 2, c0, c1), A("sq", c0, c1), 4, OP.logical_shift_right, 1023, OP.bitwise_and)
        if FAST:
            gcp(A3(cf, 0, 2, c0, c1), A3(cb, 0, 2, c0, c1))
        else:
            conv(A3(cf, 1, 3, c0, c1), A3(cb, 1, 3, c0, c1))
        w = c1 - c0
        if t == 0 and FAST0:
            gat("VS", A("prow"), A("pB"), A("xl", 16, 32))
        if (t == 0 and FAST0) or FAST:
            gatop(A("e0"), A3(cb, 0, 1, 0, 16), A("xl", 32, 48), A("prow"), OP.mult)
        if t == 0 and FAST0:
            gatop(A("ej"), A3(cb, 2, 3, 0, 16), A("xl", 32, 48), A("e0"), OP.add)
            ts(A3("ei", 0, 16, 0, 16), A("ej"), 2047, OP.bitwise_and)
        for row in () if (t == 0 and FAST0) or FAST else (0, 2):
            for m0 in (0, 8):
                pe([(A("ps6", a + w * m, a + w * m + w), A("id16") if row else A("DP", m * 128, m * 128 + 128), A3(cf, row, row + 1, c0, c1))
                    for m in range(m0, m0 + 8)], row + m0 == 0, row + m0 == 10)
        for x in range(0, 512, 128):
            gcp(A3(zq, h0, h1, x, x + 128), n)
        if 0 < t < RO - 1:
            conv(A("zpl", a, b), n, -1.0, 192.0)
        for m in range(16):
            conv(A("zr%d" % (t & 1), 16 * a + m, 16 * b, 16), n, qs=ZPLAN[t])

    H = ((0, 0, 128), (1, 128, 256))
    for t in range(RO):
        z, zr, cb, cf, zq = "zin%d" % t if t else "zn", "zr%d" % (t & 1), "cb%d" % (t & 1), "cf%d" % (t & 1), "zq%d" % (t & 1)
        acol = A("ps6", 272, 273)
        if t == 0:
            cues(0, 0, 2)
            if not FAST0:
                conv(A3("ei", 0, 16, 0, 16), A("ps6", 0, 256))
        elif FAST:
            ts(A("bs"), A3(cb, 2, 3, 0, 16), acol, OP.add, 1024.0, OP.add)
            gatop(A("ej"), A("bs"), A("xl", 32, 48), A("e0"), OP.add)
            ts(A3("ei", 0, 16, 0, 16), A("ej"), 2047, OP.bitwise_and)
        elif not SPLIT:
            ts(A3("ei", 0, 16, 0, 16), A("ps6", 0, 256), acol, OP.add, 1024.0, OP.add)
            ts(A("bs"), A3(cb, 2, 3, 0, 16), acol, OP.add, 1024.0, OP.add)
        for (h, a, b) in H:
            if t and SPLIT:
                if h:
                    cues(t, 1, 2)
                ts(A3("ei", 8 * h, 8 * h + 8, 0, 16), A("ps6", a, b), acol, OP.add, 1024.0, OP.add)
                ts(A("bs", 8 * h, 8 * h + 8), A3(cb, 2, 3, 8 * h, 8 * h + 8), acol, OP.add, 1024.0, OP.add)
                ts(A("ej", a, b), A3("ei", 8 * h, 8 * h + 8, 0, 16), 2047, OP.bitwise_and)
            elif not FAST and (t or not FAST0):
                ts(A("ej", a, b), A3("ei", 0, 16, 8 * h, 8 * h + 8), 2047, OP.bitwise_and)
            conv(A("e16", a, b), A("ej", a, b) if not FAST and (t or not FAST0) else A3("ei", 0, 16, 8 * h, 8 * h + 8))
        for (h, a, b) in H:
            c0, c1, ps, X = 8 * h, 8 * h + 8, "ps%d" % (2 + h), "X%d" % h
            gd, ga, px, yd, ya, fa = ["%s%d" % (n, h) for n in ("gd", "ga", "px", "yd", "ya", "fa")]
            key = lambda k: A(ps, k, 128, 16)
            for j in range(4):
                x, y, q = 512 * j, 512 * j + 512, GPLAN[t][4 * h + j]
                lst, zz = A("e16", a + 32 * j, a + 32 * j + 32), A3(zq, h, h + 1, 0, 512)
                if q == "S":
                    gat("S", A(gd, x, y), A("gist", 0, E), lst)
                    d = A("ps%d" % bank[0])
                    bank[0] ^= 1
                    pe([(d, A("id16"), A(gd, x, y))] + [(A(d[1][0], v, v + 128), A("id16"), A(z, a, b)) for v in range(0, 512, 128)])
                    act(A(ga, x, y), d, AF.Abs, 1.0, -192.0)
                else:
                    gatop(A(gd, x, y), A("gist", 0, E), lst, zz, OP.add)
                    if q == "A":
                        act(A(ga, x, y), A(gd, x, y), AF.Abs, 1.0, -192.0)
                    else:
                        ts(A(ga, x, y), A(gd, x, y), 192.0, OP.min, -96.0, OP.add)
                        pe(sums(key, lambda m: A(gd, 128 * m, 128 * m + 128), 4 * j, A("cw", 32, 40), 4), j == 0, False)
                pe(sums(key, lambda m: A(ga, 128 * m, 128 * m + 128), 4 * j, A("cw", 40, 48) if q == "V" else A("cw", 32, 40), 4), j == 0 and q != "V", False)
            pe([(A(ps, 0, 128), A("c2k"), A("dM")), (A(ps, 0, 128), A("one16", 0, 128), A("dP"))], False, True)
            km = "km%d" % h
            scan(A(km, 0, 128), A("rmin"), A(ps, 0, 128), 4.0e7, OP.max, OP.min)
            ts(A(km, 128, 136), A(km, 15, 128, 16), 2047, OP.bitwise_and)
            gatop(A("Xh", a, b), A(km), A("xl", 8, 16), A("msk", 0, 128), OP.mult)
            pe([(A(ps, 0, 8), A("Xh", a, b), A("cw", 8, 16))])
            i2, i3 = [A("ki", 32 * h + 8 * x, 32 * h + 8 * x + 8) for x in range(2)]
            tt(i2, A(ps, 0, 8), A3(cb, 0, 1, c0, c1), OP.mult)
            tt(i3, i2, A("bs", c0, c1) if t else A3(cb, 2, 3, c0, c1), OP.add)
            ts(A("el", c0, c1), i3, 2047, OP.bitwise_and)
            conv(A("elu", c0, c1), A("el", c0, c1))
            gat("VS", A("ju", a, b), A("ixi", 0, E), A("elu", c0, c1))
            for q in range(0, 128, PCUT):
                gat("VS", A(px, 16 * q, 16 * (q + PCUT)), A("pt", 0, W), A("ju", a + q, a + q + PCUT))
            gcp(A("jh", a, b), A("ju", a, b))
            nT = A(ps, 128, 256)
            pe([(A(ps, 128 + k, 256, 16), A(px, k, 2048, 16), A("idf", k, 128, 16)) for k in range(16)], each=True)
            conv(A("qx", a, b), nT, 1.0, 128.0)
            conv(A("fr", a, b), nT)
            pe([(A(ps, 0, 128), A("fr", a, b), A("idf")), (A(ps, 0, 128), A("qx", a, b), A("ni16"))])
            conv(A("nu", a, b), A(ps, 0, 128), 4096.0, 128.0 * 4096)
            gcp(A("nh", a, b), A("nu", a, b))
            for x in range(0, 2048, FCUT):
                addto(A(zr, 2048 * h + x, 2048 * h + x + FCUT), A(px, x, x + FCUT), 2.0 + 3.0 * FCUT / 2048)
        for (h, a, b) in H:
            head[0] = HZ
            terms = []
            for x in (0, 1024):
                diff, l = ZMAX[t][2 * h + x // 1024] == "d", a + x // 16
                src = A(zr, 2048 * h + x, 2048 * h + x + 1024) if diff else A("px%d" % h, x, x + 1024)
                scan(A("zs%d" % h, x, x + 1024), A("rz"), src, 0.0, OP.min, OP.max)
                zp = A("ps6", 256 + l, 320 + l)
                terms += [(zp, A("ni16"), A(z, l, l + 64))] * (2 if diff else 1) + [(zp, A("id16"), A("zs%d" % h, x + 15, x + 1024, 16))]
            pe(terms)
            zp = A("ps6", 256 + a, 256 + b)
            if t < RO - 1:
                conv(A("zo%d" % t, a, b), zp, -0.5, 96.25)
            else:
                conv(A("ze", a, b), zp, -0.5, 96.25)
                conv(A("zo%d" % t, a, b), A("ze", a, b), -1.0, 192.0)
        dst = T.cores[(rank + 1) % len(T.cores)] if t < RO - 1 else T.cores[(rank - t) % len(T.cores)]
        land = "zin%d" % (t + 1) if t < RO - 1 else "zfin"
        eng = topo.engines(core, dst)[:NENG]
        rid, pid, _se = topo.addr(dst)
        mask = sum(1 << e for e in eng)
        for a, b in ((0, 128), (128, 256)) if SPLIT and t < RO - 1 else ((0, 256),):
            sem = "arr%d" % (2 * t + a // 128)
            add("G", [lambda land=land, rid=rid, pid=pid, mask=mask, t=t, a=a, b=b, sem=sem: g.remote_dma(
                T[land][:, a:b], T["zo%d" % t][:, a:b], T.sem[sem], T.sem.snd, pid, rid, mask)],
                [(land, a, b, 1)], [("zo%d" % t, a, b, 1)], 1.0, RLAT, "r", sem, len(eng))
        gcp(A("elh"), A("el"))
        gcp(A("elf"), A("el"))
        pe(spread("ps7", 0, A("elh")), each=True)
        conv(A("eB"), A("ps7", 0, 256))
        tt(A("of", 0, 16), firsts("eB", "elf", "eq", 0, "ps7", 0), A("elf"), OP.max)
        pe(spread("ps5", 0, A3(cf, 0, 2, 0, 16)), each=True)
        conv(A("xq"), A("ps5", 0, 256), A("hkf", 1, 2))
        tt(A("vi"), A("ps5", 256, 512), A("xq"), OP.add)
        ts(A("vj"), A("vi"), 1023, OP.bitwise_and)
        gcp(A("v16"), A("vj"))
        if t < RO - 1:
            cues(t + 1, 0, 1 if SPLIT else 2)
        for (h, a, b) in H:
            c0, c1, ps, X, kc = 8 * h, 8 * h + 8, "ps%d" % (2 + h), "X%d" % h, "kc%d" % h
            px, yd, ya = "px%d" % h, "yd%d" % h, "ya%d" % h
            pe([(A(ps, 256, 512), A("one"), A("dCA")), (A(ps, 256, 384), A("jh", a, b), A("id16"))], True, False)
            for q, r in YCUT[h]:
                x, y, lst = 16 * q, 16 * r, A("nu", a + q, a + r)
                if YPLAN[t][2 * h + q // 64] == "V":
                    gatop(A(yd, x, y), A("xw"), lst, A(px, x + 1, y + 1), OP.subtract)
                else:
                    gat("S", A(yd, x, y), A("xcb"), lst, -1.0, 192.0)
                    addto(A(yd, x, y), A(px, x + 1, y + 1), 3.5)
                act(A(ya, x, y), A(yd, x, y), AF.Abs, 1.0, -192.0)
            pe(sums(lambda k: A(ps, 256 + k, 512, 16), lambda k: A(ya, k, 2048, 16), 0, A("cw", 0, 16), 16), False, True)
            act(A("sg", a, b), A(ps, 384, 512), AF.Sign)
            scan(A("cn", a, b), A("rcnt"), A("sg", a, b), 0.0, OP.mult, OP.add)
            ts(A(kc, 128, 136), A("cn", a + 15, b, 16), -6.0, OP.is_le)
            if t < RO - 1:
                act(A("junk", c0, c1), A("cn", a + 15, b, 16), AF.Sign, -1.0, -5.0, total=A("acol", h, h + 1))
            scan(A(kc, 0, 128), A("rmax"), A(ps, 256, 384), -4.0e7, OP.min, OP.max)
            gatop(A(X), A(kc), A("xl", 0, 16), A("msk", 2 * a, 2 * b), OP.mult)
            pe([(A(ps, 0, 8), A(X, 0, 128), blk8), (A(ps, 8, 16), A(X, 128, 256), blk8)], each=True)
            if t < RO - 1:
                pe([(A(ps, 16, 24), A("idf"), A("dmp", c0, c1)), (A(ps, 16, 24), A(X, 128, 256), A("bm4"))])
                tt(A("of", 16 + c0, 16 + c1), A(ps, 16, 24), A("of", c0, c1), OP.max)
                scat(A("gist"), A("of", 16 + c0, 16 + c1), A("zpl" if t else "zin0", a, b))
            conv(A3("ksl", h, h + 1, 0, 16), A(ps, 0, 16))
            gat("VS", A("rT", a, b), A(kc), A("xl", 8, 16))
        if t < RO - 1:
            cnt = A("ps6", 272, 273)
            pe([(cnt, A("hlf"), A("acol", h, h + 1)) for h in (0, 1)])
        pe([(A("ps4", 0, 256), A("one16", 0, 128), A("dB"))], True, False)
        for (h, a, b) in H:
            fa, far = "fa%d" % h, lambda k: A("ps4", a + k, b, 16)
            pe([(A("ps4", 256 + a, 256 + b), A("v16", a, b), A("id16")), (A("ps4", 256 + a, 256 + b), A("jh", a, b), A("ni16"))], False, False)
            for x in range(0, 2048, FCUT):
                d = A(zr, 2048 * h + x, 2048 * h + x + FCUT)
                if FABS[t][h] == "S":
                    act(A(fa, x, x + FCUT), d, AF.Abs, 1.0, -192.0)
                elif FABS[t][h] == "V":
                    ts(A(fa, x, x + FCUT), d, 192.0, OP.min, -96.0, OP.add)
                else:
                    k, y = folds.index((t, 2048 * h + x)), 2048 * h + x
                    tr = RemoteDMATransfer(dst_ids=[DstId(rid=hrid, pnc=hpid)], dma_engine_mask=bits(core, helper, 16 - HENG, 16), remote_sem=T.sem["out%d" % k],
                                           srcs=[d[0], T.c192[:]], dsts=[T.zr0[:, y:y + FCUT]], alu_op=3)
                    add("G", [lambda tr=tr: g.remote_dma_fused([tr], local_sem=T.sem.snd)], [A(fa, x, x + FCUT)[1], ("fold", 0, 1, 1)], [d[1], A("c192")[1]],
                        1.0, HLAT, "r", "ret%d" % k, RENG)
                    ops[-1]["sent"], ops[-1]["deps"] = HENG, {i: (w if ops[i]["w"][:1] == [A(fa, x, x + FCUT)[1]] or ops[i]["w"][1:] != [("fold", 0, 1, 1)] else False)
                                                              for i, w in ops[-1]["deps"].items()}
            if FABS[t][h] == "H":
                pe([(A("ps4", a, b), A("one16", 0, 128), A("c24"))], False, False)
            if FABS[t][h] == "S":
                pe(sums(far, lambda k: A(fa, k, 2048, 16), 0, A("cw", 8, 16), 16), False, False)
            else:
                pe(sums(far, lambda k: A(zr, 2048 * h + k, 2048 * h + 2048, 16), 0, A("cw", 8, 16), 16), False, False)
                pe(sums(far, lambda k: A(fa, k, 2048, 16), 0, A("cw", 24, 32), 16), False, False)
        pe([(A("ps4", a, b), A("k2b"), A("rT", a, b)) for (h, a, b) in H], False, True)
        act(A("mk"), A("ps4", 0, 256), AF.Sign)
        tt(A("pn"), A("ps4", 256, 512), A("mk"), OP.mult)
        nn = A("ps4", 0, 256)
        pe([(nn, A("id16"), A("v16")), (nn, A("id16"), A("jh"))] + [(A("ps4", a, b), A("pn", a, b), A("id16")) for (h, a, b) in H])
        conv(A("nn"), nn, 0.5)
        if t == RO - 1:
            for x in range(0, E, 512):
                gcp(A("nm", x, x + 512), A("ixi", x, x + 512))
        scat(A("ixi" if t < RO - 1 else "nm"), A("of", 0, 16), A("nn"))
        tab, writes = "pt" if t < RO - 1 else "lkt", []
        for h0, h1 in ((0, 1), (1, 2)) if LSPLIT[t] else ((0, 2),):
            a, b, c0, c1 = 128 * h0, 128 * h1, 8 * h0, 8 * h1
            w = c1 - c0
            ij, sl = 2 * c0, A("sl", 2 * c0, 2 * c1)
            ts(A("ij", ij, ij + w), A3("ksl", h0, h1, 0, 8), 1023, OP.bitwise_and)
            ts(A("ij", ij + w, ij + 2 * w), A3("ksl", h0, h1, 0, 8), 10, OP.logical_shift_right, 15, OP.bitwise_and)
            conv(sl, A("ij", ij, ij + 2 * w))
            gcp(A("ILu", c0, c1), A("ij", ij, ij + w))
            tt(A("own", c0, c1), A("ij", ij, ij + w), A3("ksl", h0, h1, 8, 16), OP.max)
            pe(spread("ps7", 0, sl), each=True)
            conv(A("IB", a, b), A("ps7", 0, b - a))
            ts(A("oh", a, b), A("ps7", b - a, 2 * (b - a)), A("kcol"), OP.is_equal, 1.0 / 4096 if t < RO - 1 else 1.0, OP.mult)
            dp = A("ps5", 256 + a, 256 + b)
            pe([(dp, A("sh16"), A("jh", a, b)), (dp, A("ni16"), A("nh", a, b))])
            tt(A("dl", a, b), dp, A("oh", a, b), OP.mult)
            gat("VS", A("nl", a, b), A(tab, 0, W), A("ILu", c0, c1))
            tt(A("of", 32 + c0, 32 + c1), firsts("IB", "own", "eq2", 256, "ps5" if t < RO - 1 else "ps%d" % h0, 16, a, b), A("own", c0, c1), OP.max)
            scat(A(tab), A("of", 32 + c0, 32 + c1), A("nl", a, b), A("dl", a, b))
        if t == RO - 2:
            for x, ps in ((0, "ps5"), (512, "ps7")):
                pe([(A(ps), A("idf"), A("pt", x, x + 512)), (A(ps), A("ni16"), A("xcb", x, x + 512))])
                conv(A("lkt", x, x + 512), A(ps), 4096.0)
    dma("Y", T.yz[:], T.zfin[:], 2.5, [], [("zfin", 0, 256, 1)])
    dma("Y", T.yi[:], T.nm[:, 0:E], 5.0, [], [("nm", 0, E, 1)])
    dma("Y", T.yl[:], T.lkt[:, 0:W], 3.5, [], [("lkt", 0, W, 1)])

    n = len(ops)
    users, done = [[] for _ in range(n)], []
    for o in ops:
        seen = 0
        for d in o["deps"]:
            seen |= done[d]
        o["deps"] = {d: w for d, w in o["deps"].items() if not seen >> d & 1}
        done.append(seen | sum(1 << d for d, w in o["deps"].items() if w))
    for o in ops:
        for d in o["deps"]:
            users[d].append(o["i"])
    way = [0.0] * n
    for i in range(n - 1, -1, -1):
        o = ops[i]
        way[i] = o["cost"] + max([way[j] + (o["lat"] + WAKE if ops[j]["deps"][i] else 0.0) for j in users[i]] + [o["lat"]])
    choice = [[(q, o["alts"][q][1]) for q in o["q"]] if "alts" in o else [(o["q"], o["cost"])] for o in ops]
    lat = [o["lat"] for o in ops]
    ahead = ([[(j, lat[i] + WAKE if ops[j]["deps"][i] else None) for j in users[i]] for i in range(n)], [len(o["deps"]) for o in ops], [0.0] * n, lat)
    back = ([[(d, lat[d] + WAKE if w else None) for d, w in o["deps"].items()] for o in ops], [len(u) for u in users], lat, [0.0] * n)

    def place(key, lean, way):
        then, left, avail, after = way[0], list(way[1]), list(way[2]), way[3]
        start, on, span, end = [0.0] * n, [""] * n, 0.0, [0.0] * n
        begins, ends = {q: [] for q in queues}, {q: [] for q in queues}
        ready = sorted((key[i], i) for i in range(n) if left[i] == 0)
        while ready:
            i = ready.pop()[1]
            top = None
            for q, c in choice[i]:
                b, e, s = begins[q], ends[q], avail[i]
                k = len(e)
                if k and e[-1] > s:
                    lo, hi = 0, k
                    while lo < hi:
                        mid = (lo + hi) >> 1
                        if e[mid] > s:
                            hi = mid
                        else:
                            lo = mid + 1
                    while lo < k and b[lo] < s + c:
                        s = e[lo]
                        lo += 1
                    k = lo
                v = s + c + (lean[i] if q == "V" else 0.0)
                if top is None or v < top[0]:
                    top = (v, q, s, c, k)
            _v, q, s, c, k = top
            begins[q].insert(k, s)
            ends[q].insert(k, s + c)
            f = s + c
            start[i], on[i], end[i] = s, q, f
            if f + after[i] > span:
                span = f + after[i]
            for j, wait in then[i]:
                w = s + 1e-6 if wait is None else f + wait
                if w > avail[j]:
                    avail[j] = w
                left[j] -= 1
                if left[j] == 0:
                    x, lo, hi = (key[j], j), 0, len(ready)
                    while lo < hi:
                        mid = (lo + hi) >> 1
                        if ready[mid] < x:
                            lo = mid + 1
                        else:
                            hi = mid
                    ready.insert(lo, x)
        return start, on, span, end

    def timed(lines, on, old=None, t0=-1.0):
        then, before = ahead[0], back[0]
        avail, end, why = (list(old[0]), list(old[3]), list(old[4])) if old else ([0.0] * n, [0.0] * n, [-1] * n)
        left, nxt, todo, count = [-1] * n, [-1] * n, [], 0
        new = [s >= t0 for s in avail]
        for line in lines.values():
            a, k = -1, len(line)
            while k and new[line[k - 1]]:
                k -= 1
            if k:
                a = line[k - 1]
            for j in line[k:]:
                s, cause, c = 0.0, -1, 0
                for d, wait in before[j]:
                    if new[d]:
                        c += 1
                    else:
                        w = avail[d] + 1e-6 if wait is None else end[d] + wait
                        if w > s:
                            s, cause = w, d
                if a >= 0:
                    if new[a]:
                        nxt[a] = j
                        c += 1
                    elif end[a] >= s:
                        s, cause = end[a], a
                left[j], why[j], a = c, cause, j
                end[j] = s
                count += 1
                if c == 0:
                    todo.append(j)
        while todo:
            i = todo.pop()
            count -= 1
            s = avail[i] = end[i]
            f = end[i] = s + price[i][on[i]]
            for j, wait in then[i]:
                w = s + 1e-6 if wait is None else f + wait
                if w > end[j]:
                    end[j], why[j] = w, i
                left[j] -= 1
                if left[j] == 0:
                    todo.append(j)
            j = nxt[i]
            if j >= 0:
                if f >= end[j]:
                    end[j], why[j] = f, i
                left[j] -= 1
                if left[j] == 0:
                    todo.append(j)
        if count:
            return None
        span, last = max((end[i] + lat[i], i) for i in final)
        chain = [last]
        while why[chain[-1]] >= 0:
            chain.append(why[chain[-1]])
        return avail, span, chain, end, why

    def polish(start, on, rng):
        on = list(on)
        lines = {q: sorted((i for i in range(n) if on[i] == q), key=lambda i: (start[i], i)) for q in queues}
        now = timed(lines, on)
        top = (now[0], list(on), now[1])
        for k in range(MOVES):
            chain = now[2]
            x = int(rng.randint(len(chain) - 1))
            v, u, kind = chain[x], chain[x + 1], rng.rand()
            if kind < 0.1:
                v = int(rng.randint(n))
            q = on[v]
            if kind < 0.3:
                if len(choice[v]) < 2:
                    continue
                r = [c for c, _p in choice[v] if c != q][int(rng.randint(len(choice[v]) - 1))]
                at = now[0][v] - rng.rand()
                new = dict(lines)
                new[q] = [i for i in lines[q] if i != v]
                p = sum(1 for i in lines[r] if now[0][i] < at)
                new[r] = lines[r][:p] + [v] + lines[r][p:]
                on[v], t0 = r, at
            else:
                if on[u] != q or u in ops[v]["deps"]:
                    continue
                line, far = lines[q], int(rng.randint(4))
                p = line.index(u)
                if kind < 0.65:
                    a = max(0, p - far)
                    new = dict(lines)
                    new[q], t0 = line[:a] + [v] + line[a:p + 1] + line[p + 2:], now[0][line[a]]
                else:
                    b = min(len(line), p + 2 + far)
                    new = dict(lines)
                    new[q], t0 = line[:p] + line[p + 1:b] + [u] + line[b:], now[0][u]
            got = timed(new, on, now, t0)
            if got is not None and got[1] <= now[1] - HEAT * (1.0 - k / MOVES) * np.log(rng.rand()):
                lines, now = new, got
                if now[1] < top[2]:
                    top = (now[0], list(on), now[1])
            else:
                on[v] = q
        return top

    price, final = [dict(c) for c in choice], [i for i in range(n) if not users[i]]
    if n not in ORDER:
        key, lean = np.array([way[i] + ops[i]["head"] for i in range(n)]), np.full(n, LEAN)
        best = top = place(key.tolist(), lean.tolist(), ahead)
        rng = np.random.RandomState(SEED)
        for k in range(TRIES):
            near = (np.abs(np.array(best[0]) - rng.rand() * best[2]) < 5.0) * (rng.rand(n) < (0.05, 0.2, 0.5)[k % 3])
            nl = lean + near * (rng.rand(n) < 0.3) * rng.randn(n)
            if k % 2 == 1:
                nk = np.array(place((np.array(best[3]) + near * rng.randn(n)).tolist(), nl.tolist(), back)[3])
            else:
                nk = key + near * rng.randn(n) * (0.5, 1.5, 4.0)[(k // 4) % 3]
            new = place(nk.tolist(), nl.tolist(), ahead)
            if new[2] <= best[2] + SLACK * (1.0 - k / TRIES) * rng.rand():
                key, lean, best = nk, nl, new
                if best[2] < top[2]:
                    top = best
        ORDER[n] = polish(top[0], top[1], rng)
    start, on, _span = ORDER[n]
    order = sorted(range(n), key=lambda i: (start[i], i))
    for o in ops:
        if "alts" in o:
            o["q"] = on[o["i"]]
            o["calls"], o["cost"] = [o["alts"][o["q"]][0]], o["alts"][o["q"]][1]
    EST.append((ops, (start, order, _span), way))

    know = {q: {} for q in queues}
    clock = [None] * n
    count = {q: 0 for q in queues}
    total = {}
    for i in order:
        o = ops[i]
        q = o["q"]
        k = know[q]
        for d in sorted(o["deps"]):
            if not o["deps"][d]:
                continue
            sem, val, ck = clock[d]
            if k.get(sem, 0) < val:
                queues[q].wait_ge(T.sem[sem], val)
                k[sem] = val
                for s2, v2 in ck.items():
                    if k.get(s2, 0) < v2:
                        k[s2] = v2
        ck = dict(k)
        inst = None
        for f in o["calls"]:
            inst = f()
        if o["kind"] == "c":
            count[q] += 1
            inst.then_inc(T.sem["e" + q], 1)
            clock[i] = ("e" + q, count[q], ck)
            total["e" + q] = count[q]
        elif o["kind"] == "d":
            inst.then_inc(T.sem[o["sem"]], 16)
            clock[i] = (o["sem"], 16, ck)
            total[o["sem"]] = 16
        else:
            clock[i] = (o["sem"], o["val"], {})
            total[o["sem"]] = o["val"]
            total["snd"] = total.get("snd", 0) + o.get("sent", o["val"])
    for sem in sorted(total):
        if know["G"].get(sem, 0) < total[sem]:
            g.wait_ge(T.sem[sem], total[sem])
